import numpy as np
import ml_dtypes


def mxq(x, axis, fmt="e4m3"):
    dtype, down = {"e4m3": (ml_dtypes.float8_e4m3fn, 7), "e5m2": (ml_dtypes.float8_e5m2, 14)}[fmt]
    v = np.moveaxis(np.asarray(x, np.float32).astype(ml_dtypes.bfloat16).astype(np.float64), axis, -1)
    blocks = v.reshape(v.shape[:-1] + (-1, 32))
    amax = np.abs(blocks).max(-1, keepdims=True)
    byte = np.maximum(np.where(amax > 0, np.frexp(amax)[1] - 1 + 127, 0) - down, 1)
    scale = np.exp2(byte - 127.0)
    codes = (blocks / scale).astype(np.float32).astype(dtype).astype(np.float64)
    return np.moveaxis((codes * scale).reshape(v.shape), -1, axis)


WIDE = False


def mx_kscale(k):
    if not WIDE:
        return np.ones(k)
    levels = np.array([10, -10, 5, -5, 0])
    if k % 512:
        return np.exp2(np.random.permutation(np.resize(levels, k // 32))).repeat(32)
    a = np.empty((k // 512, 16))
    for p in range(k // 512):
        a[p, :8] = np.random.permutation(np.resize(levels, 8))
        for g in range(8):
            far = levels[np.abs(levels - a[p, g]) >= 10]
            a[p, g + 8] = far[np.random.randint(len(far))]
    return np.exp2(a.ravel()).repeat(32)


def f64(x):
    return np.asarray(x).astype(np.float64)


def striped(idx):
    return np.tile(idx.reshape(-1, 16).T, (8, 1)).astype(np.uint16)


def unstriped(offs):
    return offs[:16].T.reshape(-1).astype(np.int64)


E2M1 = np.array([0.0, 0.5, 1.0, 1.5, 2.0, 3.0, 4.0, 6.0, -0.0, -0.5, -1.0, -1.5, -2.0, -3.0, -4.0, -6.0])


def pack_weight(w, fmt):
    k, n = w.shape
    w = f64(np.asarray(w, np.float32).astype(ml_dtypes.bfloat16)).reshape(k // 32, 32, n)
    amax = np.abs(w).max(1)
    if fmt == "e4m3":
        byte = np.frexp(amax)[1] - 1 + 127 - 7
    else:
        mant, ex = np.frexp(amax / 6.0)
        byte = np.where(mant > 0.5, ex, ex - 1) + 127
    byte = np.clip(np.where(amax > 0, byte, 1), 1, 254)
    scaled = (w * np.exp2(127.0 - byte)[:, None, :]).reshape(k, n).astype(np.float32)
    by_word = np.ascontiguousarray(scaled.reshape(k // 512, 128, 4, n).transpose(0, 1, 3, 2))
    if fmt == "e4m3":
        words = by_word.astype(ml_dtypes.float8_e4m3fn).view(np.uint8)
    else:
        c = by_word.astype(ml_dtypes.float4_e2m1fn).view(np.uint8) & 0xF
        words = (c[..., 0::2] | (c[..., 1::2] << 4)).reshape(k // 512, 128, 2 * n)
    return np.ascontiguousarray(words), np.ascontiguousarray(byte.astype(np.uint8).reshape(k // 512, 16, n))


def unpack_weight(words, scales, fmt):
    g, _, n = scales.shape
    words = np.ascontiguousarray(words).reshape(g, 128, n, -1)
    if fmt == "e4m3":
        vals = words.view(ml_dtypes.float8_e4m3fn).astype(np.float64)
    else:
        nib = np.empty((g, 128, n, 4), np.uint8)
        nib[..., 0::2] = words & 0xF
        nib[..., 1::2] = words >> 4
        vals = E2M1[nib]
    vals = vals * np.repeat(np.exp2(scales.astype(np.float64) - 127.0), 8, axis=1)[..., None]
    return vals.transpose(0, 1, 3, 2).reshape(g * 512, n)


def gelu(v):
    return 0.5 * v * (1.0 + np.tanh(np.sqrt(2.0 / np.pi) * (v + 0.044715 * v**3)))


K, T, S, T2, S2, N, C = 512, 2048, 1024, 4096, 1536, 512, 8

def setup_inputs():
    n = np.random.standard_normal
    s, u = mx_kscale(K)[:, None], mx_kscale(S)[:, None]
    centres = n((K, C))
    x = (0.8 * centres[:, np.random.randint(C, size=T)] + 0.6 * n((K, T))) * np.exp(0.2 * n(T)) * 1.2 / np.sqrt(K)
    z = (0.8 * centres[:, np.random.randint(C, size=T2)] + 0.6 * n((K, T2))) * np.exp(0.2 * n(T2)) * 1.2 / np.sqrt(K)
    idx, idx2 = np.random.permutation(T)[:S], np.random.permutation(T2)[:S2]
    tab_words, tab_scales = pack_weight(x * s, "e4m3")
    tab2_words, tab2_scales = pack_weight(z / s, "e4m3")
    hx = 0.5 * np.square(unpack_weight(tab_words, tab_scales, "e4m3")[:, idx] / s).sum(0)
    hz = 0.5 * np.square(unpack_weight(tab2_words, tab2_scales, "e4m3")[:, idx2] * s).sum(0)
    w4_words, w4_scales = pack_weight(2.0 * n((S, N)) / np.sqrt(S) / u, "e2m1")
    return dict(tab_words=tab_words, tab_scales=tab_scales, tab2_words=tab2_words, tab2_scales=tab2_scales,
                offs=striped(idx), offs2=striped(idx2),
                hx=hx.astype(np.float32), hz=hz.astype(np.float32),
                pw=(np.exp(0.3 * n(S)) * u[:, 0]).astype(np.float32),
                w4_words=w4_words, w4_scales=w4_scales,
                w=(n((S, N)) / np.sqrt(S) / u).astype(np.float32),
                b=(0.5 * n(N)).astype(np.float32))

def reference(tab_words, tab_scales, tab2_words, tab2_scales, offs, offs2, hx, hz, pw, w4_words, w4_scales, w, b):
    v = unpack_weight(tab_words, tab_scales, "e4m3")[:, unstriped(offs)]
    v2 = unpack_weight(tab2_words, tab2_scales, "e4m3")[:, unstriped(offs2)]
    A = v.T @ v2
    h = np.exp(A - f64(hx)[:, None] - f64(hz)[None, :]) * f64(pw)[:, None]
    hq = mxq(h, 0, "e4m3")
    w4 = unpack_weight(w4_words, w4_scales, "e2m1")
    y = w4.T @ hq + mxq(f64(w), 0, "e4m3").T @ hq
    return y + f64(b)[:, None]

@@ -1,0 +1,258 @@
+from contextlib import ExitStack
+
+import concourse.mybir as mybir
+
+K, T, S, T2, S2, N = 512, 2048, 1024, 4096, 1536, 512
+FLOPS = 2 * K * S * S2 + 2 * 2 * S * N * S2
+
+F32 = mybir.dt.float32
+BF16 = mybir.dt.bfloat16
+I32 = mybir.dt.int32
+U32 = mybir.dt.uint32
+U16 = mybir.dt.uint16
+U8 = mybir.dt.uint8
+FP8X4 = mybir.dt.float8_e4m3fn_x4
+FP4X4 = mybir.dt.float4_e2m1fn_x4
+ALU = mybir.AluOpType
+ACT = mybir.ActivationFunctionType
+
+P = 128
+PACK = 4
+PASS = P * PACK
+PASSES = S // PASS
+N_TILES = N // P
+GATHER = 512
+CHUNKS = [512,512,512]
+V2_ROW = 4
+
+
+def tile_list_gp_inducing_mean_kernel(
+    tc, tab_words, tab_scales, tab2_words, tab2_scales, offs, offs2, hx, hz, pw, w4_words, w4_scales, w, b, out
+):
+    nc = tc.nc
+    with ExitStack() as ctx:
+        keep = ctx.enter_context(tc.tile_pool(name="keep", bufs=1))
+        ring = ctx.enter_context(tc.tile_pool(name="ring", bufs=3))
+        outp = ctx.enter_context(tc.tile_pool(name="outp", bufs=4))
+        psum_a = ctx.enter_context(tc.psum_pool(name="psum_a", bufs=4))
+        psum_y = ctx.enter_context(tc.psum_pool(name="psum_y", bufs=1))
+
+        idx = keep.tile([P, S // 16], U16, name="idx")
+        idx2 = keep.tile([P, S2 // 16], U16, name="idx2")
+        tabw = keep.tile([P, T], I32, name="tabw", align_bytes=64)
+        tabs = keep.tile([P, T], U8, name="tabs", align_bytes=64)
+        tab2w = keep.tile([P, T2], I32, name="tab2w", align_bytes=64)
+        tab2s = keep.tile([P, T2], U8, name="tab2s", align_bytes=64)
+        w4w = keep.tile([P, PASSES, 2 * N], U8, name="w4w", align_bytes=64)
+        w4s = keep.tile([P, PASSES, N], U8, name="w4s", align_bytes=64)
+        hx_t = keep.tile([P, PASSES, PACK], F32, name="hx_t")
+        pw_t = keep.tile([P, PASSES, PACK], F32, name="pw_t")
+        b_t = keep.tile([P, N_TILES], F32, name="b_t")
+        hz_t = [keep.tile([P, GATHER], F32, name=f"hz_t{g}") for g in range(S2 // GATHER)]
+        w_raw = [keep.tile([P, PACK, N], F32, name=f"w_raw{a}") for a in range(PASSES)]
+
+        nc.vector.memset(tabs[:].bitcast(I32), 0)
+        nc.vector.memset(tab2s[:].bitcast(I32), 0)
+        nc.vector.memset(w4s[:].bitcast(I32), 0)
+
+        nc.sync.dma_start(idx[:], offs)
+        for q in range(4):
+            nc.sync.dma_start(tabs[32 * q : 32 * q + 4, :].bitcast(I32), tab_scales[0, 4 * q : 4 * q + 4, :].bitcast(I32))
+        nc.sync.dma_start(tabw[:], tab_words[0].rearrange("p t i -> p (t i)").bitcast(I32))
+        nc.sync.dma_start(idx2[:], offs2)
+        nc.sync.dma_start(tab2w[:], tab2_words[0].rearrange("p t i -> p (t i)").bitcast(I32))
+        for q in range(4):
+            nc.scalar.dma_start(
+                tab2s[32 * q + V2_ROW : 32 * q + V2_ROW + 4, :].bitcast(I32),
+                tab2_scales[0, 4 * q : 4 * q + 4, :].bitcast(I32),
+            )
+        nc.scalar.dma_start(pw_t[:], pw.rearrange("(a p t) -> p a t", a=PASSES, t=PACK))
+        nc.scalar.dma_start(hx_t[:], hx.rearrange("(a p t) -> p a t", a=PASSES, t=PACK))
+        nc.sync.dma_start(hz_t[0][:], hz[0:GATHER].partition_broadcast(P))
+        for a in range(PASSES):
+            nc.sync.dma_start(w_raw[a][:], w[a * PASS : (a + 1) * PASS, :].rearrange("(p t) n -> p t n", t=PACK))
+        nc.sync.dma_start(w4w[:].bitcast(I32), w4_words.rearrange("a p c -> p a c").bitcast(I32))
+        for q in range(4):
+            nc.sync.dma_start(
+                w4s[32 * q : 32 * q + 4, :, :].bitcast(I32),
+                w4_scales[:, 4 * q : 4 * q + 4, :].rearrange("a r c -> r a c").bitcast(I32),
+            )
+        for g in range(1, S2 // GATHER):
+            nc.sync.dma_start(hz_t[g][:], hz[g * GATHER : (g + 1) * GATHER].partition_broadcast(P))
+        with nc.allow_non_contiguous_dma(reason="one bias value a partition"):
+            nc.sync.dma_start(b_t[:], b.rearrange("(c p) -> p c", p=P))
+
+        up = keep.tile([P, PASSES, PACK], F32, name="up")
+        down = keep.tile([P, PASSES, PACK], F32, name="down")
+        ln_in = keep.tile([P, 2, PASSES, PACK], F32, name="ln_in")
+        ln_out = keep.tile([P, 2, PASSES, PACK], F32, name="ln_out")
+        ln_pw = keep.tile([P, PASSES, PACK], F32, name="ln_pw")
+        bias = keep.tile([P, PASSES, PACK], F32, name="bias")
+        warm = keep.tile([P, 1], F32, name="warm")
+        nc.gpsimd.tensor_scalar(down[:], pw_t[:], 2.0**60, 2.0**-64, ALU.is_lt, ALU.max)
+        nc.gpsimd.tensor_scalar(up[:], pw_t[:], 2.0**-60, 2.0**63, ALU.is_lt, ALU.mult)
+        nc.gpsimd.tensor_scalar(up[:], up[:], 1.0, 1.0, ALU.max, ALU.mult)
+        nc.gpsimd.tensor_tensor(ln_in[:, 1], up[:], down[:], ALU.mult)
+        nc.gpsimd.tensor_tensor(ln_in[:, 0], pw_t[:], ln_in[:, 1], ALU.mult)
+        nc.scalar.activation(ln_out[:], ln_in[:], ACT.Ln)
+        nc.scalar.activation(warm[:], ln_out[:, 1, 0, 0:1], ACT.Exp)
+        nc.gpsimd.tensor_tensor(ln_pw[:], ln_out[:, 0], ln_out[:, 1], ALU.subtract)
+        nc.gpsimd.tensor_tensor(bias[:], ln_pw[:], hx_t[:], ALU.subtract)
+
+        vw = [keep.tile([P, PASS], U32, name=f"vw{a}", align_bytes=64) for a in range(PASSES)]
+        vs_list = [keep.tile([P, PASS], U8, name=f"vs_list{a}", align_bytes=64) for a in range(PASSES)]
+        vs = [keep.tile([P, PASS], U8, name=f"vs{a}", align_bytes=64) for a in range(PASSES)]
+        v2w = [keep.tile([P, GATHER], U32, name=f"v2w{g}", align_bytes=64) for g in range(S2 // GATHER)]
+        v2s = [keep.tile([P, GATHER], U8, name=f"v2s{g}", align_bytes=64) for g in range(S2 // GATHER)]
+        wq = [keep.tile([P, N], U32, name=f"wq{a}", align_bytes=64) for a in range(PASSES)]
+        wqs = [keep.tile([P, N], U8, name=f"wqs{a}", align_bytes=64) for a in range(PASSES)]
+        cols = GATHER // 16
+
+        def gather_v_scales(a):
+            nc.vector.tensor_copy(vs_list[a][:], tabs[:].indirect(idx[:, a * cols : (a + 1) * cols]))
+
+        def order_v_scales(a):
+            nc.vector.tensor_copy(
+                vs[a][:].rearrange("p (t m) -> p t m", t=PACK), vs_list[a][:].rearrange("p (m t) -> p t m", t=PACK)
+            )
+
+        def gather_v_words(a):
+            nc.vector.tensor_copy(
+                vw[a][:].rearrange("p (t m) -> p m t", t=PACK),
+                tabw[:].bitcast(U32).indirect(idx[:, a * cols : (a + 1) * cols]),
+            )
+
+        def gather_v2_scales(g):
+            nc.vector.tensor_copy(v2s[g][:], tab2s[:].indirect(idx2[:, g * cols : (g + 1) * cols]))
+
+        def gather_v2_words(g):
+            nc.vector.tensor_copy(v2w[g][:], tab2w[:].bitcast(U32).indirect(idx2[:, g * cols : (g + 1) * cols]))
+
+        w_bf = [keep.tile([P, N * PACK], BF16, name=f"w_bf{a}", align_bytes=64) for a in range(PASSES)]
+
+        def round_w(a):
+            nc.scalar.activation(
+                w_bf[a][:].rearrange("p (c i t) -> p c t i", i=4, t=PACK),
+                w_raw[a][:].rearrange("p t (c i) -> p c t i", i=4),
+                ACT.Copy,
+            )
+
+        def quantize_w(a):
+            nc.vector.quantize_mx(out=wq[a][:].bitcast(FP8X4), scales=wqs[a][:], in_=w_bf[a][:])
+
+        starts = [sum(CHUNKS[:c]) for c in range(len(CHUNKS))]
+        units = [(c, a) for c in range(len(CHUNKS)) for a in range(PASSES)]
+        banks, z, h_bf, hq, hqs, acc = {}, {}, {}, {}, {}, {}
+
+        def product_a(u, t):
+            c, a = units[u]
+            g, lo = divmod(starts[c], GATHER)
+            js = slice(lo, lo + CHUNKS[c])
+            banks[u, t] = psum_a.tile([P, GATHER], F32, name="bank_a")
+            nc.tensor.matmul_mx(
+                out=banks[u, t][:, 0 : CHUNKS[c]],
+                lhsT=vw[a][:, t * P : (t + 1) * P].bitcast(FP8X4),
+                lhsT_scale=vs[a][:, t * P : (t + 1) * P],
+                rhs=v2w[g][:, js].bitcast(FP8X4),
+                rhs_scale=v2s[g][V2_ROW:P, js],
+                start=True,
+                stop=True,
+            )
+
+        def exponent(u, t):
+            c, a = units[u]
+            g, lo = divmod(starts[c], GATHER)
+            if t == 0:
+                z[u] = ring.tile([P, PACK, CHUNKS[c]], F32, name="z")
+            nc.vector.scalar_tensor_tensor(
+                z[u][:, t, :], banks[u, t][:, 0 : CHUNKS[c]], bias[:, a, t : t + 1], hz_t[g][:, lo : lo + CHUNKS[c]],
+                ALU.add, ALU.subtract,
+            )
+
+        def kernel_values(u):
+            c, a = units[u]
+            h_bf[u] = ring.tile([P, CHUNKS[c] * PACK], BF16, name="h_bf", align_bytes=64)
+            nc.scalar.activation(
+                h_bf[u][:].rearrange("p (c i t) -> p c t i", i=4, t=PACK),
+                z[u][:].rearrange("p t (c i) -> p c t i", i=4),
+                ACT.Exp,
+            )
+
+        def quantize_h(u):
+            c, a = units[u]
+            hq[u] = ring.tile([P, CHUNKS[c]], U32, name="hq", align_bytes=64)
+            hqs[u] = ring.tile([P, CHUNKS[c]], U8, name="hqs", align_bytes=64)
+            nc.vector.quantize_mx(out=hq[u][:].bitcast(FP8X4), scales=hqs[u][:], in_=h_bf[u][:])
+
+        def y_passes(u, nt, js):
+            c, a = units[u]
+            nc.tensor.matmul_mx(
+                out=acc[c, nt][:, js],
+                lhsT=w4w[:, a, 2 * nt * P : 2 * (nt + 1) * P].bitcast(FP4X4),
+                lhsT_scale=w4s[:, a, nt * P : (nt + 1) * P],
+                rhs=hq[u][:, js].bitcast(FP8X4),
+                rhs_scale=hqs[u][:, js],
+                start=(a == 0),
+                stop=False,
+            )
+            nc.tensor.matmul_mx(
+                out=acc[c, nt][:, js],
+                lhsT=wq[a][:, nt * P : (nt + 1) * P].bitcast(FP8X4),
+                lhsT_scale=wqs[a][:, nt * P : (nt + 1) * P],
+                rhs=hq[u][:, js].bitcast(FP8X4),
+                rhs_scale=hqs[u][:, js],
+                start=False,
+                stop=(a == PASSES - 1),
+            )
+
+        def product_y(u, nt):
+            c, a = units[u]
+            width = CHUNKS[c]
+            if a == 0:
+                acc[c, nt] = psum_y.tile([P, GATHER], F32, name=f"bank_y{nt}")
+            if width in (P, GATHER):
+                y_passes(u, nt, slice(0, width))
+            elif a == PASSES - 1:
+                for lo in range(0, width, P):
+                    for earlier in range(u - a, u + 1):
+                        y_passes(earlier, nt, slice(lo, lo + P))
+            if a == PASSES - 1:
+                res = outp.tile([P, width], F32, name="res")
+                if (c, nt) in [(len(CHUNKS) - 1, 1), (len(CHUNKS) - 1, 3)]:
+                    nc.vector.tensor_scalar(res[:], acc[c, nt][:, 0:width], b_t[:, nt : nt + 1], None, ALU.add)
+                else:
+                    nc.scalar.activation(res[:], acc[c, nt][:, 0:width], ACT.Identity, bias=b_t[:, nt : nt + 1])
+                nc.sync.dma_start(out[nt * P : (nt + 1) * P, starts[c] : starts[c] + width], res[:])
+
+        gather_v_scales(0)
+        gather_v2_scales(0)
+        order_v_scales(0)
+        gather_v_words(0)
+        gather_v2_words(0)
+        for t in range(PACK):
+            product_a(0, t)
+        gather_v_scales(1)
+        gather_v_words(1)
+        order_v_scales(1)
+        round_w(0)
+        gathered = 1
+        for u in range(len(units) + 2):
+            for t in range(PACK):
+                if u < len(units):
+                    exponent(u, t)
+                if u + 1 < len(units):
+                    product_a(u + 1, t)
+                if u >= 2:
+                    product_y(u - 2, t)
+            if u < len(units):
+                kernel_values(u)
+            if u + 2 < len(units) and starts[units[u + 2][0]] // GATHER == gathered:
+                gather_v2_scales(gathered)
+                gather_v2_words(gathered)
+                gathered += 1
+            if u == 0:
+                round_w(1)
+            if u < PASSES:
+                quantize_w(u)
+            if 1 <= u <= len(units):
+                quantize_h(u - 1)

@@ -22,7 +22,7 @@ PASS = P * PACK
 PASSES = S // PASS
 N_TILES = N // P
 GATHER = 512
-CHUNKS = [512,512,512]
+CHUNKS = [512,512,256,128,128]
 V2_ROW = 4
 
 
@@ -32,8 +32,8 @@ def tile_list_gp_inducing_mean_kernel(
     nc = tc.nc
     with ExitStack() as ctx:
         keep = ctx.enter_context(tc.tile_pool(name="keep", bufs=1))
-        ring = ctx.enter_context(tc.tile_pool(name="ring", bufs=3))
-        outp = ctx.enter_context(tc.tile_pool(name="outp", bufs=4))
+        ring = ctx.enter_context(tc.tile_pool(name="ring", bufs=4))
+        outp = ctx.enter_context(tc.tile_pool(name="outp", bufs=1))
         psum_a = ctx.enter_context(tc.psum_pool(name="psum_a", bufs=4))
         psum_y = ctx.enter_context(tc.psum_pool(name="psum_y", bufs=1))
 
@@ -53,34 +53,36 @@ def tile_list_gp_inducing_mean_kernel(
 
         nc.vector.memset(tabs[:].bitcast(I32), 0)
         nc.vector.memset(tab2s[:].bitcast(I32), 0)
-        nc.vector.memset(w4s[:].bitcast(I32), 0)
+        nc.gpsimd.memset(w4s[:].bitcast(I32), 0)
+
+        def load_scales(tile, row, source, quads):
+            for q in quads:
+                nc.sync.dma_start(
+                    tile[32 * q + row : 32 * q + row + 4, :].bitcast(I32), source[0, 4 * q : 4 * q + 4, :].bitcast(I32)
+                )
 
         nc.sync.dma_start(idx[:], offs)
-        for q in range(4):
-            nc.sync.dma_start(tabs[32 * q : 32 * q + 4, :].bitcast(I32), tab_scales[0, 4 * q : 4 * q + 4, :].bitcast(I32))
-        nc.sync.dma_start(tabw[:], tab_words[0].rearrange("p t i -> p (t i)").bitcast(I32))
         nc.sync.dma_start(idx2[:], offs2)
+        load_scales(tabs, 0, tab_scales, range(4))
+        load_scales(tab2s, V2_ROW, tab2_scales, range(1))
+        nc.sync.dma_start(tabw[:], tab_words[0].rearrange("p t i -> p (t i)").bitcast(I32))
+        load_scales(tab2s, V2_ROW, tab2_scales, range(1, 4))
+        nc.sync.dma_start(pw_t[:], pw.rearrange("(a p t) -> p a t", a=PASSES, t=PACK))
+        nc.sync.dma_start(hx_t[:], hx.rearrange("(a p t) -> p a t", a=PASSES, t=PACK))
         nc.sync.dma_start(tab2w[:], tab2_words[0].rearrange("p t i -> p (t i)").bitcast(I32))
-        for q in range(4):
-            nc.scalar.dma_start(
-                tab2s[32 * q + V2_ROW : 32 * q + V2_ROW + 4, :].bitcast(I32),
-                tab2_scales[0, 4 * q : 4 * q + 4, :].bitcast(I32),
-            )
-        nc.scalar.dma_start(pw_t[:], pw.rearrange("(a p t) -> p a t", a=PASSES, t=PACK))
-        nc.scalar.dma_start(hx_t[:], hx.rearrange("(a p t) -> p a t", a=PASSES, t=PACK))
         nc.sync.dma_start(hz_t[0][:], hz[0:GATHER].partition_broadcast(P))
-        for a in range(PASSES):
-            nc.sync.dma_start(w_raw[a][:], w[a * PASS : (a + 1) * PASS, :].rearrange("(p t) n -> p t n", t=PACK))
+        nc.sync.dma_start(w_raw[0][:], w[0:PASS, :].rearrange("(p t) n -> p t n", t=PACK))
+        nc.sync.dma_start(w_raw[1][:], w[PASS : 2 * PASS, :].rearrange("(p t) n -> p t n", t=PACK))
+        nc.sync.dma_start(hz_t[1][:], hz[GATHER : 2 * GATHER].partition_broadcast(P))
         nc.sync.dma_start(w4w[:].bitcast(I32), w4_words.rearrange("a p c -> p a c").bitcast(I32))
         for q in range(4):
             nc.sync.dma_start(
                 w4s[32 * q : 32 * q + 4, :, :].bitcast(I32),
                 w4_scales[:, 4 * q : 4 * q + 4, :].rearrange("a r c -> r a c").bitcast(I32),
             )
-        for g in range(1, S2 // GATHER):
-            nc.sync.dma_start(hz_t[g][:], hz[g * GATHER : (g + 1) * GATHER].partition_broadcast(P))
         with nc.allow_non_contiguous_dma(reason="one bias value a partition"):
             nc.sync.dma_start(b_t[:], b.rearrange("(c p) -> p c", p=P))
+        nc.sync.dma_start(hz_t[2][:], hz[2 * GATHER : 3 * GATHER].partition_broadcast(P))
 
         up = keep.tile([P, PASSES, PACK], F32, name="up")
         down = keep.tile([P, PASSES, PACK], F32, name="down")
@@ -99,31 +101,14 @@ def tile_list_gp_inducing_mean_kernel(
         nc.gpsimd.tensor_tensor(ln_pw[:], ln_out[:, 0], ln_out[:, 1], ALU.subtract)
         nc.gpsimd.tensor_tensor(bias[:], ln_pw[:], hx_t[:], ALU.subtract)
 
-        vw = [keep.tile([P, PASS], U32, name=f"vw{a}", align_bytes=64) for a in range(PASSES)]
-        vs_list = [keep.tile([P, PASS], U8, name=f"vs_list{a}", align_bytes=64) for a in range(PASSES)]
-        vs = [keep.tile([P, PASS], U8, name=f"vs{a}", align_bytes=64) for a in range(PASSES)]
+        vw = keep.tile([P, PASSES, PASS], U32, name="vw", align_bytes=64)
+        vs_list = keep.tile([P, S], U8, name="vs_list", align_bytes=64)
+        vs = keep.tile([P, PASSES, PASS], U8, name="vs", align_bytes=64)
         v2w = [keep.tile([P, GATHER], U32, name=f"v2w{g}", align_bytes=64) for g in range(S2 // GATHER)]
-        v2s = [keep.tile([P, GATHER], U8, name=f"v2s{g}", align_bytes=64) for g in range(S2 // GATHER)]
+        v2s = keep.tile([P, S2], U8, name="v2s", align_bytes=64)
         wq = [keep.tile([P, N], U32, name=f"wq{a}", align_bytes=64) for a in range(PASSES)]
         wqs = [keep.tile([P, N], U8, name=f"wqs{a}", align_bytes=64) for a in range(PASSES)]
         cols = GATHER // 16
-
-        def gather_v_scales(a):
-            nc.vector.tensor_copy(vs_list[a][:], tabs[:].indirect(idx[:, a * cols : (a + 1) * cols]))
-
-        def order_v_scales(a):
-            nc.vector.tensor_copy(
-                vs[a][:].rearrange("p (t m) -> p t m", t=PACK), vs_list[a][:].rearrange("p (m t) -> p t m", t=PACK)
-            )
-
-        def gather_v_words(a):
-            nc.vector.tensor_copy(
-                vw[a][:].rearrange("p (t m) -> p m t", t=PACK),
-                tabw[:].bitcast(U32).indirect(idx[:, a * cols : (a + 1) * cols]),
-            )
-
-        def gather_v2_scales(g):
-            nc.vector.tensor_copy(v2s[g][:], tab2s[:].indirect(idx2[:, g * cols : (g + 1) * cols]))
 
         def gather_v2_words(g):
             nc.vector.tensor_copy(v2w[g][:], tab2w[:].bitcast(U32).indirect(idx2[:, g * cols : (g + 1) * cols]))
@@ -142,7 +127,7 @@ def tile_list_gp_inducing_mean_kernel(
 
         starts = [sum(CHUNKS[:c]) for c in range(len(CHUNKS))]
         units = [(c, a) for c in range(len(CHUNKS)) for a in range(PASSES)]
-        banks, z, h_bf, hq, hqs, acc = {}, {}, {}, {}, {}, {}
+        banks, z, h_bf, hq, hqs, acc, res = {}, {}, {}, {}, {}, {}, {}
 
         def product_a(u, t):
             c, a = units[u]
@@ -151,10 +136,10 @@ def tile_list_gp_inducing_mean_kernel(
             banks[u, t] = psum_a.tile([P, GATHER], F32, name="bank_a")
             nc.tensor.matmul_mx(
                 out=banks[u, t][:, 0 : CHUNKS[c]],
-                lhsT=vw[a][:, t * P : (t + 1) * P].bitcast(FP8X4),
-                lhsT_scale=vs[a][:, t * P : (t + 1) * P],
+                lhsT=vw[:, a, t * P : (t + 1) * P].bitcast(FP8X4),
+                lhsT_scale=vs[:, a, t * P : (t + 1) * P],
                 rhs=v2w[g][:, js].bitcast(FP8X4),
-                rhs_scale=v2s[g][V2_ROW:P, js],
+                rhs_scale=v2s[V2_ROW:P, starts[c] : starts[c] + CHUNKS[c]],
                 start=True,
                 stop=True,
             )
@@ -217,24 +202,30 @@ def tile_list_gp_inducing_mean_kernel(
                     for earlier in range(u - a, u + 1):
                         y_passes(earlier, nt, slice(lo, lo + P))
             if a == PASSES - 1:
-                res = outp.tile([P, width], F32, name="res")
-                if (c, nt) in [(len(CHUNKS) - 1, 1), (len(CHUNKS) - 1, 3)]:
-                    nc.vector.tensor_scalar(res[:], acc[c, nt][:, 0:width], b_t[:, nt : nt + 1], None, ALU.add)
+                if nt == 0:
+                    res[c] = outp.tile([P, N_TILES, width], F32, name=f"res{c}")
+                if (c, nt) in [(2, 3), (3, 1), (3, 3), (4, 1), (4, 3)]:
+                    nc.vector.tensor_scalar(res[c][:, nt, :], acc[c, nt][:, 0:width], b_t[:, nt : nt + 1], None, ALU.add)
                 else:
-                    nc.scalar.activation(res[:], acc[c, nt][:, 0:width], ACT.Identity, bias=b_t[:, nt : nt + 1])
-                nc.sync.dma_start(out[nt * P : (nt + 1) * P, starts[c] : starts[c] + width], res[:])
+                    nc.scalar.activation(res[c][:, nt, :], acc[c, nt][:, 0:width], ACT.Identity, bias=b_t[:, nt : nt + 1])
+                per_store = 1 if width == GATHER else 2
+                if (nt + 1) % per_store == 0:
+                    first = nt + 1 - per_store
+                    nc.sync.dma_start(
+                        out[first * P : (nt + 1) * P, starts[c] : starts[c] + width].rearrange("(s p) j -> p s j", p=P),
+                        res[c][:, first : nt + 1, :],
+                    )
 
-        gather_v_scales(0)
-        gather_v2_scales(0)
-        order_v_scales(0)
-        gather_v_words(0)
+        round_w(0)
+        nc.vector.tensor_copy(vs_list[:], tabs[:].indirect(idx[:]))
+        nc.vector.tensor_copy(v2s[:], tab2s[:].indirect(idx2[:]))
+        nc.vector.tensor_copy(
+            vs[:].rearrange("p a (t m) -> p a t m", t=PACK), vs_list[:].rearrange("p (a m t) -> p a t m", a=PASSES, t=PACK)
+        )
+        nc.vector.tensor_copy(vw[:].rearrange("p a (t m) -> p a m t", t=PACK), tabw[:].bitcast(U32).indirect(idx[:]))
         gather_v2_words(0)
         for t in range(PACK):
             product_a(0, t)
-        gather_v_scales(1)
-        gather_v_words(1)
-        order_v_scales(1)
-        round_w(0)
         gathered = 1
         for u in range(len(units) + 2):
             for t in range(PACK):
@@ -247,7 +238,6 @@ def tile_list_gp_inducing_mean_kernel(
             if u < len(units):
                 kernel_values(u)
             if u + 2 < len(units) and starts[units[u + 2][0]] // GATHER == gathered:
-                gather_v2_scales(gathered)
                 gather_v2_words(gathered)
                 gathered += 1
             if u == 0:

@@ -1,6 +1,7 @@
 from contextlib import ExitStack
 
 import concourse.mybir as mybir
+from concourse.masks import make_identity
 
 K, T, S, T2, S2, N = 512, 2048, 1024, 4096, 1536, 512
 FLOPS = 2 * K * S * S2 + 2 * 2 * S * N * S2
@@ -22,8 +23,18 @@ PASS = P * PACK
 PASSES = S // PASS
 N_TILES = N // P
 GATHER = 512
-CHUNKS = [512,512,256,128,128]
+BANK = 512
+CHUNKS = [512, 512, 384, 128]
 V2_ROW = 4
+
+
+def pieces(width, allowed):
+    runs, lo = [], 0
+    while lo < width:
+        step = max(n for n in allowed if n <= width - lo)
+        runs.append(slice(lo, lo + step))
+        lo = lo + step
+    return runs
 
 
 def tile_list_gp_inducing_mean_kernel(
@@ -33,9 +44,8 @@ def tile_list_gp_inducing_mean_kernel(
     with ExitStack() as ctx:
         keep = ctx.enter_context(tc.tile_pool(name="keep", bufs=1))
         ring = ctx.enter_context(tc.tile_pool(name="ring", bufs=4))
-        outp = ctx.enter_context(tc.tile_pool(name="outp", bufs=1))
         psum_a = ctx.enter_context(tc.psum_pool(name="psum_a", bufs=4))
-        psum_y = ctx.enter_context(tc.psum_pool(name="psum_y", bufs=1))
+        psum_y = ctx.enter_context(tc.psum_pool(name="psum_y", bufs=4))
 
         idx = keep.tile([P, S // 16], U16, name="idx")
         idx2 = keep.tile([P, S2 // 16], U16, name="idx2")
@@ -45,35 +55,36 @@ def tile_list_gp_inducing_mean_kernel(
         tab2s = keep.tile([P, T2], U8, name="tab2s", align_bytes=64)
         w4w = keep.tile([P, PASSES, 2 * N], U8, name="w4w", align_bytes=64)
         w4s = keep.tile([P, PASSES, N], U8, name="w4s", align_bytes=64)
-        hx_t = keep.tile([P, PASSES, PACK], F32, name="hx_t")
+        hx_t = keep.tile([P, PASSES, PACK], F32, name="hx_t", align_bytes=64)
         pw_t = keep.tile([P, PASSES, PACK], F32, name="pw_t")
         b_t = keep.tile([P, N_TILES], F32, name="b_t")
-        hz_t = [keep.tile([P, GATHER], F32, name=f"hz_t{g}") for g in range(S2 // GATHER)]
-        w_raw = [keep.tile([P, PACK, N], F32, name=f"w_raw{a}") for a in range(PASSES)]
+        hz_col = keep.tile([P, S2 // GATHER, PACK], F32, name="hz_col")
+        hz_t = [keep.tile([P, GATHER], F32, name=f"hz_t{g}", align_bytes=64) for g in range(S2 // GATHER)]
+        w_raw = [keep.tile([P, PACK, N], F32, name=f"w_raw{a}", align_bytes=64) for a in range(PASSES)]
+        ident = keep.tile([P, P], F32, name="ident")
 
         nc.vector.memset(tabs[:].bitcast(I32), 0)
         nc.vector.memset(tab2s[:].bitcast(I32), 0)
+        make_identity(nc, ident[:])
         nc.gpsimd.memset(w4s[:].bitcast(I32), 0)
 
-        def load_scales(tile, row, source, quads):
-            for q in quads:
+        def load_scales(tile, row, source):
+            for q in range(4):
                 nc.sync.dma_start(
                     tile[32 * q + row : 32 * q + row + 4, :].bitcast(I32), source[0, 4 * q : 4 * q + 4, :].bitcast(I32)
                 )
 
         nc.sync.dma_start(idx[:], offs)
         nc.sync.dma_start(idx2[:], offs2)
-        load_scales(tabs, 0, tab_scales, range(4))
-        load_scales(tab2s, V2_ROW, tab2_scales, range(1))
+        load_scales(tabs, 0, tab_scales)
         nc.sync.dma_start(tabw[:], tab_words[0].rearrange("p t i -> p (t i)").bitcast(I32))
-        load_scales(tab2s, V2_ROW, tab2_scales, range(1, 4))
+        nc.sync.dma_start(hz_col[:], hz.rearrange("(g p c) -> p g c", p=P, c=PACK))
         nc.sync.dma_start(pw_t[:], pw.rearrange("(a p t) -> p a t", a=PASSES, t=PACK))
-        nc.sync.dma_start(hx_t[:], hx.rearrange("(a p t) -> p a t", a=PASSES, t=PACK))
+        load_scales(tab2s, V2_ROW, tab2_scales)
         nc.sync.dma_start(tab2w[:], tab2_words[0].rearrange("p t i -> p (t i)").bitcast(I32))
-        nc.sync.dma_start(hz_t[0][:], hz[0:GATHER].partition_broadcast(P))
+        nc.sync.dma_start(hx_t[:], hx.rearrange("(a p t) -> p a t", a=PASSES, t=PACK))
         nc.sync.dma_start(w_raw[0][:], w[0:PASS, :].rearrange("(p t) n -> p t n", t=PACK))
         nc.sync.dma_start(w_raw[1][:], w[PASS : 2 * PASS, :].rearrange("(p t) n -> p t n", t=PACK))
-        nc.sync.dma_start(hz_t[1][:], hz[GATHER : 2 * GATHER].partition_broadcast(P))
         nc.sync.dma_start(w4w[:].bitcast(I32), w4_words.rearrange("a p c -> p a c").bitcast(I32))
         for q in range(4):
             nc.sync.dma_start(
@@ -82,81 +93,99 @@ def tile_list_gp_inducing_mean_kernel(
             )
         with nc.allow_non_contiguous_dma(reason="one bias value a partition"):
             nc.sync.dma_start(b_t[:], b.rearrange("(c p) -> p c", p=P))
-        nc.sync.dma_start(hz_t[2][:], hz[2 * GATHER : 3 * GATHER].partition_broadcast(P))
 
-        up = keep.tile([P, PASSES, PACK], F32, name="up")
-        down = keep.tile([P, PASSES, PACK], F32, name="down")
-        ln_in = keep.tile([P, 2, PASSES, PACK], F32, name="ln_in")
-        ln_out = keep.tile([P, 2, PASSES, PACK], F32, name="ln_out")
-        ln_pw = keep.tile([P, PASSES, PACK], F32, name="ln_pw")
+        for g in range(S2 // GATHER):
+            spread = psum_y.tile([P, BANK], F32, name="bank_y")
+            for c in range(PACK):
+                nc.tensor.transpose(spread[:, c * P : (c + 1) * P], hz_col[:, g, c : c + 1].to_broadcast([P, P]), ident[:])
+            nc.scalar.copy(hz_t[g][:].rearrange("p (m c) -> p m c", c=PACK), spread[:].rearrange("p (c m) -> p m c", c=PACK))
+
+        ln_in = keep.tile([P, 3, PASSES * PACK], F32, name="ln_in")
+        terms = keep.tile([P, 4, PASSES * PACK], F32, name="terms")
         bias = keep.tile([P, PASSES, PACK], F32, name="bias")
         warm = keep.tile([P, 1], F32, name="warm")
-        nc.gpsimd.tensor_scalar(down[:], pw_t[:], 2.0**60, 2.0**-64, ALU.is_lt, ALU.max)
-        nc.gpsimd.tensor_scalar(up[:], pw_t[:], 2.0**-60, 2.0**63, ALU.is_lt, ALU.mult)
-        nc.gpsimd.tensor_scalar(up[:], up[:], 1.0, 1.0, ALU.max, ALU.mult)
-        nc.gpsimd.tensor_tensor(ln_in[:, 1], up[:], down[:], ALU.mult)
-        nc.gpsimd.tensor_tensor(ln_in[:, 0], pw_t[:], ln_in[:, 1], ALU.mult)
-        nc.scalar.activation(ln_out[:], ln_in[:], ACT.Ln)
-        nc.scalar.activation(warm[:], ln_out[:, 1, 0, 0:1], ACT.Exp)
-        nc.gpsimd.tensor_tensor(ln_pw[:], ln_out[:, 0], ln_out[:, 1], ALU.subtract)
-        nc.gpsimd.tensor_tensor(bias[:], ln_pw[:], hx_t[:], ALU.subtract)
+        pw_flat = pw_t[:].rearrange("p a t -> p (a t)")
+        nc.vector.tensor_scalar(ln_in[:, 0, :], pw_flat, 2.0**-64, 2.0**64, ALU.max, ALU.min)
+        nc.vector.tensor_scalar(ln_in[:, 1, :], pw_flat, 2.0**64, 2.0**-64, ALU.max, ALU.mult)
+        nc.vector.tensor_scalar(ln_in[:, 2, :], pw_flat, 2.0**-64, 2.0**64, ALU.min, ALU.mult)
+        nc.scalar.activation(terms[:, 0:3, :], ln_in[:], ACT.Ln)
+        nc.scalar.activation(warm[:], terms[:, 1, 0:1], ACT.Exp)
+        nc.scalar.activation(terms[:, 3, :], hx_t[:].rearrange("p a t -> p (a t)"), ACT.Copy, scale=-1.0)
+        nc.vector.tensor_reduce(
+            bias[:].rearrange("p a t -> p (a t)"), terms[:].rearrange("p k i -> p i k"), mybir.AxisListType.X, ALU.add
+        )
 
         vw = keep.tile([P, PASSES, PASS], U32, name="vw", align_bytes=64)
         vs_list = keep.tile([P, S], U8, name="vs_list", align_bytes=64)
         vs = keep.tile([P, PASSES, PASS], U8, name="vs", align_bytes=64)
-        v2w = [keep.tile([P, GATHER], U32, name=f"v2w{g}", align_bytes=64) for g in range(S2 // GATHER)]
-        v2s = keep.tile([P, S2], U8, name="v2s", align_bytes=64)
         wq = [keep.tile([P, N], U32, name=f"wq{a}", align_bytes=64) for a in range(PASSES)]
         wqs = [keep.tile([P, N], U8, name=f"wqs{a}", align_bytes=64) for a in range(PASSES)]
+        w_bf = [keep.tile([P, N * PACK], BF16, name=f"w_bf{a}", align_bytes=64) for a in range(PASSES)]
         cols = GATHER // 16
+        v2w, v2s = {}, {}
 
-        def gather_v2_words(g):
+        def gather_v2_scales(first, count, tag):
+            gathered = keep.tile([P, count * GATHER], U8, name=tag, align_bytes=64)
+            nc.vector.tensor_copy(gathered[:], tab2s[:].indirect(idx2[:, first * cols : (first + count) * cols]))
+            for g in range(count):
+                v2s[first + g] = gathered[V2_ROW:P, g * GATHER : (g + 1) * GATHER]
+
+        def gather_v2_words(g, tag):
+            v2w[g] = keep.tile([P, GATHER], U32, name=tag, align_bytes=64)
             nc.vector.tensor_copy(v2w[g][:], tab2w[:].bitcast(U32).indirect(idx2[:, g * cols : (g + 1) * cols]))
 
-        w_bf = [keep.tile([P, N * PACK], BF16, name=f"w_bf{a}", align_bytes=64) for a in range(PASSES)]
-
-        def round_w(a):
+        def round_w_scalar(a):
             nc.scalar.activation(
                 w_bf[a][:].rearrange("p (c i t) -> p c t i", i=4, t=PACK),
                 w_raw[a][:].rearrange("p t (c i) -> p c t i", i=4),
                 ACT.Copy,
             )
 
+        def round_w_gpsimd(a):
+            for nt in range(N_TILES):
+                nc.gpsimd.tensor_scalar(
+                    w_bf[a][:, nt * PASS : (nt + 1) * PASS].rearrange("p (n t) -> p n t", t=PACK),
+                    w_raw[a][:, :, nt * P : (nt + 1) * P].rearrange("p t n -> p n t"),
+                    1.0, 0.0, ALU.mult, ALU.add,
+                )
+
         def quantize_w(a):
             nc.vector.quantize_mx(out=wq[a][:].bitcast(FP8X4), scales=wqs[a][:], in_=w_bf[a][:])
 
         starts = [sum(CHUNKS[:c]) for c in range(len(CHUNKS))]
         units = [(c, a) for c in range(len(CHUNKS)) for a in range(PASSES)]
-        banks, z, h_bf, hq, hqs, acc, res = {}, {}, {}, {}, {}, {}, {}
+        slabs, z, h_bf, hq, hqs, acc = {}, {}, {}, {}, {}, {}
 
         def product_a(u, t):
             c, a = units[u]
             g, lo = divmod(starts[c], GATHER)
-            js = slice(lo, lo + CHUNKS[c])
-            banks[u, t] = psum_a.tile([P, GATHER], F32, name="bank_a")
-            nc.tensor.matmul_mx(
-                out=banks[u, t][:, 0 : CHUNKS[c]],
-                lhsT=vw[:, a, t * P : (t + 1) * P].bitcast(FP8X4),
-                lhsT_scale=vs[:, a, t * P : (t + 1) * P],
-                rhs=v2w[g][:, js].bitcast(FP8X4),
-                rhs_scale=v2s[V2_ROW:P, starts[c] : starts[c] + CHUNKS[c]],
-                start=True,
-                stop=True,
-            )
+            width = CHUNKS[c]
+            share = BANK // width
+            if t % share == 0:
+                slabs[u] = psum_a.tile([P, BANK], F32, name="bank_a")
+            slabs[u, t] = slabs[u][:, (t % share) * width : (t % share + 1) * width]
+            for js in pieces(width, (512, 256, 128)):
+                nc.tensor.matmul_mx(
+                    out=slabs[u, t][:, js],
+                    lhsT=vw[:, a, t * P : (t + 1) * P].bitcast(FP8X4),
+                    lhsT_scale=vs[:, a, t * P : (t + 1) * P],
+                    rhs=v2w[g][:, lo + js.start : lo + js.stop].bitcast(FP8X4),
+                    rhs_scale=v2s[g][:, lo + js.start : lo + js.stop],
+                    start=True,
+                    stop=True,
+                )
 
         def exponent(u, t):
             c, a = units[u]
             g, lo = divmod(starts[c], GATHER)
             if t == 0:
-                z[u] = ring.tile([P, PACK, CHUNKS[c]], F32, name="z")
+                z[u] = ring.tile([P, PACK, CHUNKS[c]], F32, name="z", bufs=2)
             nc.vector.scalar_tensor_tensor(
-                z[u][:, t, :], banks[u, t][:, 0 : CHUNKS[c]], bias[:, a, t : t + 1], hz_t[g][:, lo : lo + CHUNKS[c]],
-                ALU.add, ALU.subtract,
+                z[u][:, t, :], slabs[u, t], bias[:, a, t : t + 1], hz_t[g][:, lo : lo + CHUNKS[c]], ALU.add, ALU.subtract
             )
 
         def kernel_values(u):
-            c, a = units[u]
-            h_bf[u] = ring.tile([P, CHUNKS[c] * PACK], BF16, name="h_bf", align_bytes=64)
+            h_bf[u] = keep.tile([P, CHUNKS[units[u][0]] * PACK], BF16, name=f"h_bf{u}", align_bytes=64)
             nc.scalar.activation(
                 h_bf[u][:].rearrange("p (c i t) -> p c t i", i=4, t=PACK),
                 z[u][:].rearrange("p t (c i) -> p c t i", i=4),
@@ -164,70 +193,78 @@ def tile_list_gp_inducing_mean_kernel(
             )
 
         def quantize_h(u):
-            c, a = units[u]
-            hq[u] = ring.tile([P, CHUNKS[c]], U32, name="hq", align_bytes=64)
-            hqs[u] = ring.tile([P, CHUNKS[c]], U8, name="hqs", align_bytes=64)
-            nc.vector.quantize_mx(out=hq[u][:].bitcast(FP8X4), scales=hqs[u][:], in_=h_bf[u][:])
-
-        def y_passes(u, nt, js):
-            c, a = units[u]
-            nc.tensor.matmul_mx(
-                out=acc[c, nt][:, js],
-                lhsT=w4w[:, a, 2 * nt * P : 2 * (nt + 1) * P].bitcast(FP4X4),
-                lhsT_scale=w4s[:, a, nt * P : (nt + 1) * P],
-                rhs=hq[u][:, js].bitcast(FP8X4),
-                rhs_scale=hqs[u][:, js],
-                start=(a == 0),
-                stop=False,
-            )
-            nc.tensor.matmul_mx(
-                out=acc[c, nt][:, js],
-                lhsT=wq[a][:, nt * P : (nt + 1) * P].bitcast(FP8X4),
-                lhsT_scale=wqs[a][:, nt * P : (nt + 1) * P],
-                rhs=hq[u][:, js].bitcast(FP8X4),
-                rhs_scale=hqs[u][:, js],
-                start=False,
-                stop=(a == PASSES - 1),
-            )
+            width = CHUNKS[units[u][0]]
+            hq[u] = keep.tile([P, width], U32, name=f"hq{u}", align_bytes=64)
+            hqs[u] = keep.tile([P, width], U8, name=f"hqs{u}", align_bytes=64)
+            for js in pieces(width, (512, 256, 128)):
+                nc.vector.quantize_mx(
+                    out=hq[u][:, js].bitcast(FP8X4), scales=hqs[u][:, js], in_=h_bf[u][:, PACK * js.start : PACK * js.stop]
+                )
 
         def product_y(u, nt):
             c, a = units[u]
             width = CHUNKS[c]
-            if a == 0:
-                acc[c, nt] = psum_y.tile([P, GATHER], F32, name=f"bank_y{nt}")
-            if width in (P, GATHER):
-                y_passes(u, nt, slice(0, width))
-            elif a == PASSES - 1:
-                for lo in range(0, width, P):
-                    for earlier in range(u - a, u + 1):
-                        y_passes(earlier, nt, slice(lo, lo + P))
-            if a == PASSES - 1:
-                if nt == 0:
-                    res[c] = outp.tile([P, N_TILES, width], F32, name=f"res{c}")
-                if (c, nt) in [(2, 3), (3, 1), (3, 3), (4, 1), (4, 3)]:
-                    nc.vector.tensor_scalar(res[c][:, nt, :], acc[c, nt][:, 0:width], b_t[:, nt : nt + 1], None, ALU.add)
-                else:
-                    nc.scalar.activation(res[c][:, nt, :], acc[c, nt][:, 0:width], ACT.Identity, bias=b_t[:, nt : nt + 1])
-                per_store = 1 if width == GATHER else 2
-                if (nt + 1) % per_store == 0:
-                    first = nt + 1 - per_store
-                    nc.sync.dma_start(
-                        out[first * P : (nt + 1) * P, starts[c] : starts[c] + width].rearrange("(s p) j -> p s j", p=P),
-                        res[c][:, first : nt + 1, :],
-                    )
+            share = min(BANK // width, 2)
+            place = nt % share
+            if a == 0 and place == 0:
+                acc[c, nt // share] = psum_y.tile([P, BANK], F32, name="bank_y")
+            target = acc[c, nt // share][:, place * width : (place + 1) * width]
+            for js in pieces(width, (512, 128)):
+                nc.tensor.matmul_mx(
+                    out=target[:, js],
+                    lhsT=w4w[:, a, 2 * nt * P : 2 * (nt + 1) * P].bitcast(FP4X4),
+                    lhsT_scale=w4s[:, a, nt * P : (nt + 1) * P],
+                    rhs=hq[u][:, js].bitcast(FP8X4),
+                    rhs_scale=hqs[u][:, js],
+                    start=(a == 0 and place == 0 and js.start == 0),
+                    stop=False,
+                )
+            for js in pieces(width, (512, 256, 128)):
+                nc.tensor.matmul_mx(
+                    out=target[:, js],
+                    lhsT=wq[a][:, nt * P : (nt + 1) * P].bitcast(FP8X4),
+                    lhsT_scale=wqs[a][:, nt * P : (nt + 1) * P],
+                    rhs=hq[u][:, js].bitcast(FP8X4),
+                    rhs_scale=hqs[u][:, js],
+                    start=False,
+                    stop=(a == PASSES - 1 and place == share - 1 and js.stop == width),
+                )
 
-        round_w(0)
+        def finish(u, nt):
+            c, a = units[u]
+            width = CHUNKS[c]
+            share = min(BANK // width, 2)
+            if a < PASSES - 1 or nt % share < share - 1:
+                return
+            first = nt + 1 - share
+            bank = acc[c, nt // share][:, 0 : share * width].rearrange("p (s j) -> p s j", s=share)
+            res = keep.tile([P, share, width], F32, name=f"res{c}_{first}")
+            if c >= 2 and nt >= 2:
+                nc.vector.tensor_tensor(
+                    res[:], bank, b_t[:, first : nt + 1].unsqueeze(2).to_broadcast([P, share, width]), ALU.add
+                )
+            else:
+                for k in range(share):
+                    nc.scalar.activation(res[:, k, :], bank[:, k, :], ACT.Identity, bias=b_t[:, first + k : first + k + 1])
+            nc.sync.dma_start(
+                out[first * P : (nt + 1) * P, starts[c] : starts[c] + width].rearrange("(s p) j -> p s j", p=P), res[:]
+            )
+
         nc.vector.tensor_copy(vs_list[:], tabs[:].indirect(idx[:]))
-        nc.vector.tensor_copy(v2s[:], tab2s[:].indirect(idx2[:]))
         nc.vector.tensor_copy(
-            vs[:].rearrange("p a (t m) -> p a t m", t=PACK), vs_list[:].rearrange("p (a m t) -> p a t m", a=PASSES, t=PACK)
+            vs[:].rearrange("p a (t m) -> p a m t", t=PACK), vs_list[:].rearrange("p (a m t) -> p a m t", a=PASSES, t=PACK)
         )
         nc.vector.tensor_copy(vw[:].rearrange("p a (t m) -> p a m t", t=PACK), tabw[:].bitcast(U32).indirect(idx[:]))
-        gather_v2_words(0)
+        gather_v2_scales(0, 2, "v2s0")
+        gather_v2_words(0, "v2w0")
+        gather_v2_words(1, "v2w1")
+        round_w_scalar(0)
+        round_w_gpsimd(1)
         for t in range(PACK):
             product_a(0, t)
-        gathered = 1
         for u in range(len(units) + 2):
+            if u == 1:
+                quantize_w(0)
             for t in range(PACK):
                 if u < len(units):
                     exponent(u, t)
@@ -237,12 +274,13 @@ def tile_list_gp_inducing_mean_kernel(
                     product_y(u - 2, t)
             if u < len(units):
                 kernel_values(u)
-            if u + 2 < len(units) and starts[units[u + 2][0]] // GATHER == gathered:
-                gather_v2_words(gathered)
-                gathered += 1
-            if u == 0:
-                round_w(1)
-            if u < PASSES:
-                quantize_w(u)
             if 1 <= u <= len(units):
                 quantize_h(u - 1)
+            if u >= 2:
+                for nt in range(N_TILES):
+                    finish(u - 2, nt)
+            if u == 1:
+                quantize_w(1)
+            if u == 2:
+                gather_v2_scales(2, 1, "w_bf1")
+                gather_v2_words(2, "h_bf1")

@@ -69,10 +69,8 @@ def tile_list_gp_inducing_mean_kernel(
         nc.gpsimd.memset(w4s[:].bitcast(I32), 0)
 
         def load_scales(tile, row, source):
-            for q in range(4):
-                nc.sync.dma_start(
-                    tile[32 * q + row : 32 * q + row + 4, :].bitcast(I32), source[0, 4 * q : 4 * q + 4, :].bitcast(I32)
-                )
+            for r in range(4):
+                nc.sync.dma_start(tile[row + r : P : 32, :].bitcast(I32), source[0, r:16:4, :].bitcast(I32))
 
         nc.sync.dma_start(idx[:], offs)
         nc.sync.dma_start(idx2[:], offs2)
@@ -86,10 +84,9 @@ def tile_list_gp_inducing_mean_kernel(
         nc.sync.dma_start(w_raw[0][:], w[0:PASS, :].rearrange("(p t) n -> p t n", t=PACK))
         nc.sync.dma_start(w_raw[1][:], w[PASS : 2 * PASS, :].rearrange("(p t) n -> p t n", t=PACK))
         nc.sync.dma_start(w4w[:].bitcast(I32), w4_words.rearrange("a p c -> p a c").bitcast(I32))
-        for q in range(4):
+        for r in range(4):
             nc.sync.dma_start(
-                w4s[32 * q : 32 * q + 4, :, :].bitcast(I32),
-                w4_scales[:, 4 * q : 4 * q + 4, :].rearrange("a r c -> r a c").bitcast(I32),
+                w4s[r:P:32, :, :].bitcast(I32), w4_scales[:, r:16:4, :].rearrange("a q c -> q a c").bitcast(I32)
             )
         with nc.allow_non_contiguous_dma(reason="one bias value a partition"):
             nc.sync.dma_start(b_t[:], b.rearrange("(c p) -> p c", p=P))
@@ -239,7 +236,7 @@ def tile_list_gp_inducing_mean_kernel(
             first = nt + 1 - share
             bank = acc[c, nt // share][:, 0 : share * width].rearrange("p (s j) -> p s j", s=share)
             res = keep.tile([P, share, width], F32, name=f"res{c}_{first}")
-            if c >= 2 and nt >= 2:
+            if c == 3 and nt >= 2:
                 nc.vector.tensor_tensor(
                     res[:], bank, b_t[:, first : nt + 1].unsqueeze(2).to_broadcast([P, share, width]), ALU.add
                 )
@@ -259,7 +256,7 @@ def tile_list_gp_inducing_mean_kernel(
         gather_v2_words(0, "v2w0")
         gather_v2_words(1, "v2w1")
         round_w_scalar(0)
-        round_w_gpsimd(1)
+        round_w_scalar(1)
         for t in range(PACK):
             product_a(0, t)
         for u in range(len(units) + 2):

@@ -58,8 +58,8 @@ def tile_list_gp_inducing_mean_kernel(
         hx_t = keep.tile([P, PASSES, PACK], F32, name="hx_t", align_bytes=64)
         pw_t = keep.tile([P, PASSES, PACK], F32, name="pw_t")
         b_t = keep.tile([P, N_TILES], F32, name="b_t")
-        hz_col = keep.tile([P, S2 // GATHER, PACK], F32, name="hz_col")
-        hz_t = [keep.tile([P, GATHER], F32, name=f"hz_t{g}", align_bytes=64) for g in range(S2 // GATHER)]
+        hz_col = keep.tile([P, S2 // P], F32, name="hz_col")
+        hz_t = keep.tile([P, S2], F32, name="hz_t")
         w_raw = [keep.tile([P, PACK, N], F32, name=f"w_raw{a}", align_bytes=64) for a in range(PASSES)]
         ident = keep.tile([P, P], F32, name="ident")
 
@@ -73,11 +73,11 @@ def tile_list_gp_inducing_mean_kernel(
                 nc.sync.dma_start(tile[row + r : P : 32, :].bitcast(I32), source[0, r:16:4, :].bitcast(I32))
 
         nc.sync.dma_start(idx[:], offs)
-        nc.sync.dma_start(idx2[:], offs2)
-        load_scales(tabs, 0, tab_scales)
-        nc.sync.dma_start(tabw[:], tab_words[0].rearrange("p t i -> p (t i)").bitcast(I32))
-        nc.sync.dma_start(hz_col[:], hz.rearrange("(g p c) -> p g c", p=P, c=PACK))
         nc.sync.dma_start(pw_t[:], pw.rearrange("(a p t) -> p a t", a=PASSES, t=PACK))
+        load_scales(tabs, 0, tab_scales)
+        nc.sync.dma_start(idx2[:], offs2)
+        nc.sync.dma_start(tabw[:], tab_words[0].rearrange("p t i -> p (t i)").bitcast(I32))
+        nc.sync.dma_start(hz_col[:], hz.rearrange("(p c) -> p c", p=P))
         load_scales(tab2s, V2_ROW, tab2_scales)
         nc.sync.dma_start(tab2w[:], tab2_words[0].rearrange("p t i -> p (t i)").bitcast(I32))
         nc.sync.dma_start(hx_t[:], hx.rearrange("(a p t) -> p a t", a=PASSES, t=PACK))
@@ -94,23 +94,36 @@ def tile_list_gp_inducing_mean_kernel(
         for g in range(S2 // GATHER):
             spread = psum_y.tile([P, BANK], F32, name="bank_y")
             for c in range(PACK):
-                nc.tensor.transpose(spread[:, c * P : (c + 1) * P], hz_col[:, g, c : c + 1].to_broadcast([P, P]), ident[:])
-            nc.scalar.copy(hz_t[g][:].rearrange("p (m c) -> p m c", c=PACK), spread[:].rearrange("p (c m) -> p m c", c=PACK))
+                nc.tensor.transpose(spread[:, c * P : (c + 1) * P], hz_col[:, PACK * g + c : PACK * g + c + 1].to_broadcast([P, P]), ident[:])
+            nc.scalar.copy(
+                hz_t[:].rearrange("p (m c) -> p m c", m=P)[:, :, PACK * g : PACK * (g + 1)],
+                spread[:].rearrange("p (c m) -> p m c", c=PACK),
+            )
 
-        ln_in = keep.tile([P, 3, PASSES * PACK], F32, name="ln_in")
-        terms = keep.tile([P, 4, PASSES * PACK], F32, name="terms")
+        ln_in = keep.tile([P, PASSES, PACK, 3], F32, name="ln_in")
+        ln_out = keep.tile([P, PASSES, PACK, 3], F32, name="ln_out")
+        ln_pw = keep.tile([P, PASSES, PACK], F32, name="ln_pw")
         bias = keep.tile([P, PASSES, PACK], F32, name="bias")
+        nc.gpsimd.tensor_scalar(ln_in[:, :, :, 0], pw_t[:], 2.0**-64, 2.0**64, ALU.max, ALU.min)
+        nc.gpsimd.tensor_scalar(ln_in[:, :, :, 1], pw_t[:], 2.0**64, 2.0**-64, ALU.max, ALU.mult)
+        nc.gpsimd.tensor_scalar(ln_in[:, :, :, 2], pw_t[:], 2.0**-64, 2.0**64, ALU.min, ALU.mult)
+        for a in range(PASSES):
+            for t in range(PACK):
+                nc.scalar.activation(ln_out[:, a, t, :], ln_in[:, a, t, :], ACT.Ln, accum_out=ln_pw[:, a, t : t + 1])
         warm = keep.tile([P, 1], F32, name="warm")
-        pw_flat = pw_t[:].rearrange("p a t -> p (a t)")
-        nc.vector.tensor_scalar(ln_in[:, 0, :], pw_flat, 2.0**-64, 2.0**64, ALU.max, ALU.min)
-        nc.vector.tensor_scalar(ln_in[:, 1, :], pw_flat, 2.0**64, 2.0**-64, ALU.max, ALU.mult)
-        nc.vector.tensor_scalar(ln_in[:, 2, :], pw_flat, 2.0**-64, 2.0**64, ALU.min, ALU.mult)
-        nc.scalar.activation(terms[:, 0:3, :], ln_in[:], ACT.Ln)
-        nc.scalar.activation(warm[:], terms[:, 1, 0:1], ACT.Exp)
-        nc.scalar.activation(terms[:, 3, :], hx_t[:].rearrange("p a t -> p (a t)"), ACT.Copy, scale=-1.0)
-        nc.vector.tensor_reduce(
-            bias[:].rearrange("p a t -> p (a t)"), terms[:].rearrange("p k i -> p i k"), mybir.AxisListType.X, ALU.add
-        )
+        nc.scalar.activation(warm[:], ln_pw[:, PASSES - 1, PACK - 1 : PACK], ACT.Exp)
+        for a in range(PASSES):
+            for t in range(PACK):
+                nc.scalar.activation(
+                    bias[:, a, t : t + 1], hx_t[:, a, t : t + 1], ACT.Identity, bias=ln_pw[:, a, t : t + 1], scale=-1.0
+                )
+
+        offsets_last = keep.tile([P, PASSES, PACK, CHUNKS[-1]], F32, name="offsets_last")
+        for a in range(PASSES):
+            for t in range(PACK):
+                nc.scalar.activation(
+                    offsets_last[:, a, t, :], hz_t[:, S2 - CHUNKS[-1] : S2], ACT.Identity, bias=bias[:, a, t : t + 1], scale=-1.0
+                )
 
         vw = keep.tile([P, PASSES, PASS], U32, name="vw", align_bytes=64)
         vs_list = keep.tile([P, S], U8, name="vs_list", align_bytes=64)
@@ -137,14 +150,6 @@ def tile_list_gp_inducing_mean_kernel(
                 w_raw[a][:].rearrange("p t (c i) -> p c t i", i=4),
                 ACT.Copy,
             )
-
-        def round_w_gpsimd(a):
-            for nt in range(N_TILES):
-                nc.gpsimd.tensor_scalar(
-                    w_bf[a][:, nt * PASS : (nt + 1) * PASS].rearrange("p (n t) -> p n t", t=PACK),
-                    w_raw[a][:, :, nt * P : (nt + 1) * P].rearrange("p t n -> p n t"),
-                    1.0, 0.0, ALU.mult, ALU.add,
-                )
 
         def quantize_w(a):
             nc.vector.quantize_mx(out=wq[a][:].bitcast(FP8X4), scales=wqs[a][:], in_=w_bf[a][:])
@@ -174,11 +179,14 @@ def tile_list_gp_inducing_mean_kernel(
 
         def exponent(u, t):
             c, a = units[u]
-            g, lo = divmod(starts[c], GATHER)
             if t == 0:
                 z[u] = ring.tile([P, PACK, CHUNKS[c]], F32, name="z", bufs=2)
+            if c == len(CHUNKS) - 1:
+                if t == PACK - 1:
+                    nc.vector.tensor_tensor(z[u][:], slabs[u][:].rearrange("p (t j) -> p t j", t=PACK), offsets_last[:, a], ALU.add)
+                return
             nc.vector.scalar_tensor_tensor(
-                z[u][:, t, :], slabs[u, t], bias[:, a, t : t + 1], hz_t[g][:, lo : lo + CHUNKS[c]], ALU.add, ALU.subtract
+                z[u][:, t, :], slabs[u, t], bias[:, a, t : t + 1], hz_t[:, starts[c] : starts[c] + CHUNKS[c]], ALU.add, ALU.subtract
             )
 
         def kernel_values(u):
@@ -236,7 +244,7 @@ def tile_list_gp_inducing_mean_kernel(
             first = nt + 1 - share
             bank = acc[c, nt // share][:, 0 : share * width].rearrange("p (s j) -> p s j", s=share)
             res = keep.tile([P, share, width], F32, name=f"res{c}_{first}")
-            if c == 3 and nt >= 2:
+            if c == 1 and nt >= 2 or c == 2 and nt % 2 == 1 or (c, nt) == (3, 3):
                 nc.vector.tensor_tensor(
                     res[:], bank, b_t[:, first : nt + 1].unsqueeze(2).to_broadcast([P, share, width]), ALU.add
                 )

@@ -26,6 +26,8 @@ GATHER = 512
 BANK = 512
 CHUNKS = [512, 512, 384, 128]
 V2_ROW = 4
+HELPED = ((0, 0),)
+SHIFTED = 128
 
 
 def pieces(width, allowed):
@@ -75,12 +77,12 @@ def tile_list_gp_inducing_mean_kernel(
         nc.sync.dma_start(idx[:], offs)
         nc.sync.dma_start(pw_t[:], pw.rearrange("(a p t) -> p a t", a=PASSES, t=PACK))
         load_scales(tabs, 0, tab_scales)
-        nc.sync.dma_start(idx2[:], offs2)
+        nc.sync.dma_start(hx_t[:], hx.rearrange("(a p t) -> p a t", a=PASSES, t=PACK))
         nc.sync.dma_start(tabw[:], tab_words[0].rearrange("p t i -> p (t i)").bitcast(I32))
+        nc.sync.dma_start(idx2[:], offs2)
         nc.sync.dma_start(hz_col[:], hz.rearrange("(p c) -> p c", p=P))
         load_scales(tab2s, V2_ROW, tab2_scales)
         nc.sync.dma_start(tab2w[:], tab2_words[0].rearrange("p t i -> p (t i)").bitcast(I32))
-        nc.sync.dma_start(hx_t[:], hx.rearrange("(a p t) -> p a t", a=PASSES, t=PACK))
         nc.sync.dma_start(w_raw[0][:], w[0:PASS, :].rearrange("(p t) n -> p t n", t=PACK))
         nc.sync.dma_start(w_raw[1][:], w[PASS : 2 * PASS, :].rearrange("(p t) n -> p t n", t=PACK))
         nc.sync.dma_start(w4w[:].bitcast(I32), w4_words.rearrange("a p c -> p a c").bitcast(I32))
@@ -100,16 +102,16 @@ def tile_list_gp_inducing_mean_kernel(
                 spread[:].rearrange("p (c m) -> p m c", c=PACK),
             )
 
-        ln_in = keep.tile([P, PASSES, PACK, 3], F32, name="ln_in")
+        ln_in = keep.tile([P, 3, PASSES, PACK], F32, name="ln_in")
         ln_out = keep.tile([P, PASSES, PACK, 3], F32, name="ln_out")
         ln_pw = keep.tile([P, PASSES, PACK], F32, name="ln_pw")
         bias = keep.tile([P, PASSES, PACK], F32, name="bias")
-        nc.gpsimd.tensor_scalar(ln_in[:, :, :, 0], pw_t[:], 2.0**-64, 2.0**64, ALU.max, ALU.min)
-        nc.gpsimd.tensor_scalar(ln_in[:, :, :, 1], pw_t[:], 2.0**64, 2.0**-64, ALU.max, ALU.mult)
-        nc.gpsimd.tensor_scalar(ln_in[:, :, :, 2], pw_t[:], 2.0**-64, 2.0**64, ALU.min, ALU.mult)
+        nc.vector.tensor_scalar(ln_in[:, 0], pw_t[:], 2.0**-64, 2.0**64, ALU.max, ALU.min)
+        nc.vector.tensor_scalar(ln_in[:, 1], pw_t[:], 2.0**64, 2.0**-64, ALU.max, ALU.mult)
+        nc.vector.tensor_scalar(ln_in[:, 2], pw_t[:], 2.0**-64, 2.0**64, ALU.min, ALU.mult)
         for a in range(PASSES):
             for t in range(PACK):
-                nc.scalar.activation(ln_out[:, a, t, :], ln_in[:, a, t, :], ACT.Ln, accum_out=ln_pw[:, a, t : t + 1])
+                nc.scalar.activation(ln_out[:, a, t, :], ln_in[:, :, a, t], ACT.Ln, accum_out=ln_pw[:, a, t : t + 1])
         warm = keep.tile([P, 1], F32, name="warm")
         nc.scalar.activation(warm[:], ln_pw[:, PASSES - 1, PACK - 1 : PACK], ACT.Exp)
         for a in range(PASSES):
@@ -118,11 +120,11 @@ def tile_list_gp_inducing_mean_kernel(
                     bias[:, a, t : t + 1], hx_t[:, a, t : t + 1], ACT.Identity, bias=ln_pw[:, a, t : t + 1], scale=-1.0
                 )
 
-        offsets_last = keep.tile([P, PASSES, PACK, CHUNKS[-1]], F32, name="offsets_last")
+        shift = keep.tile([P, PASSES, PACK, SHIFTED], F32, name="shift")
         for a in range(PASSES):
             for t in range(PACK):
                 nc.scalar.activation(
-                    offsets_last[:, a, t, :], hz_t[:, S2 - CHUNKS[-1] : S2], ACT.Identity, bias=bias[:, a, t : t + 1], scale=-1.0
+                    shift[:, a, t, :], hz_t[:, S2 - SHIFTED : S2], ACT.Identity, bias=bias[:, a, t : t + 1], scale=-1.0
                 )
 
         vw = keep.tile([P, PASSES, PASS], U32, name="vw", align_bytes=64)
@@ -156,7 +158,7 @@ def tile_list_gp_inducing_mean_kernel(
 
         starts = [sum(CHUNKS[:c]) for c in range(len(CHUNKS))]
         units = [(c, a) for c in range(len(CHUNKS)) for a in range(PASSES)]
-        slabs, z, h_bf, hq, hqs, acc = {}, {}, {}, {}, {}, {}
+        banks, slabs, z, h_bf, hq, hqs, acc = {}, {}, {}, {}, {}, {}, {}
 
         def product_a(u, t):
             c, a = units[u]
@@ -164,8 +166,8 @@ def tile_list_gp_inducing_mean_kernel(
             width = CHUNKS[c]
             share = BANK // width
             if t % share == 0:
-                slabs[u] = psum_a.tile([P, BANK], F32, name="bank_a")
-            slabs[u, t] = slabs[u][:, (t % share) * width : (t % share + 1) * width]
+                banks[u, t // share] = psum_a.tile([P, BANK], F32, name="bank_a")
+            slabs[u, t] = banks[u, t // share][:, (t % share) * width : (t % share + 1) * width]
             for js in pieces(width, (512, 256, 128)):
                 nc.tensor.matmul_mx(
                     out=slabs[u, t][:, js],
@@ -181,9 +183,19 @@ def tile_list_gp_inducing_mean_kernel(
             c, a = units[u]
             if t == 0:
                 z[u] = ring.tile([P, PACK, CHUNKS[c]], F32, name="z", bufs=2)
-            if c == len(CHUNKS) - 1:
-                if t == PACK - 1:
-                    nc.vector.tensor_tensor(z[u][:], slabs[u][:].rearrange("p (t j) -> p t j", t=PACK), offsets_last[:, a], ALU.add)
+            if starts[c] >= S2 - SHIFTED:
+                width = CHUNKS[c]
+                share = BANK // width
+                lo = starts[c] - (S2 - SHIFTED)
+                if t % share == share - 1:
+                    ts = slice(t + 1 - share, t + 1)
+                    bank = banks[u, t // share][:, 0 : share * width].rearrange("p (t j) -> p t j", t=share)
+                    nc.vector.tensor_tensor(z[u][:, ts, :], bank, shift[:, a, ts, lo : lo + width], ALU.add)
+                return
+            if (u, t) in HELPED:
+                biased = keep.tile([P, CHUNKS[c]], F32, name=f"biased{u}_{t}")
+                nc.scalar.activation(biased[:], slabs[u, t], ACT.Identity, bias=bias[:, a, t : t + 1])
+                nc.gpsimd.tensor_tensor(z[u][:, t, :], biased[:], hz_t[:, starts[c] : starts[c] + CHUNKS[c]], ALU.subtract)
                 return
             nc.vector.scalar_tensor_tensor(
                 z[u][:, t, :], slabs[u, t], bias[:, a, t : t + 1], hz_t[:, starts[c] : starts[c] + CHUNKS[c]], ALU.add, ALU.subtract
@@ -263,22 +275,28 @@ def tile_list_gp_inducing_mean_kernel(
         gather_v2_scales(0, 2, "v2s0")
         gather_v2_words(0, "v2w0")
         gather_v2_words(1, "v2w1")
-        round_w_scalar(0)
-        round_w_scalar(1)
         for t in range(PACK):
             product_a(0, t)
         for u in range(len(units) + 2):
             if u == 1:
                 quantize_w(0)
+            narrow = u + 1 < len(units) and CHUNKS[units[u + 1][0]] <= 128
+            if narrow:
+                for t in range(PACK):
+                    product_a(u + 1, t)
             for t in range(PACK):
                 if u < len(units):
                     exponent(u, t)
-                if u + 1 < len(units):
+                if u + 1 < len(units) and not narrow:
                     product_a(u + 1, t)
                 if u >= 2:
                     product_y(u - 2, t)
+            if u == 0:
+                round_w_scalar(0)
             if u < len(units):
                 kernel_values(u)
+            if u == 0:
+                round_w_scalar(1)
             if 1 <= u <= len(units):
                 quantize_h(u - 1)
             if u >= 2:
@@ -287,5 +305,5 @@ def tile_list_gp_inducing_mean_kernel(
             if u == 1:
                 quantize_w(1)
             if u == 2:
-                gather_v2_scales(2, 1, "w_bf1")
+                gather_v2_scales(2, 1, "h_bf0")
                 gather_v2_words(2, "h_bf1")

@@ -22,12 +22,15 @@ PACK = 4
 PASS = P * PACK
 PASSES = S // PASS
 N_TILES = N // P
-GATHER = 512
 BANK = 512
+LINE = 4
+LIST_ROWS = 16
+SCALE_ROWS = 4
+GATHER = 512
 CHUNKS = [512, 512, 384, 128]
+LAST = len(CHUNKS) - 1
 V2_ROW = 4
-HELPED = ((0, 0),)
-SHIFTED = 128
+LN_LOW, LN_HIGH = 2.0**-64, 2.0**64
 
 
 def pieces(width, allowed):
@@ -45,12 +48,12 @@ def tile_list_gp_inducing_mean_kernel(
     nc = tc.nc
     with ExitStack() as ctx:
         keep = ctx.enter_context(tc.tile_pool(name="keep", bufs=1))
-        ring = ctx.enter_context(tc.tile_pool(name="ring", bufs=4))
+        ring = ctx.enter_context(tc.tile_pool(name="ring", bufs=2))
         psum_a = ctx.enter_context(tc.psum_pool(name="psum_a", bufs=4))
         psum_y = ctx.enter_context(tc.psum_pool(name="psum_y", bufs=4))
 
-        idx = keep.tile([P, S // 16], U16, name="idx")
-        idx2 = keep.tile([P, S2 // 16], U16, name="idx2")
+        idx = keep.tile([P, S // LIST_ROWS], U16, name="idx")
+        idx2 = keep.tile([P, S2 // LIST_ROWS], U16, name="idx2")
         tabw = keep.tile([P, T], I32, name="tabw", align_bytes=64)
         tabs = keep.tile([P, T], U8, name="tabs", align_bytes=64)
         tab2w = keep.tile([P, T2], I32, name="tab2w", align_bytes=64)
@@ -70,9 +73,11 @@ def tile_list_gp_inducing_mean_kernel(
         make_identity(nc, ident[:])
         nc.gpsimd.memset(w4s[:].bitcast(I32), 0)
 
-        def load_scales(tile, row, source):
-            for r in range(4):
-                nc.sync.dma_start(tile[row + r : P : 32, :].bitcast(I32), source[0, r:16:4, :].bitcast(I32))
+        def load_scales(tile, first_row, source):
+            for r in range(SCALE_ROWS):
+                nc.sync.dma_start(
+                    tile[first_row + r : P : 32, :].bitcast(I32), source[0, r : 4 * SCALE_ROWS : SCALE_ROWS, :].bitcast(I32)
+                )
 
         nc.sync.dma_start(idx[:], offs)
         nc.sync.dma_start(pw_t[:], pw.rearrange("(a p t) -> p a t", a=PASSES, t=PACK))
@@ -83,35 +88,37 @@ def tile_list_gp_inducing_mean_kernel(
         nc.sync.dma_start(hz_col[:], hz.rearrange("(p c) -> p c", p=P))
         load_scales(tab2s, V2_ROW, tab2_scales)
         nc.sync.dma_start(tab2w[:], tab2_words[0].rearrange("p t i -> p (t i)").bitcast(I32))
-        nc.sync.dma_start(w_raw[0][:], w[0:PASS, :].rearrange("(p t) n -> p t n", t=PACK))
-        nc.sync.dma_start(w_raw[1][:], w[PASS : 2 * PASS, :].rearrange("(p t) n -> p t n", t=PACK))
+        for a in range(PASSES):
+            nc.sync.dma_start(w_raw[a][:], w[a * PASS : (a + 1) * PASS, :].rearrange("(p t) n -> p t n", t=PACK))
         nc.sync.dma_start(w4w[:].bitcast(I32), w4_words.rearrange("a p c -> p a c").bitcast(I32))
-        for r in range(4):
+        for r in range(SCALE_ROWS):
             nc.sync.dma_start(
-                w4s[r:P:32, :, :].bitcast(I32), w4_scales[:, r:16:4, :].rearrange("a q c -> q a c").bitcast(I32)
+                w4s[r:P:32, :, :].bitcast(I32),
+                w4_scales[:, r : 4 * SCALE_ROWS : SCALE_ROWS, :].rearrange("a q c -> q a c").bitcast(I32),
             )
         with nc.allow_non_contiguous_dma(reason="one bias value a partition"):
             nc.sync.dma_start(b_t[:], b.rearrange("(c p) -> p c", p=P))
 
-        for g in range(S2 // GATHER):
+        for group in range(S2 // BANK):
             spread = psum_y.tile([P, BANK], F32, name="bank_y")
-            for c in range(PACK):
-                nc.tensor.transpose(spread[:, c * P : (c + 1) * P], hz_col[:, PACK * g + c : PACK * g + c + 1].to_broadcast([P, P]), ident[:])
+            for c in range(LINE):
+                column = hz_col[:, LINE * group + c : LINE * group + c + 1]
+                nc.tensor.transpose(spread[:, c * P : (c + 1) * P], column.to_broadcast([P, P]), ident[:])
             nc.scalar.copy(
-                hz_t[:].rearrange("p (m c) -> p m c", m=P)[:, :, PACK * g : PACK * (g + 1)],
-                spread[:].rearrange("p (c m) -> p m c", c=PACK),
+                hz_t[:].rearrange("p (m c) -> p m c", m=P)[:, :, LINE * group : LINE * (group + 1)],
+                spread[:].rearrange("p (c m) -> p m c", c=LINE),
             )
 
-        ln_in = keep.tile([P, 3, PASSES, PACK], F32, name="ln_in")
-        ln_out = keep.tile([P, PASSES, PACK, 3], F32, name="ln_out")
+        factors = keep.tile([P, 3, PASSES, PACK], F32, name="factors")
+        ln_factors = keep.tile([P, PASSES, PACK, 3], F32, name="ln_factors")
         ln_pw = keep.tile([P, PASSES, PACK], F32, name="ln_pw")
         bias = keep.tile([P, PASSES, PACK], F32, name="bias")
-        nc.vector.tensor_scalar(ln_in[:, 0], pw_t[:], 2.0**-64, 2.0**64, ALU.max, ALU.min)
-        nc.vector.tensor_scalar(ln_in[:, 1], pw_t[:], 2.0**64, 2.0**-64, ALU.max, ALU.mult)
-        nc.vector.tensor_scalar(ln_in[:, 2], pw_t[:], 2.0**-64, 2.0**64, ALU.min, ALU.mult)
+        nc.vector.tensor_scalar(factors[:, 0], pw_t[:], LN_LOW, LN_HIGH, ALU.max, ALU.min)
+        nc.vector.tensor_scalar(factors[:, 1], pw_t[:], LN_HIGH, LN_LOW, ALU.max, ALU.mult)
+        nc.vector.tensor_scalar(factors[:, 2], pw_t[:], LN_LOW, LN_HIGH, ALU.min, ALU.mult)
         for a in range(PASSES):
             for t in range(PACK):
-                nc.scalar.activation(ln_out[:, a, t, :], ln_in[:, :, a, t], ACT.Ln, accum_out=ln_pw[:, a, t : t + 1])
+                nc.scalar.activation(ln_factors[:, a, t, :], factors[:, :, a, t], ACT.Ln, accum_out=ln_pw[:, a, t : t + 1])
         warm = keep.tile([P, 1], F32, name="warm")
         nc.scalar.activation(warm[:], ln_pw[:, PASSES - 1, PACK - 1 : PACK], ACT.Exp)
         for a in range(PASSES):
@@ -120,11 +127,11 @@ def tile_list_gp_inducing_mean_kernel(
                     bias[:, a, t : t + 1], hx_t[:, a, t : t + 1], ACT.Identity, bias=ln_pw[:, a, t : t + 1], scale=-1.0
                 )
 
-        shift = keep.tile([P, PASSES, PACK, SHIFTED], F32, name="shift")
+        shift = keep.tile([P, PASSES, PACK, CHUNKS[LAST]], F32, name="shift")
         for a in range(PASSES):
             for t in range(PACK):
                 nc.scalar.activation(
-                    shift[:, a, t, :], hz_t[:, S2 - SHIFTED : S2], ACT.Identity, bias=bias[:, a, t : t + 1], scale=-1.0
+                    shift[:, a, t, :], hz_t[:, S2 - CHUNKS[LAST] : S2], ACT.Identity, bias=bias[:, a, t : t + 1], scale=-1.0
                 )
 
         vw = keep.tile([P, PASSES, PASS], U32, name="vw", align_bytes=64)
@@ -133,23 +140,23 @@ def tile_list_gp_inducing_mean_kernel(
         wq = [keep.tile([P, N], U32, name=f"wq{a}", align_bytes=64) for a in range(PASSES)]
         wqs = [keep.tile([P, N], U8, name=f"wqs{a}", align_bytes=64) for a in range(PASSES)]
         w_bf = [keep.tile([P, N * PACK], BF16, name=f"w_bf{a}", align_bytes=64) for a in range(PASSES)]
-        cols = GATHER // 16
+        list_cols = GATHER // LIST_ROWS
         v2w, v2s = {}, {}
 
         def gather_v2_scales(first, count, tag):
             gathered = keep.tile([P, count * GATHER], U8, name=tag, align_bytes=64)
-            nc.vector.tensor_copy(gathered[:], tab2s[:].indirect(idx2[:, first * cols : (first + count) * cols]))
+            nc.vector.tensor_copy(gathered[:], tab2s[:].indirect(idx2[:, first * list_cols : (first + count) * list_cols]))
             for g in range(count):
                 v2s[first + g] = gathered[V2_ROW:P, g * GATHER : (g + 1) * GATHER]
 
         def gather_v2_words(g, tag):
             v2w[g] = keep.tile([P, GATHER], U32, name=tag, align_bytes=64)
-            nc.vector.tensor_copy(v2w[g][:], tab2w[:].bitcast(U32).indirect(idx2[:, g * cols : (g + 1) * cols]))
+            nc.vector.tensor_copy(v2w[g][:], tab2w[:].bitcast(U32).indirect(idx2[:, g * list_cols : (g + 1) * list_cols]))
 
-        def round_w_scalar(a):
+        def round_w(a):
             nc.scalar.activation(
-                w_bf[a][:].rearrange("p (c i t) -> p c t i", i=4, t=PACK),
-                w_raw[a][:].rearrange("p t (c i) -> p c t i", i=4),
+                w_bf[a][:].rearrange("p (c i t) -> p c t i", i=LINE, t=PACK),
+                w_raw[a][:].rearrange("p t (c i) -> p c t i", i=LINE),
                 ACT.Copy,
             )
 
@@ -166,8 +173,8 @@ def tile_list_gp_inducing_mean_kernel(
             width = CHUNKS[c]
             share = BANK // width
             if t % share == 0:
-                banks[u, t // share] = psum_a.tile([P, BANK], F32, name="bank_a")
-            slabs[u, t] = banks[u, t // share][:, (t % share) * width : (t % share + 1) * width]
+                banks[u] = psum_a.tile([P, BANK], F32, name="bank_a")
+            slabs[u, t] = banks[u][:, (t % share) * width : (t % share + 1) * width]
             for js in pieces(width, (512, 256, 128)):
                 nc.tensor.matmul_mx(
                     out=slabs[u, t][:, js],
@@ -182,32 +189,27 @@ def tile_list_gp_inducing_mean_kernel(
         def exponent(u, t):
             c, a = units[u]
             if t == 0:
-                z[u] = ring.tile([P, PACK, CHUNKS[c]], F32, name="z", bufs=2)
-            if starts[c] >= S2 - SHIFTED:
-                width = CHUNKS[c]
-                share = BANK // width
-                lo = starts[c] - (S2 - SHIFTED)
-                if t % share == share - 1:
-                    ts = slice(t + 1 - share, t + 1)
-                    bank = banks[u, t // share][:, 0 : share * width].rearrange("p (t j) -> p t j", t=share)
-                    nc.vector.tensor_tensor(z[u][:, ts, :], bank, shift[:, a, ts, lo : lo + width], ALU.add)
-                return
-            if (u, t) in HELPED:
-                biased = keep.tile([P, CHUNKS[c]], F32, name=f"biased{u}_{t}")
-                nc.scalar.activation(biased[:], slabs[u, t], ACT.Identity, bias=bias[:, a, t : t + 1])
-                nc.gpsimd.tensor_tensor(z[u][:, t, :], biased[:], hz_t[:, starts[c] : starts[c] + CHUNKS[c]], ALU.subtract)
-                return
-            nc.vector.scalar_tensor_tensor(
-                z[u][:, t, :], slabs[u, t], bias[:, a, t : t + 1], hz_t[:, starts[c] : starts[c] + CHUNKS[c]], ALU.add, ALU.subtract
-            )
+                z[u] = ring.tile([P, CHUNKS[c] // LINE, PACK, LINE], F32, name="z")
+            if c < LAST:
+                nc.vector.scalar_tensor_tensor(
+                    z[u][:, :, t, :],
+                    slabs[u, t].rearrange("p (c i) -> p c i", i=LINE),
+                    bias[:, a, t : t + 1],
+                    hz_t[:, starts[c] : starts[c] + CHUNKS[c]].rearrange("p (c i) -> p c i", i=LINE),
+                    ALU.add,
+                    ALU.subtract,
+                )
+            elif t == PACK - 1:
+                nc.vector.tensor_tensor(
+                    z[u][:].rearrange("p c t i -> p t c i"),
+                    banks[u][:].rearrange("p (t c i) -> p t c i", t=PACK, i=LINE),
+                    shift[:, a].rearrange("p t (c i) -> p t c i", i=LINE),
+                    ALU.add,
+                )
 
         def kernel_values(u):
             h_bf[u] = keep.tile([P, CHUNKS[units[u][0]] * PACK], BF16, name=f"h_bf{u}", align_bytes=64)
-            nc.scalar.activation(
-                h_bf[u][:].rearrange("p (c i t) -> p c t i", i=4, t=PACK),
-                z[u][:].rearrange("p t (c i) -> p c t i", i=4),
-                ACT.Exp,
-            )
+            nc.scalar.activation(h_bf[u][:].rearrange("p (c i t) -> p c t i", i=LINE, t=PACK), z[u][:], ACT.Exp)
 
         def quantize_h(u):
             width = CHUNKS[units[u][0]]
@@ -218,10 +220,13 @@ def tile_list_gp_inducing_mean_kernel(
                     out=hq[u][:, js].bitcast(FP8X4), scales=hqs[u][:, js], in_=h_bf[u][:, PACK * js.start : PACK * js.stop]
                 )
 
+        def tiles_per_bank(c):
+            return 2 if c == LAST else 1
+
         def product_y(u, nt):
             c, a = units[u]
             width = CHUNKS[c]
-            share = min(BANK // width, 2)
+            share = tiles_per_bank(c)
             place = nt % share
             if a == 0 and place == 0:
                 acc[c, nt // share] = psum_y.tile([P, BANK], F32, name="bank_y")
@@ -247,63 +252,61 @@ def tile_list_gp_inducing_mean_kernel(
                     stop=(a == PASSES - 1 and place == share - 1 and js.stop == width),
                 )
 
-        def finish(u, nt):
-            c, a = units[u]
+        def finish(c):
             width = CHUNKS[c]
-            share = min(BANK // width, 2)
-            if a < PASSES - 1 or nt % share < share - 1:
-                return
-            first = nt + 1 - share
-            bank = acc[c, nt // share][:, 0 : share * width].rearrange("p (s j) -> p s j", s=share)
-            res = keep.tile([P, share, width], F32, name=f"res{c}_{first}")
-            if c == 1 and nt >= 2 or c == 2 and nt % 2 == 1 or (c, nt) == (3, 3):
-                nc.vector.tensor_tensor(
-                    res[:], bank, b_t[:, first : nt + 1].unsqueeze(2).to_broadcast([P, share, width]), ALU.add
+            share = tiles_per_bank(c)
+            for k in range(N_TILES // share):
+                first = k * share
+                bank = acc[c, k][:, 0 : share * width].rearrange("p (s j) -> p s j", s=share)
+                res = keep.tile([P, share, width], F32, name=f"res{c}_{first}")
+                if c > 0 and k % 2 == 1:
+                    nc.vector.tensor_tensor(
+                        res[:], bank, b_t[:, first : first + share].unsqueeze(2).to_broadcast([P, share, width]), ALU.add
+                    )
+                else:
+                    for s in range(share):
+                        nc.scalar.activation(res[:, s, :], bank[:, s, :], ACT.Identity, bias=b_t[:, first + s : first + s + 1])
+                nc.sync.dma_start(
+                    out[first * P : (first + share) * P, starts[c] : starts[c] + width].rearrange("(s p) j -> p s j", p=P),
+                    res[:],
                 )
-            else:
-                for k in range(share):
-                    nc.scalar.activation(res[:, k, :], bank[:, k, :], ACT.Identity, bias=b_t[:, first + k : first + k + 1])
-            nc.sync.dma_start(
-                out[first * P : (nt + 1) * P, starts[c] : starts[c] + width].rearrange("(s p) j -> p s j", p=P), res[:]
-            )
 
         nc.vector.tensor_copy(vs_list[:], tabs[:].indirect(idx[:]))
         nc.vector.tensor_copy(
-            vs[:].rearrange("p a (t m) -> p a m t", t=PACK), vs_list[:].rearrange("p (a m t) -> p a m t", a=PASSES, t=PACK)
+            vs[:].rearrange("p a (t m) -> p a t m", t=PACK), vs_list[:].rearrange("p (a m t) -> p a t m", a=PASSES, t=PACK)
         )
         nc.vector.tensor_copy(vw[:].rearrange("p a (t m) -> p a m t", t=PACK), tabw[:].bitcast(U32).indirect(idx[:]))
         gather_v2_scales(0, 2, "v2s0")
         gather_v2_words(0, "v2w0")
         gather_v2_words(1, "v2w1")
+        round_w(0)
         for t in range(PACK):
             product_a(0, t)
+
         for u in range(len(units) + 2):
             if u == 1:
                 quantize_w(0)
-            narrow = u + 1 < len(units) and CHUNKS[units[u + 1][0]] <= 128
-            if narrow:
+            one_bank_next = u + 1 < len(units) and units[u + 1][0] == LAST
+            if one_bank_next:
                 for t in range(PACK):
                     product_a(u + 1, t)
             for t in range(PACK):
                 if u < len(units):
                     exponent(u, t)
-                if u + 1 < len(units) and not narrow:
+                if u + 1 < len(units) and not one_bank_next:
                     product_a(u + 1, t)
                 if u >= 2:
                     product_y(u - 2, t)
-            if u == 0:
-                round_w_scalar(0)
             if u < len(units):
                 kernel_values(u)
             if u == 0:
-                round_w_scalar(1)
+                round_w(1)
             if 1 <= u <= len(units):
                 quantize_h(u - 1)
-            if u >= 2:
-                for nt in range(N_TILES):
-                    finish(u - 2, nt)
+            if u >= 2 and units[u - 2][1] == PASSES - 1:
+                finish(units[u - 2][0])
             if u == 1:
                 quantize_w(1)
             if u == 2:
-                gather_v2_scales(2, 1, "h_bf0")
+                gather_v2_scales(2, 1, "w_bf1")
                 gather_v2_words(2, "h_bf1")

@@ -29,7 +29,7 @@ SCALE_ROWS = 4
 GATHER = 512
 CHUNKS = [512, 512, 384, 128]
 LAST = len(CHUNKS) - 1
-V2_ROW = 4
+SPREAD = 8
 LN_LOW, LN_HIGH = 2.0**-64, 2.0**64
 
 
@@ -49,6 +49,7 @@ def tile_list_gp_inducing_mean_kernel(
     with ExitStack() as ctx:
         keep = ctx.enter_context(tc.tile_pool(name="keep", bufs=1))
         ring = ctx.enter_context(tc.tile_pool(name="ring", bufs=2))
+        late = ctx.enter_context(tc.tile_pool(name="late", bufs=1))
         psum_a = ctx.enter_context(tc.psum_pool(name="psum_a", bufs=4))
         psum_y = ctx.enter_context(tc.psum_pool(name="psum_y", bufs=4))
 
@@ -57,37 +58,44 @@ def tile_list_gp_inducing_mean_kernel(
         tabw = keep.tile([P, T], I32, name="tabw", align_bytes=64)
         tabs = keep.tile([P, T], U8, name="tabs", align_bytes=64)
         tab2w = keep.tile([P, T2], I32, name="tab2w", align_bytes=64)
-        tab2s = keep.tile([P, T2], U8, name="tab2s", align_bytes=64)
-        w4w = keep.tile([P, PASSES, 2 * N], U8, name="w4w", align_bytes=64)
-        w4s = keep.tile([P, PASSES, N], U8, name="w4s", align_bytes=64)
+        raw_bytes = PACK * N * 4
+        tab2s = late.tile([P, T2], U8, name="tab2s", align_bytes=64, offset=raw_bytes - N)
+        w4s = late.tile([P, PASSES, N], U8, name="w4s", align_bytes=64, offset=raw_bytes)
+        w4w = late.tile([P, PASSES, 2 * N], U8, name="w4w", align_bytes=64, offset=raw_bytes + PASSES * N)
+        w_raw = [
+            late.tile([P, PACK, N], F32, name=f"w_raw{a}", align_bytes=64, offset=a * (raw_bytes + 3 * PASSES * N))
+            for a in range(PASSES)
+        ]
+        picked = keep.tile([P, S + S2], U8, name="picked", align_bytes=64)
+        planes = keep.tile([P, S + S2], U8, name="planes", align_bytes=64)
         hx_t = keep.tile([P, PASSES, PACK], F32, name="hx_t", align_bytes=64)
         pw_t = keep.tile([P, PASSES, PACK], F32, name="pw_t")
         b_t = keep.tile([P, N_TILES], F32, name="b_t")
         hz_col = keep.tile([P, S2 // P], F32, name="hz_col")
         hz_t = keep.tile([P, S2], F32, name="hz_t")
-        w_raw = [keep.tile([P, PACK, N], F32, name=f"w_raw{a}", align_bytes=64) for a in range(PASSES)]
         ident = keep.tile([P, P], F32, name="ident")
 
-        nc.vector.memset(tabs[:].bitcast(I32), 0)
+        nc.gpsimd.memset(tabs[:].bitcast(I32), 0)
         nc.vector.memset(tab2s[:].bitcast(I32), 0)
         make_identity(nc, ident[:])
-        nc.gpsimd.memset(w4s[:].bitcast(I32), 0)
-
-        def load_scales(tile, first_row, source):
-            for r in range(SCALE_ROWS):
-                nc.sync.dma_start(
-                    tile[first_row + r : P : 32, :].bitcast(I32), source[0, r : 4 * SCALE_ROWS : SCALE_ROWS, :].bitcast(I32)
-                )
+        nc.gpsimd.memset(planes[:].bitcast(I32), 0)
 
         nc.sync.dma_start(idx[:], offs)
         nc.sync.dma_start(pw_t[:], pw.rearrange("(a p t) -> p a t", a=PASSES, t=PACK))
-        load_scales(tabs, 0, tab_scales)
+        nc.sync.dma_start(tabs[0:P:SPREAD, :].bitcast(I32), tab_scales[0].bitcast(I32))
         nc.sync.dma_start(hx_t[:], hx.rearrange("(a p t) -> p a t", a=PASSES, t=PACK))
-        nc.sync.dma_start(tabw[:], tab_words[0].rearrange("p t i -> p (t i)").bitcast(I32))
-        nc.sync.dma_start(idx2[:], offs2)
         nc.sync.dma_start(hz_col[:], hz.rearrange("(p c) -> p c", p=P))
-        load_scales(tab2s, V2_ROW, tab2_scales)
+        nc.sync.dma_start(idx2[:], offs2)
+        nc.sync.dma_start(tab2s[0:P:SPREAD, :].bitcast(I32), tab2_scales[0].bitcast(I32))
+        nc.sync.dma_start(tabw[:], tab_words[0].rearrange("p t i -> p (t i)").bitcast(I32))
         nc.sync.dma_start(tab2w[:], tab2_words[0].rearrange("p t i -> p (t i)").bitcast(I32))
+
+        nc.vector.tensor_copy(picked[:, 0:S].rearrange("p (a t m) -> p a m t", a=PASSES, t=PACK), tabs[:].indirect(idx[:]))
+        nc.vector.tensor_copy(picked[:, S : S + S2], tab2s[:].indirect(idx2[:]))
+        for r in range(SCALE_ROWS):
+            nc.sync.dma_start(planes[r:P:32, :].bitcast(I32), picked[SPREAD * r : P : 32, :].bitcast(I32))
+
+        nc.gpsimd.memset(w4s[:].bitcast(I32), 0)
         for a in range(PASSES):
             nc.sync.dma_start(w_raw[a][:], w[a * PASS : (a + 1) * PASS, :].rearrange("(p t) n -> p t n", t=PACK))
         nc.sync.dma_start(w4w[:].bitcast(I32), w4_words.rearrange("a p c -> p a c").bitcast(I32))
@@ -135,19 +143,11 @@ def tile_list_gp_inducing_mean_kernel(
                 )
 
         vw = keep.tile([P, PASSES, PASS], U32, name="vw", align_bytes=64)
-        vs_list = keep.tile([P, S], U8, name="vs_list", align_bytes=64)
-        vs = keep.tile([P, PASSES, PASS], U8, name="vs", align_bytes=64)
         wq = [keep.tile([P, N], U32, name=f"wq{a}", align_bytes=64) for a in range(PASSES)]
         wqs = [keep.tile([P, N], U8, name=f"wqs{a}", align_bytes=64) for a in range(PASSES)]
         w_bf = [keep.tile([P, N * PACK], BF16, name=f"w_bf{a}", align_bytes=64) for a in range(PASSES)]
         list_cols = GATHER // LIST_ROWS
-        v2w, v2s = {}, {}
-
-        def gather_v2_scales(first, count, tag):
-            gathered = keep.tile([P, count * GATHER], U8, name=tag, align_bytes=64)
-            nc.vector.tensor_copy(gathered[:], tab2s[:].indirect(idx2[:, first * list_cols : (first + count) * list_cols]))
-            for g in range(count):
-                v2s[first + g] = gathered[V2_ROW:P, g * GATHER : (g + 1) * GATHER]
+        v2w = {}
 
         def gather_v2_words(g, tag):
             v2w[g] = keep.tile([P, GATHER], U32, name=tag, align_bytes=64)
@@ -179,9 +179,9 @@ def tile_list_gp_inducing_mean_kernel(
                 nc.tensor.matmul_mx(
                     out=slabs[u, t][:, js],
                     lhsT=vw[:, a, t * P : (t + 1) * P].bitcast(FP8X4),
-                    lhsT_scale=vs[:, a, t * P : (t + 1) * P],
+                    lhsT_scale=planes[:, a * PASS + t * P : a * PASS + (t + 1) * P],
                     rhs=v2w[g][:, lo + js.start : lo + js.stop].bitcast(FP8X4),
-                    rhs_scale=v2s[g][:, lo + js.start : lo + js.stop],
+                    rhs_scale=planes[:, S + starts[c] + js.start : S + starts[c] + js.stop],
                     start=True,
                     stop=True,
                 )
@@ -231,7 +231,7 @@ def tile_list_gp_inducing_mean_kernel(
             if a == 0 and place == 0:
                 acc[c, nt // share] = psum_y.tile([P, BANK], F32, name="bank_y")
             target = acc[c, nt // share][:, place * width : (place + 1) * width]
-            for js in pieces(width, (512, 128)):
+            for js in pieces(width, (512, 256, 128)):
                 nc.tensor.matmul_mx(
                     out=target[:, js],
                     lhsT=w4w[:, a, 2 * nt * P : 2 * (nt + 1) * P].bitcast(FP4X4),
@@ -271,12 +271,7 @@ def tile_list_gp_inducing_mean_kernel(
                     res[:],
                 )
 
-        nc.vector.tensor_copy(vs_list[:], tabs[:].indirect(idx[:]))
-        nc.vector.tensor_copy(
-            vs[:].rearrange("p a (t m) -> p a t m", t=PACK), vs_list[:].rearrange("p (a m t) -> p a t m", a=PASSES, t=PACK)
-        )
         nc.vector.tensor_copy(vw[:].rearrange("p a (t m) -> p a m t", t=PACK), tabw[:].bitcast(U32).indirect(idx[:]))
-        gather_v2_scales(0, 2, "v2s0")
         gather_v2_words(0, "v2w0")
         gather_v2_words(1, "v2w1")
         round_w(0)
@@ -308,5 +303,4 @@ def tile_list_gp_inducing_mean_kernel(
             if u == 1:
                 quantize_w(1)
             if u == 2:
-                gather_v2_scales(2, 1, "w_bf1")
                 gather_v2_words(2, "h_bf1")

@@ -29,6 +29,7 @@ SCALE_ROWS = 4
 GATHER = 512
 CHUNKS = [512, 512, 384, 128]
 LAST = len(CHUNKS) - 1
+HALF = N // 2
 SPREAD = 8
 LN_LOW, LN_HIGH = 2.0**-64, 2.0**64
 
@@ -58,19 +59,19 @@ def tile_list_gp_inducing_mean_kernel(
         tabw = keep.tile([P, T], I32, name="tabw", align_bytes=64)
         tabs = keep.tile([P, T], U8, name="tabs", align_bytes=64)
         tab2w = keep.tile([P, T2], I32, name="tab2w", align_bytes=64)
-        raw_bytes = PACK * N * 4
-        tab2s = late.tile([P, T2], U8, name="tab2s", align_bytes=64, offset=raw_bytes - N)
-        w4s = late.tile([P, PASSES, N], U8, name="w4s", align_bytes=64, offset=raw_bytes)
-        w4w = late.tile([P, PASSES, 2 * N], U8, name="w4w", align_bytes=64, offset=raw_bytes + PASSES * N)
-        w_raw = [
-            late.tile([P, PACK, N], F32, name=f"w_raw{a}", align_bytes=64, offset=a * (raw_bytes + 3 * PASSES * N))
-            for a in range(PASSES)
-        ]
+        half_bytes = PACK * HALF * 4
+        tab2s = late.tile([P, T2], U8, name="tab2s", align_bytes=64, offset=half_bytes - N)
+        w4s = late.tile([P, PASSES, N], U8, name="w4s", align_bytes=64, offset=half_bytes)
+        w4w = late.tile([P, PASSES, 2 * N], U8, name="w4w", align_bytes=64, offset=half_bytes + PASSES * N)
+        b_t = late.tile([P, N_TILES], F32, name="b_t", align_bytes=64, offset=half_bytes + 3 * PASSES * N)
+        w_first = keep.tile([P, PACK, HALF], F32, name="w_first", align_bytes=64)
+        w_second = late.tile([P, PACK, HALF], F32, name="w_second", align_bytes=64, offset=0)
+        w_last = late.tile([P, PACK, N], F32, name="w_last", align_bytes=64, offset=half_bytes + 3 * PASSES * N + 64)
+        w_parts = [(0, 0, w_first), (0, HALF, w_second), (1, 0, w_last)]
         picked = keep.tile([P, S + S2], U8, name="picked", align_bytes=64)
         planes = keep.tile([P, S + S2], U8, name="planes", align_bytes=64)
         hx_t = keep.tile([P, PASSES, PACK], F32, name="hx_t", align_bytes=64)
         pw_t = keep.tile([P, PASSES, PACK], F32, name="pw_t")
-        b_t = keep.tile([P, N_TILES], F32, name="b_t")
         hz_col = keep.tile([P, S2 // P], F32, name="hz_col")
         hz_t = keep.tile([P, S2], F32, name="hz_t")
         ident = keep.tile([P, P], F32, name="ident")
@@ -80,24 +81,34 @@ def tile_list_gp_inducing_mean_kernel(
         make_identity(nc, ident[:])
         nc.gpsimd.memset(planes[:].bitcast(I32), 0)
 
+        def load_w(part):
+            a, lo, tile = w_parts[part]
+            rows = w[a * PASS : (a + 1) * PASS, lo : lo + tile.shape[2]]
+            nc.sync.dma_start(tile[:], rows.rearrange("(p t) n -> p t n", t=PACK))
+
         nc.sync.dma_start(idx[:], offs)
-        nc.sync.dma_start(pw_t[:], pw.rearrange("(a p t) -> p a t", a=PASSES, t=PACK))
-        nc.sync.dma_start(tabs[0:P:SPREAD, :].bitcast(I32), tab_scales[0].bitcast(I32))
-        nc.sync.dma_start(hx_t[:], hx.rearrange("(a p t) -> p a t", a=PASSES, t=PACK))
-        nc.sync.dma_start(hz_col[:], hz.rearrange("(p c) -> p c", p=P))
         nc.sync.dma_start(idx2[:], offs2)
+        nc.sync.dma_start(tabs[0:P:SPREAD, :].bitcast(I32), tab_scales[0].bitcast(I32))
+        nc.sync.dma_start(hz_col[:], hz.rearrange("(p c) -> p c", p=P))
+        nc.sync.dma_start(pw_t[:], pw.rearrange("(a p t) -> p a t", a=PASSES, t=PACK))
         nc.sync.dma_start(tab2s[0:P:SPREAD, :].bitcast(I32), tab2_scales[0].bitcast(I32))
+        nc.sync.dma_start(hx_t[:], hx.rearrange("(a p t) -> p a t", a=PASSES, t=PACK))
         nc.sync.dma_start(tabw[:], tab_words[0].rearrange("p t i -> p (t i)").bitcast(I32))
         nc.sync.dma_start(tab2w[:], tab2_words[0].rearrange("p t i -> p (t i)").bitcast(I32))
+        load_w(0)
 
         nc.vector.tensor_copy(picked[:, 0:S].rearrange("p (a t m) -> p a m t", a=PASSES, t=PACK), tabs[:].indirect(idx[:]))
+        factors = keep.tile([P, 3, PASSES, PACK], F32, name="factors")
+        nc.vector.tensor_scalar(factors[:, 0], pw_t[:], LN_LOW, LN_HIGH, ALU.max, ALU.min)
+        nc.vector.tensor_scalar(factors[:, 1], pw_t[:], LN_HIGH, LN_LOW, ALU.max, ALU.mult)
+        nc.vector.tensor_scalar(factors[:, 2], pw_t[:], LN_LOW, LN_HIGH, ALU.min, ALU.mult)
         nc.vector.tensor_copy(picked[:, S : S + S2], tab2s[:].indirect(idx2[:]))
         for r in range(SCALE_ROWS):
             nc.sync.dma_start(planes[r:P:32, :].bitcast(I32), picked[SPREAD * r : P : 32, :].bitcast(I32))
 
         nc.gpsimd.memset(w4s[:].bitcast(I32), 0)
-        for a in range(PASSES):
-            nc.sync.dma_start(w_raw[a][:], w[a * PASS : (a + 1) * PASS, :].rearrange("(p t) n -> p t n", t=PACK))
+        load_w(1)
+        load_w(2)
         nc.sync.dma_start(w4w[:].bitcast(I32), w4_words.rearrange("a p c -> p a c").bitcast(I32))
         for r in range(SCALE_ROWS):
             nc.sync.dma_start(
@@ -117,13 +128,9 @@ def tile_list_gp_inducing_mean_kernel(
                 spread[:].rearrange("p (c m) -> p m c", c=LINE),
             )
 
-        factors = keep.tile([P, 3, PASSES, PACK], F32, name="factors")
         ln_factors = keep.tile([P, PASSES, PACK, 3], F32, name="ln_factors")
         ln_pw = keep.tile([P, PASSES, PACK], F32, name="ln_pw")
         bias = keep.tile([P, PASSES, PACK], F32, name="bias")
-        nc.vector.tensor_scalar(factors[:, 0], pw_t[:], LN_LOW, LN_HIGH, ALU.max, ALU.min)
-        nc.vector.tensor_scalar(factors[:, 1], pw_t[:], LN_HIGH, LN_LOW, ALU.max, ALU.mult)
-        nc.vector.tensor_scalar(factors[:, 2], pw_t[:], LN_LOW, LN_HIGH, ALU.min, ALU.mult)
         for a in range(PASSES):
             for t in range(PACK):
                 nc.scalar.activation(ln_factors[:, a, t, :], factors[:, :, a, t], ACT.Ln, accum_out=ln_pw[:, a, t : t + 1])
@@ -153,10 +160,11 @@ def tile_list_gp_inducing_mean_kernel(
             v2w[g] = keep.tile([P, GATHER], U32, name=tag, align_bytes=64)
             nc.vector.tensor_copy(v2w[g][:], tab2w[:].bitcast(U32).indirect(idx2[:, g * list_cols : (g + 1) * list_cols]))
 
-        def round_w(a):
+        def round_w(part):
+            a, lo, tile = w_parts[part]
             nc.scalar.activation(
-                w_bf[a][:].rearrange("p (c i t) -> p c t i", i=LINE, t=PACK),
-                w_raw[a][:].rearrange("p t (c i) -> p c t i", i=LINE),
+                w_bf[a][:, PACK * lo : PACK * (lo + tile.shape[2])].rearrange("p (c i t) -> p c t i", i=LINE, t=PACK),
+                tile[:].rearrange("p t (c i) -> p c t i", i=LINE),
                 ACT.Copy,
             )
 
@@ -215,10 +223,7 @@ def tile_list_gp_inducing_mean_kernel(
             width = CHUNKS[units[u][0]]
             hq[u] = keep.tile([P, width], U32, name=f"hq{u}", align_bytes=64)
             hqs[u] = keep.tile([P, width], U8, name=f"hqs{u}", align_bytes=64)
-            for js in pieces(width, (512, 256, 128)):
-                nc.vector.quantize_mx(
-                    out=hq[u][:, js].bitcast(FP8X4), scales=hqs[u][:, js], in_=h_bf[u][:, PACK * js.start : PACK * js.stop]
-                )
+            nc.vector.quantize_mx(out=hq[u][:].bitcast(FP8X4), scales=hqs[u][:], in_=h_bf[u][:])
 
         def tiles_per_bank(c):
             return 2 if c == LAST else 1
@@ -275,6 +280,7 @@ def tile_list_gp_inducing_mean_kernel(
         gather_v2_words(0, "v2w0")
         gather_v2_words(1, "v2w1")
         round_w(0)
+        round_w(1)
         for t in range(PACK):
             product_a(0, t)
 
@@ -295,7 +301,7 @@ def tile_list_gp_inducing_mean_kernel(
             if u < len(units):
                 kernel_values(u)
             if u == 0:
-                round_w(1)
+                round_w(2)
             if 1 <= u <= len(units):
                 quantize_h(u - 1)
             if u >= 2 and units[u - 2][1] == PASSES - 1:

@@ -26,10 +26,29 @@ BANK = 512
 LINE = 4
 LIST_ROWS = 16
 SCALE_ROWS = 4
-GATHER = 512
-CHUNKS = [512, 512, 384, 128]
-LAST = len(CHUNKS) - 1
-HALF = N // 2
+CHUNKS = [384, 512, 512, 128]
+CUTS = [384, 1152]
+CUT_OVER = ["v2w0", "v2w1"]
+CUT_AT = [-1, -1]
+SHIFTED = [3]
+SHARE = [1, 1, 1, 2]
+ON_VECTOR = [(1, 1), (1, 3), (2, 1), (2, 3), (3, 1)]
+W_CUTS = [(0, 0, 512), (1, 0, 256), (1, 256, 256)]
+ROUND_AT = [-1, -1, 0]
+QW_AT = [0.5, 2]
+QW_OVER = ["wq0", "wq1"]
+H_OVER = {}
+VW1_AT = -1
+VW1_OVER = "vw1"
+W4_BEFORE = 3
+Z_BUFS = 3
+A_BANKS = 4
+Y_LAG = 2
+F_LAG = 0
+F_FIRST = True
+SPLIT = []
+Y_IN_A = [(2, 2), (2, 3)]
+FP4_FIRST = []
 SPREAD = 8
 LN_LOW, LN_HIGH = 2.0**-64, 2.0**64
 
@@ -49,25 +68,28 @@ def tile_list_gp_inducing_mean_kernel(
     nc = tc.nc
     with ExitStack() as ctx:
         keep = ctx.enter_context(tc.tile_pool(name="keep", bufs=1))
-        ring = ctx.enter_context(tc.tile_pool(name="ring", bufs=2))
+        ring = ctx.enter_context(tc.tile_pool(name="ring", bufs=Z_BUFS))
         late = ctx.enter_context(tc.tile_pool(name="late", bufs=1))
-        psum_a = ctx.enter_context(tc.psum_pool(name="psum_a", bufs=4))
-        psum_y = ctx.enter_context(tc.psum_pool(name="psum_y", bufs=4))
+        psum_a = ctx.enter_context(tc.psum_pool(name="psum_a", bufs=A_BANKS))
+        psum_y = ctx.enter_context(tc.psum_pool(name="psum_y", bufs=8 - A_BANKS))
 
         idx = keep.tile([P, S // LIST_ROWS], U16, name="idx")
         idx2 = keep.tile([P, S2 // LIST_ROWS], U16, name="idx2")
         tabw = keep.tile([P, T], I32, name="tabw", align_bytes=64)
         tabs = keep.tile([P, T], U8, name="tabs", align_bytes=64)
         tab2w = keep.tile([P, T2], I32, name="tab2w", align_bytes=64)
-        half_bytes = PACK * HALF * 4
-        tab2s = late.tile([P, T2], U8, name="tab2s", align_bytes=64, offset=half_bytes - N)
-        w4s = late.tile([P, PASSES, N], U8, name="w4s", align_bytes=64, offset=half_bytes)
-        w4w = late.tile([P, PASSES, 2 * N], U8, name="w4w", align_bytes=64, offset=half_bytes + PASSES * N)
-        b_t = late.tile([P, N_TILES], F32, name="b_t", align_bytes=64, offset=half_bytes + 3 * PASSES * N)
-        w_first = keep.tile([P, PACK, HALF], F32, name="w_first", align_bytes=64)
-        w_second = late.tile([P, PACK, HALF], F32, name="w_second", align_bytes=64, offset=0)
-        w_last = late.tile([P, PACK, N], F32, name="w_last", align_bytes=64, offset=half_bytes + 3 * PASSES * N + 64)
-        w_parts = [(0, 0, w_first), (0, HALF, w_second), (1, 0, w_last)]
+        tab2s = late.tile([P, T2], U8, name="tab2s", align_bytes=64, offset=0)
+        w4s = late.tile([P, PASSES, N], U8, name="w4s", align_bytes=64, offset=0)
+        w4w = late.tile([P, PASSES, 2 * N], U8, name="w4w", align_bytes=64, offset=PASSES * N)
+        b_t = late.tile([P, N_TILES], F32, name="b_t", align_bytes=64, offset=3 * PASSES * N)
+        w_first = keep.tile([P, PACK * W_CUTS[0][2]], F32, name="w_first", align_bytes=64)
+        w_rest = late.tile(
+            [P, PACK * (PASSES * N - W_CUTS[0][2])], F32, name="w_rest", align_bytes=64, offset=3 * PASSES * N + 64
+        )
+        w_parts = [w_first[:].rearrange("p (t n) -> p t n", t=PACK)]
+        for a, lo, width in W_CUTS[1:]:
+            place = PACK * (a * N + lo - W_CUTS[0][2])
+            w_parts.append(w_rest[:, place : place + PACK * width].rearrange("p (t n) -> p t n", t=PACK))
         picked = keep.tile([P, S + S2], U8, name="picked", align_bytes=64)
         planes = keep.tile([P, S + S2], U8, name="planes", align_bytes=64)
         hx_t = keep.tile([P, PASSES, PACK], F32, name="hx_t", align_bytes=64)
@@ -82,39 +104,42 @@ def tile_list_gp_inducing_mean_kernel(
         nc.gpsimd.memset(planes[:].bitcast(I32), 0)
 
         def load_w(part):
-            a, lo, tile = w_parts[part]
-            rows = w[a * PASS : (a + 1) * PASS, lo : lo + tile.shape[2]]
-            nc.sync.dma_start(tile[:], rows.rearrange("(p t) n -> p t n", t=PACK))
+            a, lo, width = W_CUTS[part]
+            rows = w[a * PASS : (a + 1) * PASS, lo : lo + width]
+            nc.sync.dma_start(w_parts[part], rows.rearrange("(p t) n -> p t n", t=PACK))
 
+        nc.sync.dma_start(pw_t[:], pw.rearrange("(a p t) -> p a t", a=PASSES, t=PACK))
         nc.sync.dma_start(idx[:], offs)
-        nc.sync.dma_start(idx2[:], offs2)
         nc.sync.dma_start(tabs[0:P:SPREAD, :].bitcast(I32), tab_scales[0].bitcast(I32))
         nc.sync.dma_start(hz_col[:], hz.rearrange("(p c) -> p c", p=P))
-        nc.sync.dma_start(pw_t[:], pw.rearrange("(a p t) -> p a t", a=PASSES, t=PACK))
-        nc.sync.dma_start(tab2s[0:P:SPREAD, :].bitcast(I32), tab2_scales[0].bitcast(I32))
         nc.sync.dma_start(hx_t[:], hx.rearrange("(a p t) -> p a t", a=PASSES, t=PACK))
+        nc.sync.dma_start(idx2[:], offs2)
+        nc.sync.dma_start(tab2s[0:P:SPREAD, :].bitcast(I32), tab2_scales[0].bitcast(I32))
         nc.sync.dma_start(tabw[:], tab_words[0].rearrange("p t i -> p (t i)").bitcast(I32))
         nc.sync.dma_start(tab2w[:], tab2_words[0].rearrange("p t i -> p (t i)").bitcast(I32))
         load_w(0)
 
         nc.vector.tensor_copy(picked[:, 0:S].rearrange("p (a t m) -> p a m t", a=PASSES, t=PACK), tabs[:].indirect(idx[:]))
+        terms = keep.tile([P, 4, PASSES * PACK], F32, name="terms")
         factors = keep.tile([P, 3, PASSES, PACK], F32, name="factors")
-        nc.vector.tensor_scalar(factors[:, 0], pw_t[:], LN_LOW, LN_HIGH, ALU.max, ALU.min)
-        nc.vector.tensor_scalar(factors[:, 1], pw_t[:], LN_HIGH, LN_LOW, ALU.max, ALU.mult)
-        nc.vector.tensor_scalar(factors[:, 2], pw_t[:], LN_LOW, LN_HIGH, ALU.min, ALU.mult)
+        nc.gpsimd.tensor_scalar(factors[:, 0], pw_t[:], LN_LOW, LN_HIGH, ALU.max, ALU.min)
+        nc.gpsimd.tensor_scalar(factors[:, 1], pw_t[:], LN_HIGH, LN_LOW, ALU.max, ALU.mult)
+        nc.gpsimd.tensor_scalar(factors[:, 2], pw_t[:], LN_LOW, LN_HIGH, ALU.min, ALU.mult)
         nc.vector.tensor_copy(picked[:, S : S + S2], tab2s[:].indirect(idx2[:]))
         for r in range(SCALE_ROWS):
             nc.sync.dma_start(planes[r:P:32, :].bitcast(I32), picked[SPREAD * r : P : 32, :].bitcast(I32))
 
         nc.gpsimd.memset(w4s[:].bitcast(I32), 0)
-        load_w(1)
-        load_w(2)
-        nc.sync.dma_start(w4w[:].bitcast(I32), w4_words.rearrange("a p c -> p a c").bitcast(I32))
-        for r in range(SCALE_ROWS):
-            nc.sync.dma_start(
-                w4s[r:P:32, :, :].bitcast(I32),
-                w4_scales[:, r : 4 * SCALE_ROWS : SCALE_ROWS, :].rearrange("a q c -> q a c").bitcast(I32),
-            )
+        for part in range(1, len(W_CUTS) + 1):
+            if part == W4_BEFORE:
+                nc.sync.dma_start(w4w[:].bitcast(I32), w4_words.rearrange("a p c -> p a c").bitcast(I32))
+                for r in range(SCALE_ROWS):
+                    nc.sync.dma_start(
+                        w4s[r:P:32, :, :].bitcast(I32),
+                        w4_scales[:, r : 4 * SCALE_ROWS : SCALE_ROWS, :].rearrange("a q c -> q a c").bitcast(I32),
+                    )
+            if part < len(W_CUTS):
+                load_w(part)
         with nc.allow_non_contiguous_dma(reason="one bias value a partition"):
             nc.sync.dma_start(b_t[:], b.rearrange("(c p) -> p c", p=P))
 
@@ -128,65 +153,76 @@ def tile_list_gp_inducing_mean_kernel(
                 spread[:].rearrange("p (c m) -> p m c", c=LINE),
             )
 
-        ln_factors = keep.tile([P, PASSES, PACK, 3], F32, name="ln_factors")
-        ln_pw = keep.tile([P, PASSES, PACK], F32, name="ln_pw")
         bias = keep.tile([P, PASSES, PACK], F32, name="bias")
-        for a in range(PASSES):
-            for t in range(PACK):
-                nc.scalar.activation(ln_factors[:, a, t, :], factors[:, :, a, t], ACT.Ln, accum_out=ln_pw[:, a, t : t + 1])
+        summed = keep.tile([P, PASSES * PACK, 4], F32, name="summed")
+        nc.scalar.activation(terms[:, 0:3, :], factors[:].rearrange("p f a t -> p f (a t)"), ACT.Ln)
         warm = keep.tile([P, 1], F32, name="warm")
-        nc.scalar.activation(warm[:], ln_pw[:, PASSES - 1, PACK - 1 : PACK], ACT.Exp)
+        nc.scalar.activation(warm[:], terms[:, 0, 0:1], ACT.Exp)
+        nc.scalar.activation(terms[:, 3, :], hx_t[:].rearrange("p a t -> p (a t)"), ACT.Identity, scale=-1.0)
         for a in range(PASSES):
             for t in range(PACK):
                 nc.scalar.activation(
-                    bias[:, a, t : t + 1], hx_t[:, a, t : t + 1], ACT.Identity, bias=ln_pw[:, a, t : t + 1], scale=-1.0
+                    summed[:, a * PACK + t, :], terms[:, :, a * PACK + t], ACT.Identity, accum_out=bias[:, a, t : t + 1]
                 )
 
-        shift = keep.tile([P, PASSES, PACK, CHUNKS[LAST]], F32, name="shift")
-        for a in range(PASSES):
-            for t in range(PACK):
-                nc.scalar.activation(
-                    shift[:, a, t, :], hz_t[:, S2 - CHUNKS[LAST] : S2], ACT.Identity, bias=bias[:, a, t : t + 1], scale=-1.0
-                )
+        starts = [sum(CHUNKS[:c]) for c in range(len(CHUNKS))]
+        shift = {}
+        for c in SHIFTED:
+            shift[c] = keep.tile([P, PASSES, PACK, CHUNKS[c]], F32, name=f"shift{c}")
+            for a in range(PASSES):
+                for t in range(PACK):
+                    nc.scalar.activation(
+                        shift[c][:, a, t, :],
+                        hz_t[:, starts[c] : starts[c] + CHUNKS[c]],
+                        ACT.Identity,
+                        bias=bias[:, a, t : t + 1],
+                        scale=-1.0,
+                    )
 
-        vw = keep.tile([P, PASSES, PASS], U32, name="vw", align_bytes=64)
-        wq = [keep.tile([P, N], U32, name=f"wq{a}", align_bytes=64) for a in range(PASSES)]
-        wqs = [keep.tile([P, N], U8, name=f"wqs{a}", align_bytes=64) for a in range(PASSES)]
+        vw, wq, wqs = {}, {}, {}
         w_bf = [keep.tile([P, N * PACK], BF16, name=f"w_bf{a}", align_bytes=64) for a in range(PASSES)]
-        list_cols = GATHER // LIST_ROWS
+        cut_starts = [sum(CUTS[:g]) for g in range(len(CUTS))]
         v2w = {}
 
-        def gather_v2_words(g, tag):
-            v2w[g] = keep.tile([P, GATHER], U32, name=tag, align_bytes=64)
-            nc.vector.tensor_copy(v2w[g][:], tab2w[:].bitcast(U32).indirect(idx2[:, g * list_cols : (g + 1) * list_cols]))
+        def gather_v_words(a, tag):
+            vw[a] = keep.tile([P, PASS], U32, name=tag, align_bytes=64)
+            cols = idx[:, a * PASS // LIST_ROWS : (a + 1) * PASS // LIST_ROWS]
+            nc.vector.tensor_copy(vw[a][:].rearrange("p (t m) -> p m t", t=PACK), tabw[:].bitcast(U32).indirect(cols))
+
+        def gather_v2_words(g):
+            v2w[g] = keep.tile([P, CUTS[g]], U32, name=CUT_OVER[g], align_bytes=64)
+            cols = idx2[:, cut_starts[g] // LIST_ROWS : (cut_starts[g] + CUTS[g]) // LIST_ROWS]
+            nc.vector.tensor_copy(v2w[g][:], tab2w[:].bitcast(U32).indirect(cols))
 
         def round_w(part):
-            a, lo, tile = w_parts[part]
+            a, lo, width = W_CUTS[part]
             nc.scalar.activation(
-                w_bf[a][:, PACK * lo : PACK * (lo + tile.shape[2])].rearrange("p (c i t) -> p c t i", i=LINE, t=PACK),
-                tile[:].rearrange("p t (c i) -> p c t i", i=LINE),
+                w_bf[a][:, PACK * lo : PACK * (lo + width)].rearrange("p (c i t) -> p c t i", i=LINE, t=PACK),
+                w_parts[part].rearrange("p t (c i) -> p c t i", i=LINE),
                 ACT.Copy,
             )
 
         def quantize_w(a):
+            wq[a] = keep.tile([P, N], U32, name=QW_OVER[a], align_bytes=64)
+            wqs[a] = keep.tile([P, N], U8, name=f"wqs{a}", align_bytes=64)
             nc.vector.quantize_mx(out=wq[a][:].bitcast(FP8X4), scales=wqs[a][:], in_=w_bf[a][:])
 
-        starts = [sum(CHUNKS[:c]) for c in range(len(CHUNKS))]
         units = [(c, a) for c in range(len(CHUNKS)) for a in range(PASSES)]
         banks, slabs, z, h_bf, hq, hqs, acc = {}, {}, {}, {}, {}, {}, {}
 
         def product_a(u, t):
             c, a = units[u]
-            g, lo = divmod(starts[c], GATHER)
+            g = max(n for n in range(len(CUTS)) if cut_starts[n] <= starts[c])
+            lo = starts[c] - cut_starts[g]
             width = CHUNKS[c]
             share = BANK // width
             if t % share == 0:
-                banks[u] = psum_a.tile([P, BANK], F32, name="bank_a")
-            slabs[u, t] = banks[u][:, (t % share) * width : (t % share + 1) * width]
+                banks[u, t // share] = psum_a.tile([P, BANK], F32, name="bank_a")
+            slabs[u, t] = banks[u, t // share][:, (t % share) * width : (t % share + 1) * width]
             for js in pieces(width, (512, 256, 128)):
                 nc.tensor.matmul_mx(
                     out=slabs[u, t][:, js],
-                    lhsT=vw[:, a, t * P : (t + 1) * P].bitcast(FP8X4),
+                    lhsT=vw[a][:, t * P : (t + 1) * P].bitcast(FP8X4),
                     lhsT_scale=planes[:, a * PASS + t * P : a * PASS + (t + 1) * P],
                     rhs=v2w[g][:, lo + js.start : lo + js.stop].bitcast(FP8X4),
                     rhs_scale=planes[:, S + starts[c] + js.start : S + starts[c] + js.stop],
@@ -198,7 +234,8 @@ def tile_list_gp_inducing_mean_kernel(
             c, a = units[u]
             if t == 0:
                 z[u] = ring.tile([P, CHUNKS[c] // LINE, PACK, LINE], F32, name="z")
-            if c < LAST:
+            share = BANK // CHUNKS[c]
+            if c not in SHIFTED:
                 nc.vector.scalar_tensor_tensor(
                     z[u][:, :, t, :],
                     slabs[u, t].rearrange("p (c i) -> p c i", i=LINE),
@@ -207,36 +244,53 @@ def tile_list_gp_inducing_mean_kernel(
                     ALU.add,
                     ALU.subtract,
                 )
-            elif t == PACK - 1:
+            elif t % share == share - 1:
+                ts = slice(t + 1 - share, t + 1)
                 nc.vector.tensor_tensor(
-                    z[u][:].rearrange("p c t i -> p t c i"),
-                    banks[u][:].rearrange("p (t c i) -> p t c i", t=PACK, i=LINE),
-                    shift[:, a].rearrange("p t (c i) -> p t c i", i=LINE),
+                    z[u][:, :, ts, :].rearrange("p c t i -> p t c i"),
+                    banks[u, t // share][:].rearrange("p (t c i) -> p t c i", t=share, i=LINE),
+                    shift[c][:, a, ts, :].rearrange("p t (c i) -> p t c i", i=LINE),
                     ALU.add,
                 )
 
+        def parts(u):
+            width = CHUNKS[units[u][0]]
+            return pieces(width, (256, 128)) if u in SPLIT else [slice(0, width)]
+
         def kernel_values(u):
-            h_bf[u] = keep.tile([P, CHUNKS[units[u][0]] * PACK], BF16, name=f"h_bf{u}", align_bytes=64)
-            nc.scalar.activation(h_bf[u][:].rearrange("p (c i t) -> p c t i", i=LINE, t=PACK), z[u][:], ACT.Exp)
+            h_bf[u] = keep.tile([P, CHUNKS[units[u][0]] * PACK], BF16, name=H_OVER.get(u, f"h_bf{u}"), align_bytes=64)
+            for js in parts(u):
+                nc.scalar.activation(
+                    h_bf[u][:, PACK * js.start : PACK * js.stop].rearrange("p (c i t) -> p c t i", i=LINE, t=PACK),
+                    z[u][:, js.start // LINE : js.stop // LINE],
+                    ACT.Exp,
+                )
 
         def quantize_h(u):
             width = CHUNKS[units[u][0]]
             hq[u] = keep.tile([P, width], U32, name=f"hq{u}", align_bytes=64)
             hqs[u] = keep.tile([P, width], U8, name=f"hqs{u}", align_bytes=64)
-            nc.vector.quantize_mx(out=hq[u][:].bitcast(FP8X4), scales=hqs[u][:], in_=h_bf[u][:])
+            for js in parts(u):
+                nc.vector.quantize_mx(
+                    out=hq[u][:, js].bitcast(FP8X4), scales=hqs[u][:, js], in_=h_bf[u][:, PACK * js.start : PACK * js.stop]
+                )
 
         def tiles_per_bank(c):
-            return 2 if c == LAST else 1
+            return SHARE[c]
 
-        def product_y(u, nt):
+        def product_y(u, nt, part):
             c, a = units[u]
             width = CHUNKS[c]
             share = tiles_per_bank(c)
             place = nt % share
-            if a == 0 and place == 0:
-                acc[c, nt // share] = psum_y.tile([P, BANK], F32, name="bank_y")
+            if a == 0 and place == 0 and part.start == 0:
+                if (c, nt // share) in Y_IN_A:
+                    acc[c, nt // share] = psum_a.tile([P, BANK], F32, name="bank_a")
+                else:
+                    acc[c, nt // share] = psum_y.tile([P, BANK], F32, name="bank_y")
+            runs = [slice(part.start + js.start, part.start + js.stop) for js in pieces(part.stop - part.start, (512, 256, 128))]
             target = acc[c, nt // share][:, place * width : (place + 1) * width]
-            for js in pieces(width, (512, 256, 128)):
+            for js in runs:
                 nc.tensor.matmul_mx(
                     out=target[:, js],
                     lhsT=w4w[:, a, 2 * nt * P : 2 * (nt + 1) * P].bitcast(FP4X4),
@@ -246,7 +300,7 @@ def tile_list_gp_inducing_mean_kernel(
                     start=(a == 0 and place == 0 and js.start == 0),
                     stop=False,
                 )
-            for js in pieces(width, (512, 256, 128)):
+            for js in runs:
                 nc.tensor.matmul_mx(
                     out=target[:, js],
                     lhsT=wq[a][:, nt * P : (nt + 1) * P].bitcast(FP8X4),
@@ -264,7 +318,7 @@ def tile_list_gp_inducing_mean_kernel(
                 first = k * share
                 bank = acc[c, k][:, 0 : share * width].rearrange("p (s j) -> p s j", s=share)
                 res = keep.tile([P, share, width], F32, name=f"res{c}_{first}")
-                if c > 0 and k % 2 == 1:
+                if (c, k) in ON_VECTOR:
                     nc.vector.tensor_tensor(
                         res[:], bank, b_t[:, first : first + share].unsqueeze(2).to_broadcast([P, share, width]), ALU.add
                     )
@@ -276,37 +330,62 @@ def tile_list_gp_inducing_mean_kernel(
                     res[:],
                 )
 
-        nc.vector.tensor_copy(vw[:].rearrange("p a (t m) -> p a m t", t=PACK), tabw[:].bitcast(U32).indirect(idx[:]))
-        gather_v2_words(0, "v2w0")
-        gather_v2_words(1, "v2w1")
-        round_w(0)
-        round_w(1)
-        for t in range(PACK):
-            product_a(0, t)
+        def extras(step):
+            if step == VW1_AT:
+                gather_v_words(1, VW1_OVER)
+            for g in range(len(CUTS)):
+                if step == CUT_AT[g]:
+                    gather_v2_words(g)
+            for part in range(len(W_CUTS)):
+                if step == ROUND_AT[part]:
+                    round_w(part)
 
-        for u in range(len(units) + 2):
-            if u == 1:
-                quantize_w(0)
-            one_bank_next = u + 1 < len(units) and units[u + 1][0] == LAST
-            if one_bank_next:
-                for t in range(PACK):
-                    product_a(u + 1, t)
+        jobs = [(u, k) for u, (c, a) in enumerate(units) for k in range(PACK // (BANK // CHUNKS[c]))]
+
+        def fill_bank():
+            if jobs:
+                u, k = jobs[0]
+                c = units[u][0]
+                if units[u][1] in vw and any(cut_starts[g] <= starts[c] < cut_starts[g] + CUTS[g] for g in v2w):
+                    jobs.remove((u, k))
+                    share = BANK // CHUNKS[c]
+                    for t in range(k * share, (k + 1) * share):
+                        product_a(u, t)
+                    return 1
+            return 0
+
+        gather_v_words(0, "vw0")
+        extras(-1)
+        free = A_BANKS
+        for u in range(len(units) + Y_LAG + F_LAG):
+            for a in range(PASSES):
+                if QW_AT[a] == u - 0.5:
+                    quantize_w(a)
+            if Y_LAG == 1 and 1 <= u <= len(units):
+                quantize_h(u - 1)
+            for n in range(free):
+                free = free - fill_bank()
             for t in range(PACK):
                 if u < len(units):
                     exponent(u, t)
-                if u + 1 < len(units) and not one_bank_next:
-                    product_a(u + 1, t)
-                if u >= 2:
-                    product_y(u - 2, t)
+                    if (t + 1) % (BANK // CHUNKS[units[u][0]]) == 0:
+                        free = free + 1 - fill_bank()
+                if 0 <= u - Y_LAG < len(units):
+                    product_y(u - Y_LAG, t, parts(u - Y_LAG)[0])
+            if 0 <= u - Y_LAG < len(units):
+                for part in parts(u - Y_LAG)[1:]:
+                    for t in range(PACK):
+                        product_y(u - Y_LAG, t, part)
+            done = u - Y_LAG - F_LAG
+            if F_FIRST and done >= 0 and units[done][1] == PASSES - 1:
+                finish(units[done][0])
             if u < len(units):
                 kernel_values(u)
-            if u == 0:
-                round_w(2)
-            if 1 <= u <= len(units):
+            if Y_LAG == 2 and 1 <= u <= len(units):
                 quantize_h(u - 1)
-            if u >= 2 and units[u - 2][1] == PASSES - 1:
-                finish(units[u - 2][0])
-            if u == 1:
-                quantize_w(1)
-            if u == 2:
-                gather_v2_words(2, "h_bf1")
+            if not F_FIRST and done >= 0 and units[done][1] == PASSES - 1:
+                finish(units[done][0])
+            for a in range(PASSES):
+                if QW_AT[a] == u:
+                    quantize_w(a)
+            extras(u)

@@ -47,6 +47,7 @@ Y_LAG = 2
 F_LAG = 0
 F_FIRST = True
 SPLIT = []
+Y_FIRST = []
 Y_IN_A = [(2, 2), (2, 3)]
 FP4_FIRST = []
 SPREAD = 8
@@ -119,12 +120,13 @@ def tile_list_gp_inducing_mean_kernel(
         nc.sync.dma_start(tab2w[:], tab2_words[0].rearrange("p t i -> p (t i)").bitcast(I32))
         load_w(0)
 
-        nc.vector.tensor_copy(picked[:, 0:S].rearrange("p (a t m) -> p a m t", a=PASSES, t=PACK), tabs[:].indirect(idx[:]))
         terms = keep.tile([P, 4, PASSES * PACK], F32, name="terms")
         factors = keep.tile([P, 3, PASSES, PACK], F32, name="factors")
-        nc.gpsimd.tensor_scalar(factors[:, 0], pw_t[:], LN_LOW, LN_HIGH, ALU.max, ALU.min)
-        nc.gpsimd.tensor_scalar(factors[:, 1], pw_t[:], LN_HIGH, LN_LOW, ALU.max, ALU.mult)
-        nc.gpsimd.tensor_scalar(factors[:, 2], pw_t[:], LN_LOW, LN_HIGH, ALU.min, ALU.mult)
+        nc.vector.tensor_scalar(factors[:, 0], pw_t[:], LN_LOW, LN_HIGH, ALU.max, ALU.min)
+        nc.vector.tensor_scalar(factors[:, 1], pw_t[:], LN_HIGH, LN_LOW, ALU.max, ALU.mult)
+        nc.vector.tensor_scalar(factors[:, 2], pw_t[:], LN_LOW, LN_HIGH, ALU.min, ALU.mult)
+
+        nc.vector.tensor_copy(picked[:, 0:S].rearrange("p (a t m) -> p a m t", a=PASSES, t=PACK), tabs[:].indirect(idx[:]))
         nc.vector.tensor_copy(picked[:, S : S + S2], tab2s[:].indirect(idx2[:]))
         for r in range(SCALE_ROWS):
             nc.sync.dma_start(planes[r:P:32, :].bitcast(I32), picked[SPREAD * r : P : 32, :].bitcast(I32))
@@ -363,6 +365,9 @@ def tile_list_gp_inducing_mean_kernel(
                     quantize_w(a)
             if Y_LAG == 1 and 1 <= u <= len(units):
                 quantize_h(u - 1)
+            if u in Y_FIRST:
+                for t in range(PACK):
+                    product_y(u - Y_LAG, t, parts(u - Y_LAG)[0])
             for n in range(free):
                 free = free - fill_bank()
             for t in range(PACK):
@@ -370,7 +375,7 @@ def tile_list_gp_inducing_mean_kernel(
                     exponent(u, t)
                     if (t + 1) % (BANK // CHUNKS[units[u][0]]) == 0:
                         free = free + 1 - fill_bank()
-                if 0 <= u - Y_LAG < len(units):
+                if 0 <= u - Y_LAG < len(units) and u not in Y_FIRST:
                     product_y(u - Y_LAG, t, parts(u - Y_LAG)[0])
             if 0 <= u - Y_LAG < len(units):
                 for part in parts(u - Y_LAG)[1:]:

@@ -23,44 +23,16 @@ PASS = P * PACK
 PASSES = S // PASS
 N_TILES = N // P
 BANK = 512
+A_BANKS = 4
 LINE = 4
 LIST_ROWS = 16
 SCALE_ROWS = 4
-CHUNKS = [384, 512, 512, 128]
-CUTS = [384, 1152]
-CUT_OVER = ["v2w0", "v2w1"]
-CUT_AT = [-1, -1]
-SHIFTED = [3]
-SHARE = [1, 1, 1, 2]
-ON_VECTOR = [(1, 1), (1, 3), (2, 1), (2, 3), (3, 1)]
-W_CUTS = [(0, 0, 512), (1, 0, 256), (1, 256, 256)]
-ROUND_AT = [-1, -1, 0]
-QW_AT = [0.5, 2]
-QW_OVER = ["wq0", "wq1"]
-H_OVER = {}
-VW1_AT = -1
-VW1_OVER = "vw1"
-W4_BEFORE = 3
-Z_BUFS = 3
-A_BANKS = 4
-Y_LAG = 2
-F_LAG = 0
-F_FIRST = True
-SPLIT = []
-Y_FIRST = []
-Y_IN_A = [(2, 2), (2, 3)]
-FP4_FIRST = []
 SPREAD = 8
+CHUNKS = [512, 512, 256, 128, 128]
+LAST = len(CHUNKS) - 1
+WIDE = 2
+GATHERS = [512, 512, 256, 256]
 LN_LOW, LN_HIGH = 2.0**-64, 2.0**64
-
-
-def pieces(width, allowed):
-    runs, lo = [], 0
-    while lo < width:
-        step = max(n for n in allowed if n <= width - lo)
-        runs.append(slice(lo, lo + step))
-        lo = lo + step
-    return runs
 
 
 def tile_list_gp_inducing_mean_kernel(
@@ -69,10 +41,10 @@ def tile_list_gp_inducing_mean_kernel(
     nc = tc.nc
     with ExitStack() as ctx:
         keep = ctx.enter_context(tc.tile_pool(name="keep", bufs=1))
-        ring = ctx.enter_context(tc.tile_pool(name="ring", bufs=Z_BUFS))
+        ring = ctx.enter_context(tc.tile_pool(name="ring", bufs=2))
         late = ctx.enter_context(tc.tile_pool(name="late", bufs=1))
         psum_a = ctx.enter_context(tc.psum_pool(name="psum_a", bufs=A_BANKS))
-        psum_y = ctx.enter_context(tc.psum_pool(name="psum_y", bufs=8 - A_BANKS))
+        psum_y = ctx.enter_context(tc.psum_pool(name="psum_y", bufs=N_TILES))
 
         idx = keep.tile([P, S // LIST_ROWS], U16, name="idx")
         idx2 = keep.tile([P, S2 // LIST_ROWS], U16, name="idx2")
@@ -83,14 +55,7 @@ def tile_list_gp_inducing_mean_kernel(
         w4s = late.tile([P, PASSES, N], U8, name="w4s", align_bytes=64, offset=0)
         w4w = late.tile([P, PASSES, 2 * N], U8, name="w4w", align_bytes=64, offset=PASSES * N)
         b_t = late.tile([P, N_TILES], F32, name="b_t", align_bytes=64, offset=3 * PASSES * N)
-        w_first = keep.tile([P, PACK * W_CUTS[0][2]], F32, name="w_first", align_bytes=64)
-        w_rest = late.tile(
-            [P, PACK * (PASSES * N - W_CUTS[0][2])], F32, name="w_rest", align_bytes=64, offset=3 * PASSES * N + 64
-        )
-        w_parts = [w_first[:].rearrange("p (t n) -> p t n", t=PACK)]
-        for a, lo, width in W_CUTS[1:]:
-            place = PACK * (a * N + lo - W_CUTS[0][2])
-            w_parts.append(w_rest[:, place : place + PACK * width].rearrange("p (t n) -> p t n", t=PACK))
+        w_raw = late.tile([P, PASSES * PACK * N], F32, name="w_raw", align_bytes=64, offset=3 * PASSES * N + 64)
         picked = keep.tile([P, S + S2], U8, name="picked", align_bytes=64)
         planes = keep.tile([P, S + S2], U8, name="planes", align_bytes=64)
         hx_t = keep.tile([P, PASSES, PACK], F32, name="hx_t", align_bytes=64)
@@ -104,12 +69,7 @@ def tile_list_gp_inducing_mean_kernel(
         make_identity(nc, ident[:])
         nc.gpsimd.memset(planes[:].bitcast(I32), 0)
 
-        def load_w(part):
-            a, lo, width = W_CUTS[part]
-            rows = w[a * PASS : (a + 1) * PASS, lo : lo + width]
-            nc.sync.dma_start(w_parts[part], rows.rearrange("(p t) n -> p t n", t=PACK))
-
-        nc.sync.dma_start(pw_t[:], pw.rearrange("(a p t) -> p a t", a=PASSES, t=PACK))
+        nc.scalar.dma_start(pw_t[:], pw.rearrange("(a p t) -> p a t", a=PASSES, t=PACK))
         nc.sync.dma_start(idx[:], offs)
         nc.sync.dma_start(tabs[0:P:SPREAD, :].bitcast(I32), tab_scales[0].bitcast(I32))
         nc.sync.dma_start(hz_col[:], hz.rearrange("(p c) -> p c", p=P))
@@ -118,9 +78,7 @@ def tile_list_gp_inducing_mean_kernel(
         nc.sync.dma_start(tab2s[0:P:SPREAD, :].bitcast(I32), tab2_scales[0].bitcast(I32))
         nc.sync.dma_start(tabw[:], tab_words[0].rearrange("p t i -> p (t i)").bitcast(I32))
         nc.sync.dma_start(tab2w[:], tab2_words[0].rearrange("p t i -> p (t i)").bitcast(I32))
-        load_w(0)
 
-        terms = keep.tile([P, 4, PASSES * PACK], F32, name="terms")
         factors = keep.tile([P, 3, PASSES, PACK], F32, name="factors")
         nc.vector.tensor_scalar(factors[:, 0], pw_t[:], LN_LOW, LN_HIGH, ALU.max, ALU.min)
         nc.vector.tensor_scalar(factors[:, 1], pw_t[:], LN_HIGH, LN_LOW, ALU.max, ALU.mult)
@@ -132,16 +90,15 @@ def tile_list_gp_inducing_mean_kernel(
             nc.sync.dma_start(planes[r:P:32, :].bitcast(I32), picked[SPREAD * r : P : 32, :].bitcast(I32))
 
         nc.gpsimd.memset(w4s[:].bitcast(I32), 0)
-        for part in range(1, len(W_CUTS) + 1):
-            if part == W4_BEFORE:
-                nc.sync.dma_start(w4w[:].bitcast(I32), w4_words.rearrange("a p c -> p a c").bitcast(I32))
-                for r in range(SCALE_ROWS):
-                    nc.sync.dma_start(
-                        w4s[r:P:32, :, :].bitcast(I32),
-                        w4_scales[:, r : 4 * SCALE_ROWS : SCALE_ROWS, :].rearrange("a q c -> q a c").bitcast(I32),
-                    )
-            if part < len(W_CUTS):
-                load_w(part)
+        w_rows = [w_raw[:, a * PACK * N : (a + 1) * PACK * N].rearrange("p (t n) -> p t n", t=PACK) for a in range(PASSES)]
+        for a in range(PASSES):
+            nc.sync.dma_start(w_rows[a], w[a * PASS : (a + 1) * PASS, :].rearrange("(p t) n -> p t n", t=PACK))
+        nc.sync.dma_start(w4w[:].bitcast(I32), w4_words.rearrange("a p c -> p a c").bitcast(I32))
+        for r in range(SCALE_ROWS):
+            nc.sync.dma_start(
+                w4s[r:P:32, :, :].bitcast(I32),
+                w4_scales[:, r : 4 * SCALE_ROWS : SCALE_ROWS, :].rearrange("a q c -> q a c").bitcast(I32),
+            )
         with nc.allow_non_contiguous_dma(reason="one bias value a partition"):
             nc.sync.dma_start(b_t[:], b.rearrange("(c p) -> p c", p=P))
 
@@ -155,162 +112,134 @@ def tile_list_gp_inducing_mean_kernel(
                 spread[:].rearrange("p (c m) -> p m c", c=LINE),
             )
 
+        terms = keep.tile([P, 4, PASSES * PACK], F32, name="terms")
+        terms_out = keep.tile([P, PASSES * PACK, 4], F32, name="terms_out")
         bias = keep.tile([P, PASSES, PACK], F32, name="bias")
-        summed = keep.tile([P, PASSES * PACK, 4], F32, name="summed")
         nc.scalar.activation(terms[:, 0:3, :], factors[:].rearrange("p f a t -> p f (a t)"), ACT.Ln)
         warm = keep.tile([P, 1], F32, name="warm")
         nc.scalar.activation(warm[:], terms[:, 0, 0:1], ACT.Exp)
         nc.scalar.activation(terms[:, 3, :], hx_t[:].rearrange("p a t -> p (a t)"), ACT.Identity, scale=-1.0)
         for a in range(PASSES):
             for t in range(PACK):
-                nc.scalar.activation(
-                    summed[:, a * PACK + t, :], terms[:, :, a * PACK + t], ACT.Identity, accum_out=bias[:, a, t : t + 1]
-                )
+                slab = a * PACK + t
+                nc.scalar.activation(terms_out[:, slab, :], terms[:, :, slab], ACT.Identity, accum_out=bias[:, a, t : t + 1])
 
         starts = [sum(CHUNKS[:c]) for c in range(len(CHUNKS))]
-        shift = {}
-        for c in SHIFTED:
-            shift[c] = keep.tile([P, PASSES, PACK, CHUNKS[c]], F32, name=f"shift{c}")
-            for a in range(PASSES):
-                for t in range(PACK):
-                    nc.scalar.activation(
-                        shift[c][:, a, t, :],
-                        hz_t[:, starts[c] : starts[c] + CHUNKS[c]],
-                        ACT.Identity,
-                        bias=bias[:, a, t : t + 1],
-                        scale=-1.0,
-                    )
+        shift = keep.tile([P, PASSES, PACK, S2 - starts[WIDE]], F32, name="shift")
+        for a in range(PASSES):
+            for t in range(PACK):
+                nc.scalar.activation(
+                    shift[:, a, t, :], hz_t[:, starts[WIDE] : S2], ACT.Identity, bias=bias[:, a, t : t + 1], scale=-1.0
+                )
 
-        vw, wq, wqs = {}, {}, {}
+        vw = keep.tile([P, PASSES, PASS], U32, name="vw", align_bytes=64)
+        wq = [keep.tile([P, N], U32, name=f"wq{a}", align_bytes=64) for a in range(PASSES)]
+        wqs = [keep.tile([P, N], U8, name=f"wqs{a}", align_bytes=64) for a in range(PASSES)]
         w_bf = [keep.tile([P, N * PACK], BF16, name=f"w_bf{a}", align_bytes=64) for a in range(PASSES)]
-        cut_starts = [sum(CUTS[:g]) for g in range(len(CUTS))]
+        gather_starts = [sum(GATHERS[:g]) for g in range(len(GATHERS))]
         v2w = {}
 
-        def gather_v_words(a, tag):
-            vw[a] = keep.tile([P, PASS], U32, name=tag, align_bytes=64)
-            cols = idx[:, a * PASS // LIST_ROWS : (a + 1) * PASS // LIST_ROWS]
-            nc.vector.tensor_copy(vw[a][:].rearrange("p (t m) -> p m t", t=PACK), tabw[:].bitcast(U32).indirect(cols))
+        def gather_v2_words(g, tag):
+            v2w[g] = keep.tile([P, GATHERS[g]], U32, name=tag, align_bytes=64)
+            entries = idx2[:, gather_starts[g] // LIST_ROWS : (gather_starts[g] + GATHERS[g]) // LIST_ROWS]
+            nc.vector.tensor_copy(v2w[g][:], tab2w[:].bitcast(U32).indirect(entries))
 
-        def gather_v2_words(g):
-            v2w[g] = keep.tile([P, CUTS[g]], U32, name=CUT_OVER[g], align_bytes=64)
-            cols = idx2[:, cut_starts[g] // LIST_ROWS : (cut_starts[g] + CUTS[g]) // LIST_ROWS]
-            nc.vector.tensor_copy(v2w[g][:], tab2w[:].bitcast(U32).indirect(cols))
-
-        def round_w(part):
-            a, lo, width = W_CUTS[part]
+        def round_w(a):
             nc.scalar.activation(
-                w_bf[a][:, PACK * lo : PACK * (lo + width)].rearrange("p (c i t) -> p c t i", i=LINE, t=PACK),
-                w_parts[part].rearrange("p t (c i) -> p c t i", i=LINE),
+                w_bf[a][:].rearrange("p (c i t) -> p c t i", i=LINE, t=PACK),
+                w_rows[a].rearrange("p t (c i) -> p c t i", i=LINE),
                 ACT.Copy,
             )
 
         def quantize_w(a):
-            wq[a] = keep.tile([P, N], U32, name=QW_OVER[a], align_bytes=64)
-            wqs[a] = keep.tile([P, N], U8, name=f"wqs{a}", align_bytes=64)
             nc.vector.quantize_mx(out=wq[a][:].bitcast(FP8X4), scales=wqs[a][:], in_=w_bf[a][:])
 
         units = [(c, a) for c in range(len(CHUNKS)) for a in range(PASSES)]
-        banks, slabs, z, h_bf, hq, hqs, acc = {}, {}, {}, {}, {}, {}, {}
+        fills = [(u, t, BANK // CHUNKS[c]) for u, (c, a) in enumerate(units) for t in range(0, PACK, BANK // CHUNKS[c])]
+        banks, z, h_bf, hq, hqs, acc = {}, {}, {}, {}, {}, {}
 
-        def product_a(u, t):
+        def products_a(f):
+            u, first, count = fills[f]
             c, a = units[u]
-            g = max(n for n in range(len(CUTS)) if cut_starts[n] <= starts[c])
-            lo = starts[c] - cut_starts[g]
+            g = max(n for n in range(len(GATHERS)) if gather_starts[n] <= starts[c])
+            lo = starts[c] - gather_starts[g]
             width = CHUNKS[c]
-            share = BANK // width
-            if t % share == 0:
-                banks[u, t // share] = psum_a.tile([P, BANK], F32, name="bank_a")
-            slabs[u, t] = banks[u, t // share][:, (t % share) * width : (t % share + 1) * width]
-            for js in pieces(width, (512, 256, 128)):
+            banks[f] = psum_a.tile([P, BANK], F32, name="bank_a")
+            for t in range(first, first + count):
                 nc.tensor.matmul_mx(
-                    out=slabs[u, t][:, js],
-                    lhsT=vw[a][:, t * P : (t + 1) * P].bitcast(FP8X4),
+                    out=banks[f][:, (t - first) * width : (t - first + 1) * width],
+                    lhsT=vw[:, a, t * P : (t + 1) * P].bitcast(FP8X4),
                     lhsT_scale=planes[:, a * PASS + t * P : a * PASS + (t + 1) * P],
-                    rhs=v2w[g][:, lo + js.start : lo + js.stop].bitcast(FP8X4),
-                    rhs_scale=planes[:, S + starts[c] + js.start : S + starts[c] + js.stop],
+                    rhs=v2w[g][:, lo : lo + width].bitcast(FP8X4),
+                    rhs_scale=planes[:, S + starts[c] : S + starts[c] + width],
                     start=True,
                     stop=True,
                 )
 
-        def exponent(u, t):
+        def exponents(f):
+            u, first, count = fills[f]
             c, a = units[u]
-            if t == 0:
+            if first == 0:
                 z[u] = ring.tile([P, CHUNKS[c] // LINE, PACK, LINE], F32, name="z")
-            share = BANK // CHUNKS[c]
-            if c not in SHIFTED:
+            if c < WIDE:
                 nc.vector.scalar_tensor_tensor(
-                    z[u][:, :, t, :],
-                    slabs[u, t].rearrange("p (c i) -> p c i", i=LINE),
-                    bias[:, a, t : t + 1],
+                    z[u][:, :, first, :],
+                    banks[f][:].rearrange("p (c i) -> p c i", i=LINE),
+                    bias[:, a, first : first + 1],
                     hz_t[:, starts[c] : starts[c] + CHUNKS[c]].rearrange("p (c i) -> p c i", i=LINE),
                     ALU.add,
                     ALU.subtract,
                 )
-            elif t % share == share - 1:
-                ts = slice(t + 1 - share, t + 1)
+            else:
+                lo = starts[c] - starts[WIDE]
                 nc.vector.tensor_tensor(
-                    z[u][:, :, ts, :].rearrange("p c t i -> p t c i"),
-                    banks[u, t // share][:].rearrange("p (t c i) -> p t c i", t=share, i=LINE),
-                    shift[c][:, a, ts, :].rearrange("p t (c i) -> p t c i", i=LINE),
+                    z[u][:, :, first : first + count, :].rearrange("p c t i -> p t c i"),
+                    banks[f][:].rearrange("p (t c i) -> p t c i", t=count, i=LINE),
+                    shift[:, a, first : first + count, lo : lo + CHUNKS[c]].rearrange("p t (c i) -> p t c i", i=LINE),
                     ALU.add,
                 )
 
-        def parts(u):
-            width = CHUNKS[units[u][0]]
-            return pieces(width, (256, 128)) if u in SPLIT else [slice(0, width)]
-
         def kernel_values(u):
-            h_bf[u] = keep.tile([P, CHUNKS[units[u][0]] * PACK], BF16, name=H_OVER.get(u, f"h_bf{u}"), align_bytes=64)
-            for js in parts(u):
-                nc.scalar.activation(
-                    h_bf[u][:, PACK * js.start : PACK * js.stop].rearrange("p (c i t) -> p c t i", i=LINE, t=PACK),
-                    z[u][:, js.start // LINE : js.stop // LINE],
-                    ACT.Exp,
-                )
+            h_bf[u] = keep.tile([P, CHUNKS[units[u][0]] * PACK], BF16, name=f"h_bf{u}", align_bytes=64)
+            nc.scalar.activation(h_bf[u][:].rearrange("p (c i t) -> p c t i", i=LINE, t=PACK), z[u][:], ACT.Exp)
 
         def quantize_h(u):
             width = CHUNKS[units[u][0]]
             hq[u] = keep.tile([P, width], U32, name=f"hq{u}", align_bytes=64)
             hqs[u] = keep.tile([P, width], U8, name=f"hqs{u}", align_bytes=64)
-            for js in parts(u):
-                nc.vector.quantize_mx(
-                    out=hq[u][:, js].bitcast(FP8X4), scales=hqs[u][:, js], in_=h_bf[u][:, PACK * js.start : PACK * js.stop]
-                )
+            nc.vector.quantize_mx(out=hq[u][:].bitcast(FP8X4), scales=hqs[u][:], in_=h_bf[u][:])
 
         def tiles_per_bank(c):
-            return SHARE[c]
+            return 2 if WIDE <= c < LAST else 1
 
-        def product_y(u, nt, part):
+        def products_y(u):
             c, a = units[u]
             width = CHUNKS[c]
             share = tiles_per_bank(c)
-            place = nt % share
-            if a == 0 and place == 0 and part.start == 0:
-                if (c, nt // share) in Y_IN_A:
-                    acc[c, nt // share] = psum_a.tile([P, BANK], F32, name="bank_a")
-                else:
+            for nt in range(N_TILES):
+                place = nt % share
+                if a == 0 and c == LAST and nt < 2:
+                    acc[c, nt] = psum_a.tile([P, BANK], F32, name="bank_a")
+                elif a == 0 and place == 0:
                     acc[c, nt // share] = psum_y.tile([P, BANK], F32, name="bank_y")
-            runs = [slice(part.start + js.start, part.start + js.stop) for js in pieces(part.stop - part.start, (512, 256, 128))]
-            target = acc[c, nt // share][:, place * width : (place + 1) * width]
-            for js in runs:
+                target = acc[c, nt // share][:, place * width : (place + 1) * width]
                 nc.tensor.matmul_mx(
-                    out=target[:, js],
+                    out=target,
                     lhsT=w4w[:, a, 2 * nt * P : 2 * (nt + 1) * P].bitcast(FP4X4),
                     lhsT_scale=w4s[:, a, nt * P : (nt + 1) * P],
-                    rhs=hq[u][:, js].bitcast(FP8X4),
-                    rhs_scale=hqs[u][:, js],
-                    start=(a == 0 and place == 0 and js.start == 0),
+                    rhs=hq[u][:].bitcast(FP8X4),
+                    rhs_scale=hqs[u][:],
+                    start=(a == 0 and place == 0),
                     stop=False,
                 )
-            for js in runs:
                 nc.tensor.matmul_mx(
-                    out=target[:, js],
+                    out=target,
                     lhsT=wq[a][:, nt * P : (nt + 1) * P].bitcast(FP8X4),
                     lhsT_scale=wqs[a][:, nt * P : (nt + 1) * P],
-                    rhs=hq[u][:, js].bitcast(FP8X4),
-                    rhs_scale=hqs[u][:, js],
+                    rhs=hq[u][:].bitcast(FP8X4),
+                    rhs_scale=hqs[u][:],
                     start=False,
-                    stop=(a == PASSES - 1 and place == share - 1 and js.stop == width),
+                    stop=(a == PASSES - 1 and place == share - 1),
                 )
 
         def finish(c):
@@ -320,7 +249,7 @@ def tile_list_gp_inducing_mean_kernel(
                 first = k * share
                 bank = acc[c, k][:, 0 : share * width].rearrange("p (s j) -> p s j", s=share)
                 res = keep.tile([P, share, width], F32, name=f"res{c}_{first}")
-                if (c, k) in ON_VECTOR:
+                if c > 0 and k % 2 == (0 if c < WIDE else 1):
                     nc.vector.tensor_tensor(
                         res[:], bank, b_t[:, first : first + share].unsqueeze(2).to_broadcast([P, share, width]), ALU.add
                     )
@@ -332,65 +261,32 @@ def tile_list_gp_inducing_mean_kernel(
                     res[:],
                 )
 
-        def extras(step):
-            if step == VW1_AT:
-                gather_v_words(1, VW1_OVER)
-            for g in range(len(CUTS)):
-                if step == CUT_AT[g]:
-                    gather_v2_words(g)
-            for part in range(len(W_CUTS)):
-                if step == ROUND_AT[part]:
-                    round_w(part)
+        nc.vector.tensor_copy(vw[:].rearrange("p a (t m) -> p a m t", t=PACK), tabw[:].bitcast(U32).indirect(idx[:]))
+        for g in range(WIDE):
+            gather_v2_words(g, f"v2w{g}")
+        round_w(0)
+        for f in range(A_BANKS):
+            products_a(f)
 
-        jobs = [(u, k) for u, (c, a) in enumerate(units) for k in range(PACK // (BANK // CHUNKS[c]))]
-
-        def fill_bank():
-            if jobs:
-                u, k = jobs[0]
-                c = units[u][0]
-                if units[u][1] in vw and any(cut_starts[g] <= starts[c] < cut_starts[g] + CUTS[g] for g in v2w):
-                    jobs.remove((u, k))
-                    share = BANK // CHUNKS[c]
-                    for t in range(k * share, (k + 1) * share):
-                        product_a(u, t)
-                    return 1
-            return 0
-
-        gather_v_words(0, "vw0")
-        extras(-1)
-        free = A_BANKS
-        for u in range(len(units) + Y_LAG + F_LAG):
-            for a in range(PASSES):
-                if QW_AT[a] == u - 0.5:
-                    quantize_w(a)
-            if Y_LAG == 1 and 1 <= u <= len(units):
-                quantize_h(u - 1)
-            if u in Y_FIRST:
-                for t in range(PACK):
-                    product_y(u - Y_LAG, t, parts(u - Y_LAG)[0])
-            for n in range(free):
-                free = free - fill_bank()
-            for t in range(PACK):
-                if u < len(units):
-                    exponent(u, t)
-                    if (t + 1) % (BANK // CHUNKS[units[u][0]]) == 0:
-                        free = free + 1 - fill_bank()
-                if 0 <= u - Y_LAG < len(units) and u not in Y_FIRST:
-                    product_y(u - Y_LAG, t, parts(u - Y_LAG)[0])
-            if 0 <= u - Y_LAG < len(units):
-                for part in parts(u - Y_LAG)[1:]:
-                    for t in range(PACK):
-                        product_y(u - Y_LAG, t, part)
-            done = u - Y_LAG - F_LAG
-            if F_FIRST and done >= 0 and units[done][1] == PASSES - 1:
-                finish(units[done][0])
+        for u in range(len(units) + 2):
+            if u == 1:
+                quantize_w(0)
+            if u >= 2:
+                products_y(u - 2)
+            for f in range(len(fills)):
+                if fills[f][0] == u:
+                    exponents(f)
+                    if f + A_BANKS < len(fills):
+                        products_a(f + A_BANKS)
             if u < len(units):
                 kernel_values(u)
-            if Y_LAG == 2 and 1 <= u <= len(units):
+            if 1 <= u <= len(units):
                 quantize_h(u - 1)
-            if not F_FIRST and done >= 0 and units[done][1] == PASSES - 1:
-                finish(units[done][0])
-            for a in range(PASSES):
-                if QW_AT[a] == u:
-                    quantize_w(a)
-            extras(u)
+            if u >= 2 and units[u - 2][1] == PASSES - 1:
+                finish(units[u - 2][0])
+            if u == 0:
+                round_w(1)
+            if u == 2:
+                quantize_w(1)
+            if WIDE <= u < len(GATHERS):
+                gather_v2_words(u, f"h_bf{u - 1}")

@@ -28,10 +28,12 @@ LINE = 4
 LIST_ROWS = 16
 SCALE_ROWS = 4
 SPREAD = 8
-CHUNKS = [512, 512, 256, 128, 128]
-LAST = len(CHUNKS) - 1
-WIDE = 2
-GATHERS = [512, 512, 256, 256]
+TABLE_ROW = P - 4 * SCALE_ROWS
+CHUNKS = [(0, 512, 1), (512, 512, 1), (1024, 256, 2), (1280, 128, 2), (1408, 128, 1)]
+UNITS = [(0, 512, 0), (0, 512, 1), (512, 512, 0), (512, 512, 1), (1024, 256, 0), (1024, 256, 1), (1280, 128, 0), (1280, 128, 1), (1408, 128, 0), (1408, 128, 1)]
+GATHERS = [(0, 512, None), (512, 512, None), (1024, 256, 1), (1280, 256, 2)]
+SHIFT_FROM = 1024
+HELD = {}
 LN_LOW, LN_HIGH = 2.0**-64, 2.0**64
 
 
@@ -44,7 +46,7 @@ def tile_list_gp_inducing_mean_kernel(
         ring = ctx.enter_context(tc.tile_pool(name="ring", bufs=2))
         late = ctx.enter_context(tc.tile_pool(name="late", bufs=1))
         psum_a = ctx.enter_context(tc.psum_pool(name="psum_a", bufs=A_BANKS))
-        psum_y = ctx.enter_context(tc.psum_pool(name="psum_y", bufs=N_TILES))
+        psum_y = ctx.enter_context(tc.psum_pool(name="psum_y", bufs=8 - A_BANKS))
 
         idx = keep.tile([P, S // LIST_ROWS], U16, name="idx")
         idx2 = keep.tile([P, S2 // LIST_ROWS], U16, name="idx2")
@@ -55,7 +57,8 @@ def tile_list_gp_inducing_mean_kernel(
         w4s = late.tile([P, PASSES, N], U8, name="w4s", align_bytes=64, offset=0)
         w4w = late.tile([P, PASSES, 2 * N], U8, name="w4w", align_bytes=64, offset=PASSES * N)
         b_t = late.tile([P, N_TILES], F32, name="b_t", align_bytes=64, offset=3 * PASSES * N)
-        w_raw = late.tile([P, PASSES * PACK * N], F32, name="w_raw", align_bytes=64, offset=3 * PASSES * N + 64)
+        w_both = late.tile([P, PASSES * PACK * N], F32, name="w_both", align_bytes=64, offset=3 * PASSES * N + 64)
+        w_raw = [w_both[:, a * PACK * N : (a + 1) * PACK * N].rearrange("p (t n) -> p t n", t=PACK) for a in range(PASSES)]
         picked = keep.tile([P, S + S2], U8, name="picked", align_bytes=64)
         planes = keep.tile([P, S + S2], U8, name="planes", align_bytes=64)
         hx_t = keep.tile([P, PASSES, PACK], F32, name="hx_t", align_bytes=64)
@@ -64,19 +67,23 @@ def tile_list_gp_inducing_mean_kernel(
         hz_t = keep.tile([P, S2], F32, name="hz_t")
         ident = keep.tile([P, P], F32, name="ident")
 
-        nc.gpsimd.memset(tabs[:].bitcast(I32), 0)
-        nc.vector.memset(tab2s[:].bitcast(I32), 0)
+        nc.vector.memset(tabs[0:TABLE_ROW, :].bitcast(I32), 0)
+        nc.vector.memset(tab2s[0:TABLE_ROW, :].bitcast(I32), 0)
         make_identity(nc, ident[:])
-        nc.gpsimd.memset(planes[:].bitcast(I32), 0)
+        nc.vector.memset(planes[:].bitcast(I32), 0)
+
+        def load_w(a):
+            nc.sync.dma_start(w_raw[a], w[a * PASS : (a + 1) * PASS, :].rearrange("(p t) n -> p t n", t=PACK))
 
         nc.scalar.dma_start(pw_t[:], pw.rearrange("(a p t) -> p a t", a=PASSES, t=PACK))
+        nc.scalar.dma_start(hz_col[:], hz.rearrange("(p c) -> p c", p=P))
         nc.sync.dma_start(idx[:], offs)
-        nc.sync.dma_start(tabs[0:P:SPREAD, :].bitcast(I32), tab_scales[0].bitcast(I32))
-        nc.sync.dma_start(hz_col[:], hz.rearrange("(p c) -> p c", p=P))
-        nc.sync.dma_start(hx_t[:], hx.rearrange("(a p t) -> p a t", a=PASSES, t=PACK))
+        nc.sync.dma_start(tabs[TABLE_ROW:P, :].bitcast(I32), tab_scales[0].bitcast(I32))
         nc.sync.dma_start(idx2[:], offs2)
-        nc.sync.dma_start(tab2s[0:P:SPREAD, :].bitcast(I32), tab2_scales[0].bitcast(I32))
+        nc.sync.dma_start(tab2s[TABLE_ROW:P, :].bitcast(I32), tab2_scales[0].bitcast(I32))
         nc.sync.dma_start(tabw[:], tab_words[0].rearrange("p t i -> p (t i)").bitcast(I32))
+        nc.sync.dma_start(hx_t[:], hx.rearrange("(a p t) -> p a t", a=PASSES, t=PACK))
+
         nc.sync.dma_start(tab2w[:], tab2_words[0].rearrange("p t i -> p (t i)").bitcast(I32))
 
         factors = keep.tile([P, 3, PASSES, PACK], F32, name="factors")
@@ -87,12 +94,12 @@ def tile_list_gp_inducing_mean_kernel(
         nc.vector.tensor_copy(picked[:, 0:S].rearrange("p (a t m) -> p a m t", a=PASSES, t=PACK), tabs[:].indirect(idx[:]))
         nc.vector.tensor_copy(picked[:, S : S + S2], tab2s[:].indirect(idx2[:]))
         for r in range(SCALE_ROWS):
-            nc.sync.dma_start(planes[r:P:32, :].bitcast(I32), picked[SPREAD * r : P : 32, :].bitcast(I32))
+            nc.sync.dma_start(planes[r:P:32, :].bitcast(I32), picked[TABLE_ROW + r : P : SCALE_ROWS, :].bitcast(I32))
 
         nc.gpsimd.memset(w4s[:].bitcast(I32), 0)
-        w_rows = [w_raw[:, a * PACK * N : (a + 1) * PACK * N].rearrange("p (t n) -> p t n", t=PACK) for a in range(PASSES)]
-        for a in range(PASSES):
-            nc.sync.dma_start(w_rows[a], w[a * PASS : (a + 1) * PASS, :].rearrange("(p t) n -> p t n", t=PACK))
+
+        load_w(0)
+        load_w(1)
         nc.sync.dma_start(w4w[:].bitcast(I32), w4_words.rearrange("a p c -> p a c").bitcast(I32))
         for r in range(SCALE_ROWS):
             nc.sync.dma_start(
@@ -124,112 +131,119 @@ def tile_list_gp_inducing_mean_kernel(
                 slab = a * PACK + t
                 nc.scalar.activation(terms_out[:, slab, :], terms[:, :, slab], ACT.Identity, accum_out=bias[:, a, t : t + 1])
 
-        starts = [sum(CHUNKS[:c]) for c in range(len(CHUNKS))]
-        shift = keep.tile([P, PASSES, PACK, S2 - starts[WIDE]], F32, name="shift")
-        for a in range(PASSES):
-            for t in range(PACK):
-                nc.scalar.activation(
-                    shift[:, a, t, :], hz_t[:, starts[WIDE] : S2], ACT.Identity, bias=bias[:, a, t : t + 1], scale=-1.0
-                )
-
         vw = keep.tile([P, PASSES, PASS], U32, name="vw", align_bytes=64)
         wq = [keep.tile([P, N], U32, name=f"wq{a}", align_bytes=64) for a in range(PASSES)]
         wqs = [keep.tile([P, N], U8, name=f"wqs{a}", align_bytes=64) for a in range(PASSES)]
         w_bf = [keep.tile([P, N * PACK], BF16, name=f"w_bf{a}", align_bytes=64) for a in range(PASSES)]
-        gather_starts = [sum(GATHERS[:g]) for g in range(len(GATHERS))]
         v2w = {}
 
         def gather_v2_words(g, tag):
-            v2w[g] = keep.tile([P, GATHERS[g]], U32, name=tag, align_bytes=64)
-            entries = idx2[:, gather_starts[g] // LIST_ROWS : (gather_starts[g] + GATHERS[g]) // LIST_ROWS]
+            lo, width, after = GATHERS[g]
+            v2w[g] = keep.tile([P, width], U32, name=tag, align_bytes=64)
+            entries = idx2[:, lo // LIST_ROWS : (lo + width) // LIST_ROWS]
             nc.vector.tensor_copy(v2w[g][:], tab2w[:].bitcast(U32).indirect(entries))
 
-        def round_w(a):
-            nc.scalar.activation(
-                w_bf[a][:].rearrange("p (c i t) -> p c t i", i=LINE, t=PACK),
-                w_rows[a].rearrange("p t (c i) -> p c t i", i=LINE),
-                ACT.Copy,
-            )
+        def round_w(a, first, count):
+            columns = slice(first * P, (first + count) * P)
+            rounded = w_bf[a][:, first * PASS : (first + count) * PASS].rearrange("p (c i t) -> p c t i", i=LINE, t=PACK)
+            rows = w_raw[a][:, :, columns].rearrange("p t (c i) -> p c t i", i=LINE)
+            if a == 1 and first > 0:
+                nc.vector.tensor_copy(rounded, rows)
+            else:
+                nc.scalar.activation(rounded, rows, ACT.Copy)
 
         def quantize_w(a):
             nc.vector.quantize_mx(out=wq[a][:].bitcast(FP8X4), scales=wqs[a][:], in_=w_bf[a][:])
 
-        units = [(c, a) for c in range(len(CHUNKS)) for a in range(PASSES)]
-        fills = [(u, t, BANK // CHUNKS[c]) for u, (c, a) in enumerate(units) for t in range(0, PACK, BANK // CHUNKS[c])]
+        round_w(0, 0, N_TILES)
+        shift = keep.tile([P, PASSES, PACK, S2 - SHIFT_FROM], F32, name="shift")
+        for a in range(PASSES):
+            for t in range(PACK):
+                nc.scalar.activation(
+                    shift[:, a, t, :], hz_t[:, SHIFT_FROM:S2], ACT.Identity, bias=bias[:, a, t : t + 1], scale=-1.0
+                )
+
+        fills = [(u, t, BANK // width) for u, (lo, width, a) in enumerate(UNITS) for t in range(0, PACK, BANK // width)]
         banks, z, h_bf, hq, hqs, acc = {}, {}, {}, {}, {}, {}
 
         def products_a(f):
             u, first, count = fills[f]
-            c, a = units[u]
-            g = max(n for n in range(len(GATHERS)) if gather_starts[n] <= starts[c])
-            lo = starts[c] - gather_starts[g]
-            width = CHUNKS[c]
+            lo, width, a = UNITS[u]
             banks[f] = psum_a.tile([P, BANK], F32, name="bank_a")
             for t in range(first, first + count):
-                nc.tensor.matmul_mx(
-                    out=banks[f][:, (t - first) * width : (t - first + 1) * width],
-                    lhsT=vw[:, a, t * P : (t + 1) * P].bitcast(FP8X4),
-                    lhsT_scale=planes[:, a * PASS + t * P : a * PASS + (t + 1) * P],
-                    rhs=v2w[g][:, lo : lo + width].bitcast(FP8X4),
-                    rhs_scale=planes[:, S + starts[c] : S + starts[c] + width],
-                    start=True,
-                    stop=True,
-                )
+                for g, (g_lo, g_width, after) in enumerate(GATHERS):
+                    left, right = max(lo, g_lo), min(lo + width, g_lo + g_width)
+                    if left < right:
+                        place = (t - first) * width + left - lo
+                        nc.tensor.matmul_mx(
+                            out=banks[f][:, place : place + right - left],
+                            lhsT=vw[:, a, t * P : (t + 1) * P].bitcast(FP8X4),
+                            lhsT_scale=planes[:, a * PASS + t * P : a * PASS + (t + 1) * P],
+                            rhs=v2w[g][:, left - g_lo : right - g_lo].bitcast(FP8X4),
+                            rhs_scale=planes[:, S + left : S + right],
+                            start=True,
+                            stop=True,
+                        )
 
         def exponents(f):
             u, first, count = fills[f]
-            c, a = units[u]
+            lo, width, a = UNITS[u]
             if first == 0:
-                z[u] = ring.tile([P, CHUNKS[c] // LINE, PACK, LINE], F32, name="z")
-            if c < WIDE:
-                nc.vector.scalar_tensor_tensor(
-                    z[u][:, :, first, :],
-                    banks[f][:].rearrange("p (c i) -> p c i", i=LINE),
-                    bias[:, a, first : first + 1],
-                    hz_t[:, starts[c] : starts[c] + CHUNKS[c]].rearrange("p (c i) -> p c i", i=LINE),
-                    ALU.add,
-                    ALU.subtract,
-                )
+                if u < 0:
+                    z[u] = keep.tile([P, width // LINE, PACK, LINE], F32, name=f"z{u}", align_bytes=64)
+                else:
+                    z[u] = ring.tile([P, width // LINE, PACK, LINE], F32, name="z")
+            if lo < SHIFT_FROM:
+                for t in range(first, first + count):
+                    nc.vector.scalar_tensor_tensor(
+                        z[u][:, :, t, :],
+                        banks[f][:, (t - first) * width : (t - first + 1) * width].rearrange("p (c i) -> p c i", i=LINE),
+                        bias[:, a, t : t + 1],
+                        hz_t[:, lo : lo + width].rearrange("p (c i) -> p c i", i=LINE),
+                        ALU.add,
+                        ALU.subtract,
+                    )
             else:
-                lo = starts[c] - starts[WIDE]
                 nc.vector.tensor_tensor(
                     z[u][:, :, first : first + count, :].rearrange("p c t i -> p t c i"),
                     banks[f][:].rearrange("p (t c i) -> p t c i", t=count, i=LINE),
-                    shift[:, a, first : first + count, lo : lo + CHUNKS[c]].rearrange("p t (c i) -> p t c i", i=LINE),
+                    shift[:, a, first : first + count, lo - SHIFT_FROM : lo - SHIFT_FROM + width].rearrange("p t (c i) -> p t c i", i=LINE),
                     ALU.add,
                 )
 
         def kernel_values(u):
-            h_bf[u] = keep.tile([P, CHUNKS[units[u][0]] * PACK], BF16, name=f"h_bf{u}", align_bytes=64)
+            h_bf[u] = keep.tile([P, UNITS[u][1] * PACK], BF16, name=f"h_bf{u}", align_bytes=64)
             nc.scalar.activation(h_bf[u][:].rearrange("p (c i t) -> p c t i", i=LINE, t=PACK), z[u][:], ACT.Exp)
 
         def quantize_h(u):
-            width = CHUNKS[units[u][0]]
+            width = UNITS[u][1]
             hq[u] = keep.tile([P, width], U32, name=f"hq{u}", align_bytes=64)
             hqs[u] = keep.tile([P, width], U8, name=f"hqs{u}", align_bytes=64)
             nc.vector.quantize_mx(out=hq[u][:].bitcast(FP8X4), scales=hqs[u][:], in_=h_bf[u][:])
 
-        def tiles_per_bank(c):
-            return 2 if WIDE <= c < LAST else 1
+        chunk_of = [max(c for c in range(len(CHUNKS)) if CHUNKS[c][0] <= lo) for lo, width, a in UNITS]
+        first_unit = [chunk_of.index(c) for c in range(len(CHUNKS))]
+        last_unit = [max(u for u in range(len(UNITS)) if chunk_of[u] == c) for c in range(len(CHUNKS))]
 
         def products_y(u):
-            c, a = units[u]
-            width = CHUNKS[c]
-            share = tiles_per_bank(c)
+            lo, width, a = UNITS[u]
+            c = chunk_of[u]
+            c_lo, c_width, share = CHUNKS[c]
             for nt in range(N_TILES):
                 place = nt % share
-                if a == 0 and c == LAST and nt < 2:
-                    acc[c, nt] = psum_a.tile([P, BANK], F32, name="bank_a")
-                elif a == 0 and place == 0:
-                    acc[c, nt // share] = psum_y.tile([P, BANK], F32, name="bank_y")
-                target = acc[c, nt // share][:, place * width : (place + 1) * width]
+                if u == first_unit[c] and place == 0:
+                    if c == len(CHUNKS) - 1 and nt < 2:
+                        acc[c, nt // share] = psum_a.tile([P, BANK], F32, name="bank_a")
+                    else:
+                        acc[c, nt // share] = psum_y.tile([P, BANK], F32, name="bank_y")
+                target = acc[c, nt // share][:, place * c_width + lo - c_lo : place * c_width + lo - c_lo + width]
                 nc.tensor.matmul_mx(
                     out=target,
                     lhsT=w4w[:, a, 2 * nt * P : 2 * (nt + 1) * P].bitcast(FP4X4),
                     lhsT_scale=w4s[:, a, nt * P : (nt + 1) * P],
                     rhs=hq[u][:].bitcast(FP8X4),
                     rhs_scale=hqs[u][:],
-                    start=(a == 0 and place == 0),
+                    start=(u == first_unit[c] and place == 0),
                     stop=False,
                 )
                 nc.tensor.matmul_mx(
@@ -239,17 +253,16 @@ def tile_list_gp_inducing_mean_kernel(
                     rhs=hq[u][:].bitcast(FP8X4),
                     rhs_scale=hqs[u][:],
                     start=False,
-                    stop=(a == PASSES - 1 and place == share - 1),
+                    stop=(u == last_unit[c] and place == share - 1),
                 )
 
         def finish(c):
-            width = CHUNKS[c]
-            share = tiles_per_bank(c)
+            lo, width, share = CHUNKS[c]
             for k in range(N_TILES // share):
                 first = k * share
                 bank = acc[c, k][:, 0 : share * width].rearrange("p (s j) -> p s j", s=share)
                 res = keep.tile([P, share, width], F32, name=f"res{c}_{first}")
-                if c > 0 and k % 2 == (0 if c < WIDE else 1):
+                if c > 0 and k % 2 == (0 if c < 2 else 1):
                     nc.vector.tensor_tensor(
                         res[:], bank, b_t[:, first : first + share].unsqueeze(2).to_broadcast([P, share, width]), ALU.add
                     )
@@ -257,36 +270,44 @@ def tile_list_gp_inducing_mean_kernel(
                     for s in range(share):
                         nc.scalar.activation(res[:, s, :], bank[:, s, :], ACT.Identity, bias=b_t[:, first + s : first + s + 1])
                 nc.sync.dma_start(
-                    out[first * P : (first + share) * P, starts[c] : starts[c] + width].rearrange("(s p) j -> p s j", p=P),
+                    out[first * P : (first + share) * P, lo : lo + width].rearrange("(s p) j -> p s j", p=P),
                     res[:],
                 )
 
         nc.vector.tensor_copy(vw[:].rearrange("p a (t m) -> p a m t", t=PACK), tabw[:].bitcast(U32).indirect(idx[:]))
-        for g in range(WIDE):
-            gather_v2_words(g, f"v2w{g}")
-        round_w(0)
+
+        for g in range(len(GATHERS)):
+            if GATHERS[g][2] is None:
+                gather_v2_words(g, f"v2w{g}")
         for f in range(A_BANKS):
             products_a(f)
 
-        for u in range(len(units) + 2):
+        for u in range(len(UNITS) + 2):
             if u == 1:
                 quantize_w(0)
+            if u == 3:
+                quantize_w(1)
             if u >= 2:
                 products_y(u - 2)
+
             for f in range(len(fills)):
                 if fills[f][0] == u:
                     exponents(f)
-                    if f + A_BANKS < len(fills):
+                    if f + A_BANKS < len(fills) and fills[f + A_BANKS][0] not in HELD.get(u, ()):
                         products_a(f + A_BANKS)
-            if u < len(units):
+            if u < len(UNITS):
                 kernel_values(u)
-            if 1 <= u <= len(units):
+            if 1 <= u <= len(UNITS):
                 quantize_h(u - 1)
-            if u >= 2 and units[u - 2][1] == PASSES - 1:
-                finish(units[u - 2][0])
+                for g in range(len(GATHERS)):
+                    if GATHERS[g][2] == u - 1:
+                        gather_v2_words(g, f"h_bf{u - 1}")
+            for f in range(len(fills)):
+                if fills[f][0] == u and f + A_BANKS < len(fills) and fills[f + A_BANKS][0] in HELD.get(u, ()):
+                    products_a(f + A_BANKS)
+            if u >= 2 and u - 2 in last_unit:
+                finish(chunk_of[u - 2])
             if u == 0:
-                round_w(1)
+                round_w(1, 0, 2)
             if u == 2:
-                quantize_w(1)
-            if WIDE <= u < len(GATHERS):
-                gather_v2_words(u, f"h_bf{u - 1}")
+                round_w(1, 2, N_TILES - 2)

@@ -134,8 +134,7 @@ def tile_list_gp_inducing_mean_kernel(
         vw = keep.tile([P, PASSES, PASS], U32, name="vw", align_bytes=64)
         wq = [keep.tile([P, N], U32, name=f"wq{a}", align_bytes=64) for a in range(PASSES)]
         wqs = [keep.tile([P, N], U8, name=f"wqs{a}", align_bytes=64) for a in range(PASSES)]
-        w_bf = [keep.tile([P, N * PACK], BF16, name=f"w_bf{a}", align_bytes=64) for a in range(PASSES)]
-        v2w = {}
+        w_bf, v2w = {}, {}
 
         def gather_v2_words(g, tag):
             lo, width, after = GATHERS[g]
@@ -143,19 +142,18 @@ def tile_list_gp_inducing_mean_kernel(
             entries = idx2[:, lo // LIST_ROWS : (lo + width) // LIST_ROWS]
             nc.vector.tensor_copy(v2w[g][:], tab2w[:].bitcast(U32).indirect(entries))
 
-        def round_w(a, first, count):
-            columns = slice(first * P, (first + count) * P)
-            rounded = w_bf[a][:, first * PASS : (first + count) * PASS].rearrange("p (c i t) -> p c t i", i=LINE, t=PACK)
-            rows = w_raw[a][:, :, columns].rearrange("p t (c i) -> p c t i", i=LINE)
-            if a == 1 and first > 0:
-                nc.vector.tensor_copy(rounded, rows)
-            else:
-                nc.scalar.activation(rounded, rows, ACT.Copy)
+        def round_w(a, tag):
+            w_bf[a] = keep.tile([P, N * PACK], BF16, name=tag, align_bytes=64)
+            nc.scalar.activation(
+                w_bf[a][:].rearrange("p (c i t) -> p c t i", i=LINE, t=PACK),
+                w_raw[a].rearrange("p t (c i) -> p c t i", i=LINE),
+                ACT.Copy,
+            )
 
         def quantize_w(a):
             nc.vector.quantize_mx(out=wq[a][:].bitcast(FP8X4), scales=wqs[a][:], in_=w_bf[a][:])
 
-        round_w(0, 0, N_TILES)
+        round_w(0, "w_bf0")
         shift = keep.tile([P, PASSES, PACK, S2 - SHIFT_FROM], F32, name="shift")
         for a in range(PASSES):
             for t in range(PACK):
@@ -308,6 +306,4 @@ def tile_list_gp_inducing_mean_kernel(
             if u >= 2 and u - 2 in last_unit:
                 finish(chunk_of[u - 2])
             if u == 0:
-                round_w(1, 0, 2)
-            if u == 2:
-                round_w(1, 2, N_TILES - 2)
+                round_w(1, "w_bf1")

@@ -50,18 +50,18 @@ def tile_list_gp_inducing_mean_kernel(
 
         idx = keep.tile([P, S // LIST_ROWS], U16, name="idx")
         idx2 = keep.tile([P, S2 // LIST_ROWS], U16, name="idx2")
-        tabw = keep.tile([P, T], I32, name="tabw", align_bytes=64)
-        tabs = keep.tile([P, T], U8, name="tabs", align_bytes=64)
-        tab2w = keep.tile([P, T2], I32, name="tab2w", align_bytes=64)
-        tab2s = late.tile([P, T2], U8, name="tab2s", align_bytes=64, offset=0)
-        w4s = late.tile([P, PASSES, N], U8, name="w4s", align_bytes=64, offset=0)
-        w4w = late.tile([P, PASSES, 2 * N], U8, name="w4w", align_bytes=64, offset=PASSES * N)
-        b_t = late.tile([P, N_TILES], F32, name="b_t", align_bytes=64, offset=3 * PASSES * N)
-        w_both = late.tile([P, PASSES * PACK * N], F32, name="w_both", align_bytes=64, offset=3 * PASSES * N + 64)
+        tabw = keep.tile([P, T], I32, name="tabw", align_bytes=256)
+        tabs = keep.tile([P, T], U8, name="tabs", align_bytes=256)
+        tab2w = keep.tile([P, T2], I32, name="tab2w", align_bytes=256)
+        tab2s = late.tile([P, T2], U8, name="tab2s", align_bytes=256, offset=0)
+        w4s = late.tile([P, PASSES, N], U8, name="w4s", align_bytes=256, offset=0)
+        w4w = late.tile([P, PASSES, 2 * N], U8, name="w4w", align_bytes=256, offset=PASSES * N)
+        b_t = late.tile([P, N_TILES], F32, name="b_t", align_bytes=256, offset=3 * PASSES * N)
+        w_both = late.tile([P, PASSES * PACK * N], F32, name="w_both", align_bytes=256, offset=3 * PASSES * N + 256)
         w_raw = [w_both[:, a * PACK * N : (a + 1) * PACK * N].rearrange("p (t n) -> p t n", t=PACK) for a in range(PASSES)]
-        picked = keep.tile([P, S + S2], U8, name="picked", align_bytes=64)
-        planes = keep.tile([P, S + S2], U8, name="planes", align_bytes=64)
-        hx_t = keep.tile([P, PASSES, PACK], F32, name="hx_t", align_bytes=64)
+        picked = keep.tile([P, S + S2], U8, name="picked", align_bytes=256)
+        planes = keep.tile([P, S + S2], U8, name="planes", align_bytes=256)
+        hx_t = keep.tile([P, PASSES, PACK], F32, name="hx_t", align_bytes=256)
         pw_t = keep.tile([P, PASSES, PACK], F32, name="pw_t")
         hz_col = keep.tile([P, S2 // P], F32, name="hz_col")
         hz_t = keep.tile([P, S2], F32, name="hz_t")
@@ -131,19 +131,19 @@ def tile_list_gp_inducing_mean_kernel(
                 slab = a * PACK + t
                 nc.scalar.activation(terms_out[:, slab, :], terms[:, :, slab], ACT.Identity, accum_out=bias[:, a, t : t + 1])
 
-        vw = keep.tile([P, PASSES, PASS], U32, name="vw", align_bytes=64)
-        wq = [keep.tile([P, N], U32, name=f"wq{a}", align_bytes=64) for a in range(PASSES)]
-        wqs = [keep.tile([P, N], U8, name=f"wqs{a}", align_bytes=64) for a in range(PASSES)]
+        vw = keep.tile([P, PASSES, PASS], U32, name="vw", align_bytes=256)
+        wq = [keep.tile([P, N], U32, name=f"wq{a}", align_bytes=256) for a in range(PASSES)]
+        wqs = [keep.tile([P, N], U8, name=f"wqs{a}", align_bytes=256) for a in range(PASSES)]
         w_bf, v2w = {}, {}
 
         def gather_v2_words(g, tag):
             lo, width, after = GATHERS[g]
-            v2w[g] = keep.tile([P, width], U32, name=tag, align_bytes=64)
+            v2w[g] = keep.tile([P, width], U32, name=tag, align_bytes=256)
             entries = idx2[:, lo // LIST_ROWS : (lo + width) // LIST_ROWS]
             nc.vector.tensor_copy(v2w[g][:], tab2w[:].bitcast(U32).indirect(entries))
 
         def round_w(a, tag):
-            w_bf[a] = keep.tile([P, N * PACK], BF16, name=tag, align_bytes=64)
+            w_bf[a] = keep.tile([P, N * PACK], BF16, name=tag, align_bytes=256)
             nc.scalar.activation(
                 w_bf[a][:].rearrange("p (c i t) -> p c t i", i=LINE, t=PACK),
                 w_raw[a].rearrange("p t (c i) -> p c t i", i=LINE),
@@ -188,7 +188,7 @@ def tile_list_gp_inducing_mean_kernel(
             lo, width, a = UNITS[u]
             if first == 0:
                 if u < 0:
-                    z[u] = keep.tile([P, width // LINE, PACK, LINE], F32, name=f"z{u}", align_bytes=64)
+                    z[u] = keep.tile([P, width // LINE, PACK, LINE], F32, name=f"z{u}", align_bytes=256)
                 else:
                     z[u] = ring.tile([P, width // LINE, PACK, LINE], F32, name="z")
             if lo < SHIFT_FROM:
@@ -210,13 +210,13 @@ def tile_list_gp_inducing_mean_kernel(
                 )
 
         def kernel_values(u):
-            h_bf[u] = keep.tile([P, UNITS[u][1] * PACK], BF16, name=f"h_bf{u}", align_bytes=64)
+            h_bf[u] = keep.tile([P, UNITS[u][1] * PACK], BF16, name=f"h_bf{u}", align_bytes=256)
             nc.scalar.activation(h_bf[u][:].rearrange("p (c i t) -> p c t i", i=LINE, t=PACK), z[u][:], ACT.Exp)
 
         def quantize_h(u):
             width = UNITS[u][1]
-            hq[u] = keep.tile([P, width], U32, name=f"hq{u}", align_bytes=64)
-            hqs[u] = keep.tile([P, width], U8, name=f"hqs{u}", align_bytes=64)
+            hq[u] = keep.tile([P, width], U32, name=f"hq{u}", align_bytes=256)
+            hqs[u] = keep.tile([P, width], U8, name=f"hqs{u}", align_bytes=256)
             nc.vector.quantize_mx(out=hq[u][:].bitcast(FP8X4), scales=hqs[u][:], in_=h_bf[u][:])
 
         chunk_of = [max(c for c in range(len(CHUNKS)) if CHUNKS[c][0] <= lo) for lo, width, a in UNITS]
@@ -259,7 +259,7 @@ def tile_list_gp_inducing_mean_kernel(
             for k in range(N_TILES // share):
                 first = k * share
                 bank = acc[c, k][:, 0 : share * width].rearrange("p (s j) -> p s j", s=share)
-                res = keep.tile([P, share, width], F32, name=f"res{c}_{first}")
+                res = keep.tile([P, share, width], F32, name=f"res{c}_{first}", align_bytes=256)
                 if c > 0 and k % 2 == (0 if c < 2 else 1):
                     nc.vector.tensor_tensor(
                         res[:], bank, b_t[:, first : first + share].unsqueeze(2).to_broadcast([P, share, width]), ALU.add

@@ -48,8 +48,8 @@ def tile_list_gp_inducing_mean_kernel(
         psum_a = ctx.enter_context(tc.psum_pool(name="psum_a", bufs=A_BANKS))
         psum_y = ctx.enter_context(tc.psum_pool(name="psum_y", bufs=8 - A_BANKS))
 
-        idx = keep.tile([P, S // LIST_ROWS], U16, name="idx")
-        idx2 = keep.tile([P, S2 // LIST_ROWS], U16, name="idx2")
+        idx = keep.tile([P, S // LIST_ROWS], U16, name="idx", align_bytes=256)
+        idx2 = keep.tile([P, S2 // LIST_ROWS], U16, name="idx2", align_bytes=256)
         tabw = keep.tile([P, T], I32, name="tabw", align_bytes=256)
         tabs = keep.tile([P, T], U8, name="tabs", align_bytes=256)
         tab2w = keep.tile([P, T2], I32, name="tab2w", align_bytes=256)
@@ -62,10 +62,10 @@ def tile_list_gp_inducing_mean_kernel(
         picked = keep.tile([P, S + S2], U8, name="picked", align_bytes=256)
         planes = keep.tile([P, S + S2], U8, name="planes", align_bytes=256)
         hx_t = keep.tile([P, PASSES, PACK], F32, name="hx_t", align_bytes=256)
-        pw_t = keep.tile([P, PASSES, PACK], F32, name="pw_t")
-        hz_col = keep.tile([P, S2 // P], F32, name="hz_col")
-        hz_t = keep.tile([P, S2], F32, name="hz_t")
-        ident = keep.tile([P, P], F32, name="ident")
+        pw_t = keep.tile([P, PASSES, PACK], F32, name="pw_t", align_bytes=256)
+        hz_col = keep.tile([P, S2 // P], F32, name="hz_col", align_bytes=256)
+        hz_t = keep.tile([P, S2], F32, name="hz_t", align_bytes=256)
+        ident = keep.tile([P, P], F32, name="ident", align_bytes=256)
 
         nc.vector.memset(tabs[0:TABLE_ROW, :].bitcast(I32), 0)
         nc.vector.memset(tab2s[0:TABLE_ROW, :].bitcast(I32), 0)
@@ -86,7 +86,7 @@ def tile_list_gp_inducing_mean_kernel(
 
         nc.sync.dma_start(tab2w[:], tab2_words[0].rearrange("p t i -> p (t i)").bitcast(I32))
 
-        factors = keep.tile([P, 3, PASSES, PACK], F32, name="factors")
+        factors = keep.tile([P, 3, PASSES, PACK], F32, name="factors", align_bytes=256)
         nc.vector.tensor_scalar(factors[:, 0], pw_t[:], LN_LOW, LN_HIGH, ALU.max, ALU.min)
         nc.vector.tensor_scalar(factors[:, 1], pw_t[:], LN_HIGH, LN_LOW, ALU.max, ALU.mult)
         nc.vector.tensor_scalar(factors[:, 2], pw_t[:], LN_LOW, LN_HIGH, ALU.min, ALU.mult)
@@ -119,9 +119,9 @@ def tile_list_gp_inducing_mean_kernel(
                 spread[:].rearrange("p (c m) -> p m c", c=LINE),
             )
 
-        terms = keep.tile([P, 4, PASSES * PACK], F32, name="terms")
-        terms_out = keep.tile([P, PASSES * PACK, 4], F32, name="terms_out")
-        bias = keep.tile([P, PASSES, PACK], F32, name="bias")
+        terms = keep.tile([P, 4, PASSES * PACK], F32, name="terms", align_bytes=256)
+        terms_out = keep.tile([P, PASSES * PACK, 4], F32, name="terms_out", align_bytes=256)
+        bias = keep.tile([P, PASSES, PACK], F32, name="bias", align_bytes=256)
         nc.scalar.activation(terms[:, 0:3, :], factors[:].rearrange("p f a t -> p f (a t)"), ACT.Ln)
         warm = keep.tile([P, 1], F32, name="warm")
         nc.scalar.activation(warm[:], terms[:, 0, 0:1], ACT.Exp)
@@ -154,7 +154,7 @@ def tile_list_gp_inducing_mean_kernel(
             nc.vector.quantize_mx(out=wq[a][:].bitcast(FP8X4), scales=wqs[a][:], in_=w_bf[a][:])
 
         round_w(0, "w_bf0")
-        shift = keep.tile([P, PASSES, PACK, S2 - SHIFT_FROM], F32, name="shift")
+        shift = keep.tile([P, PASSES, PACK, S2 - SHIFT_FROM], F32, name="shift", align_bytes=256)
         for a in range(PASSES):
             for t in range(PACK):
                 nc.scalar.activation(
@@ -190,7 +190,7 @@ def tile_list_gp_inducing_mean_kernel(
                 if u < 0:
                     z[u] = keep.tile([P, width // LINE, PACK, LINE], F32, name=f"z{u}", align_bytes=256)
                 else:
-                    z[u] = ring.tile([P, width // LINE, PACK, LINE], F32, name="z")
+                    z[u] = ring.tile([P, width // LINE, PACK, LINE], F32, name="z", align_bytes=256)
             if lo < SHIFT_FROM:
                 for t in range(first, first + count):
                     nc.vector.scalar_tensor_tensor(

@@ -54,11 +54,11 @@ def tile_list_gp_inducing_mean_kernel(
         tabs = keep.tile([P, T], U8, name="tabs", align_bytes=256)
         tab2w = keep.tile([P, T2], I32, name="tab2w", align_bytes=256)
         tab2s = late.tile([P, T2], U8, name="tab2s", align_bytes=256, offset=0)
-        w4s = late.tile([P, PASSES, N], U8, name="w4s", align_bytes=256, offset=0)
-        w4w = late.tile([P, PASSES, 2 * N], U8, name="w4w", align_bytes=256, offset=PASSES * N)
-        b_t = late.tile([P, N_TILES], F32, name="b_t", align_bytes=256, offset=3 * PASSES * N)
-        w_both = late.tile([P, PASSES * PACK * N], F32, name="w_both", align_bytes=256, offset=3 * PASSES * N + 256)
+        w4w = late.tile([P, PASSES, 2 * N], U8, name="w4w", align_bytes=256, offset=0)
+        b_t = late.tile([P, N_TILES], F32, name="b_t", align_bytes=256, offset=2 * PASSES * N)
+        w_both = late.tile([P, PASSES * PACK * N], F32, name="w_both", align_bytes=256, offset=2 * PASSES * N + 256)
         w_raw = [w_both[:, a * PACK * N : (a + 1) * PACK * N].rearrange("p (t n) -> p t n", t=PACK) for a in range(PASSES)]
+        w4s = keep.tile([P, PASSES, N], U8, name="w4s", align_bytes=256)
         picked = keep.tile([P, S + S2], U8, name="picked", align_bytes=256)
         planes = keep.tile([P, S + S2], U8, name="planes", align_bytes=256)
         hx_t = keep.tile([P, PASSES, PACK], F32, name="hx_t", align_bytes=256)
@@ -70,6 +70,7 @@ def tile_list_gp_inducing_mean_kernel(
         nc.vector.memset(tabs[0:TABLE_ROW, :].bitcast(I32), 0)
         nc.vector.memset(tab2s[0:TABLE_ROW, :].bitcast(I32), 0)
         make_identity(nc, ident[:])
+        nc.vector.memset(w4s[:].bitcast(I32), 0)
         nc.vector.memset(planes[:].bitcast(I32), 0)
 
         def load_w(a):
@@ -83,6 +84,11 @@ def tile_list_gp_inducing_mean_kernel(
         nc.sync.dma_start(tab2s[TABLE_ROW:P, :].bitcast(I32), tab2_scales[0].bitcast(I32))
         nc.sync.dma_start(tabw[:], tab_words[0].rearrange("p t i -> p (t i)").bitcast(I32))
         nc.sync.dma_start(hx_t[:], hx.rearrange("(a p t) -> p a t", a=PASSES, t=PACK))
+        for r in range(SCALE_ROWS):
+            nc.sync.dma_start(
+                w4s[r:P:32, :, :].bitcast(I32),
+                w4_scales[:, r : 4 * SCALE_ROWS : SCALE_ROWS, :].rearrange("a q c -> q a c").bitcast(I32),
+            )
 
         nc.sync.dma_start(tab2w[:], tab2_words[0].rearrange("p t i -> p (t i)").bitcast(I32))
 
@@ -96,16 +102,9 @@ def tile_list_gp_inducing_mean_kernel(
         for r in range(SCALE_ROWS):
             nc.sync.dma_start(planes[r:P:32, :].bitcast(I32), picked[TABLE_ROW + r : P : SCALE_ROWS, :].bitcast(I32))
 
-        nc.gpsimd.memset(w4s[:].bitcast(I32), 0)
-
         load_w(0)
         load_w(1)
         nc.sync.dma_start(w4w[:].bitcast(I32), w4_words.rearrange("a p c -> p a c").bitcast(I32))
-        for r in range(SCALE_ROWS):
-            nc.sync.dma_start(
-                w4s[r:P:32, :, :].bitcast(I32),
-                w4_scales[:, r : 4 * SCALE_ROWS : SCALE_ROWS, :].rearrange("a q c -> q a c").bitcast(I32),
-            )
         with nc.allow_non_contiguous_dma(reason="one bias value a partition"):
             nc.sync.dma_start(b_t[:], b.rearrange("(c p) -> p c", p=P))
 

@@ -27,13 +27,13 @@ A_BANKS = 4
 LINE = 4
 LIST_ROWS = 16
 SCALE_ROWS = 4
-SPREAD = 8
 TABLE_ROW = P - 4 * SCALE_ROWS
 CHUNKS = [(0, 512, 1), (512, 512, 1), (1024, 256, 2), (1280, 128, 2), (1408, 128, 1)]
-UNITS = [(0, 512, 0), (0, 512, 1), (512, 512, 0), (512, 512, 1), (1024, 256, 0), (1024, 256, 1), (1280, 128, 0), (1280, 128, 1), (1408, 128, 0), (1408, 128, 1)]
+UNITS = [(lo, width, a) for lo, width, share in CHUNKS for a in range(PASSES)]
+HALVED = ()
+W_PIECES = [(0, 0, 256), (0, 256, 512), (1, 0, 512)]
 GATHERS = [(0, 512, None), (512, 512, None), (1024, 256, 1), (1280, 256, 2)]
 SHIFT_FROM = 1024
-HELD = {}
 LN_LOW, LN_HIGH = 2.0**-64, 2.0**64
 
 
@@ -57,7 +57,10 @@ def tile_list_gp_inducing_mean_kernel(
         w4w = late.tile([P, PASSES, 2 * N], U8, name="w4w", align_bytes=256, offset=0)
         b_t = late.tile([P, N_TILES], F32, name="b_t", align_bytes=256, offset=2 * PASSES * N)
         w_both = late.tile([P, PASSES * PACK * N], F32, name="w_both", align_bytes=256, offset=2 * PASSES * N + 256)
-        w_raw = [w_both[:, a * PACK * N : (a + 1) * PACK * N].rearrange("p (t n) -> p t n", t=PACK) for a in range(PASSES)]
+        w_raw = [
+            w_both[:, PACK * (a * N + lo) : PACK * (a * N + hi)].rearrange("p (t n) -> p t n", t=PACK)
+            for a, lo, hi in W_PIECES
+        ]
         w4s = keep.tile([P, PASSES, N], U8, name="w4s", align_bytes=256)
         picked = keep.tile([P, S + S2], U8, name="picked", align_bytes=256)
         planes = keep.tile([P, S + S2], U8, name="planes", align_bytes=256)
@@ -73,8 +76,9 @@ def tile_list_gp_inducing_mean_kernel(
         nc.vector.memset(w4s[:].bitcast(I32), 0)
         nc.vector.memset(planes[:].bitcast(I32), 0)
 
-        def load_w(a):
-            nc.sync.dma_start(w_raw[a], w[a * PASS : (a + 1) * PASS, :].rearrange("(p t) n -> p t n", t=PACK))
+        def load_w(k):
+            a, lo, hi = W_PIECES[k]
+            nc.sync.dma_start(w_raw[k], w[a * PASS : (a + 1) * PASS, lo:hi].rearrange("(p t) n -> p t n", t=PACK))
 
         nc.scalar.dma_start(pw_t[:], pw.rearrange("(a p t) -> p a t", a=PASSES, t=PACK))
         nc.scalar.dma_start(hz_col[:], hz.rearrange("(p c) -> p c", p=P))
@@ -102,8 +106,8 @@ def tile_list_gp_inducing_mean_kernel(
         for r in range(SCALE_ROWS):
             nc.sync.dma_start(planes[r:P:32, :].bitcast(I32), picked[TABLE_ROW + r : P : SCALE_ROWS, :].bitcast(I32))
 
-        load_w(0)
-        load_w(1)
+        for k in range(len(W_PIECES)):
+            load_w(k)
         nc.sync.dma_start(w4w[:].bitcast(I32), w4_words.rearrange("a p c -> p a c").bitcast(I32))
         with nc.allow_non_contiguous_dma(reason="one bias value a partition"):
             nc.sync.dma_start(b_t[:], b.rearrange("(c p) -> p c", p=P))
@@ -133,7 +137,8 @@ def tile_list_gp_inducing_mean_kernel(
         vw = keep.tile([P, PASSES, PASS], U32, name="vw", align_bytes=256)
         wq = [keep.tile([P, N], U32, name=f"wq{a}", align_bytes=256) for a in range(PASSES)]
         wqs = [keep.tile([P, N], U8, name=f"wqs{a}", align_bytes=256) for a in range(PASSES)]
-        w_bf, v2w = {}, {}
+        w_bf = [keep.tile([P, N * PACK], BF16, name=f"w_bf{a}", align_bytes=256) for a in range(PASSES)]
+        v2w = {}
 
         def gather_v2_words(g, tag):
             lo, width, after = GATHERS[g]
@@ -141,18 +146,19 @@ def tile_list_gp_inducing_mean_kernel(
             entries = idx2[:, lo // LIST_ROWS : (lo + width) // LIST_ROWS]
             nc.vector.tensor_copy(v2w[g][:], tab2w[:].bitcast(U32).indirect(entries))
 
-        def round_w(a, tag):
-            w_bf[a] = keep.tile([P, N * PACK], BF16, name=tag, align_bytes=256)
+        def round_w(k):
+            a, lo, hi = W_PIECES[k]
             nc.scalar.activation(
-                w_bf[a][:].rearrange("p (c i t) -> p c t i", i=LINE, t=PACK),
-                w_raw[a].rearrange("p t (c i) -> p c t i", i=LINE),
+                w_bf[a][:, PACK * lo : PACK * hi].rearrange("p (c i t) -> p c t i", i=LINE, t=PACK),
+                w_raw[k].rearrange("p t (c i) -> p c t i", i=LINE),
                 ACT.Copy,
             )
 
         def quantize_w(a):
             nc.vector.quantize_mx(out=wq[a][:].bitcast(FP8X4), scales=wqs[a][:], in_=w_bf[a][:])
 
-        round_w(0, "w_bf0")
+        round_w(0)
+        round_w(1)
         shift = keep.tile([P, PASSES, PACK, S2 - SHIFT_FROM], F32, name="shift", align_bytes=256)
         for a in range(PASSES):
             for t in range(PACK):
@@ -167,29 +173,23 @@ def tile_list_gp_inducing_mean_kernel(
             u, first, count = fills[f]
             lo, width, a = UNITS[u]
             banks[f] = psum_a.tile([P, BANK], F32, name="bank_a")
+            g = max(g for g in range(len(GATHERS)) if GATHERS[g][0] <= lo)
             for t in range(first, first + count):
-                for g, (g_lo, g_width, after) in enumerate(GATHERS):
-                    left, right = max(lo, g_lo), min(lo + width, g_lo + g_width)
-                    if left < right:
-                        place = (t - first) * width + left - lo
-                        nc.tensor.matmul_mx(
-                            out=banks[f][:, place : place + right - left],
-                            lhsT=vw[:, a, t * P : (t + 1) * P].bitcast(FP8X4),
-                            lhsT_scale=planes[:, a * PASS + t * P : a * PASS + (t + 1) * P],
-                            rhs=v2w[g][:, left - g_lo : right - g_lo].bitcast(FP8X4),
-                            rhs_scale=planes[:, S + left : S + right],
-                            start=True,
-                            stop=True,
-                        )
+                nc.tensor.matmul_mx(
+                    out=banks[f][:, (t - first) * width : (t - first + 1) * width],
+                    lhsT=vw[:, a, t * P : (t + 1) * P].bitcast(FP8X4),
+                    lhsT_scale=planes[:, a * PASS + t * P : a * PASS + (t + 1) * P],
+                    rhs=v2w[g][:, lo - GATHERS[g][0] : lo - GATHERS[g][0] + width].bitcast(FP8X4),
+                    rhs_scale=planes[:, S + lo : S + lo + width],
+                    start=True,
+                    stop=True,
+                )
 
         def exponents(f):
             u, first, count = fills[f]
             lo, width, a = UNITS[u]
             if first == 0:
-                if u < 0:
-                    z[u] = keep.tile([P, width // LINE, PACK, LINE], F32, name=f"z{u}", align_bytes=256)
-                else:
-                    z[u] = ring.tile([P, width // LINE, PACK, LINE], F32, name="z", align_bytes=256)
+                z[u] = ring.tile([P, width // LINE, PACK, LINE], F32, name="z", align_bytes=256)
             if lo < SHIFT_FROM:
                 for t in range(first, first + count):
                     nc.vector.scalar_tensor_tensor(
@@ -208,50 +208,58 @@ def tile_list_gp_inducing_mean_kernel(
                     ALU.add,
                 )
 
+        parts = [2 if u in HALVED else 1 for u in range(len(UNITS))]
+
         def kernel_values(u):
-            h_bf[u] = keep.tile([P, UNITS[u][1] * PACK], BF16, name=f"h_bf{u}", align_bytes=256)
-            nc.scalar.activation(h_bf[u][:].rearrange("p (c i t) -> p c t i", i=LINE, t=PACK), z[u][:], ACT.Exp)
+            width = UNITS[u][1] // parts[u]
+            for part in range(parts[u]):
+                h_bf[u, part] = keep.tile([P, width * PACK], BF16, name=f"h_bf{u}_{part}", align_bytes=256)
+                nc.scalar.activation(
+                    h_bf[u, part][:].rearrange("p (c i t) -> p c t i", i=LINE, t=PACK),
+                    z[u][:, part * width // LINE : (part + 1) * width // LINE],
+                    ACT.Exp,
+                )
 
         def quantize_h(u):
-            width = UNITS[u][1]
-            hq[u] = keep.tile([P, width], U32, name=f"hq{u}", align_bytes=256)
-            hqs[u] = keep.tile([P, width], U8, name=f"hqs{u}", align_bytes=256)
-            nc.vector.quantize_mx(out=hq[u][:].bitcast(FP8X4), scales=hqs[u][:], in_=h_bf[u][:])
-
-        chunk_of = [max(c for c in range(len(CHUNKS)) if CHUNKS[c][0] <= lo) for lo, width, a in UNITS]
-        first_unit = [chunk_of.index(c) for c in range(len(CHUNKS))]
-        last_unit = [max(u for u in range(len(UNITS)) if chunk_of[u] == c) for c in range(len(CHUNKS))]
+            width = UNITS[u][1] // parts[u]
+            for part in range(parts[u]):
+                hq[u, part] = keep.tile([P, width], U32, name=f"hq{u}_{part}", align_bytes=256)
+                hqs[u, part] = keep.tile([P, width], U8, name=f"hqs{u}_{part}", align_bytes=256)
+                nc.vector.quantize_mx(out=hq[u, part][:].bitcast(FP8X4), scales=hqs[u, part][:], in_=h_bf[u, part][:])
 
         def products_y(u):
-            lo, width, a = UNITS[u]
-            c = chunk_of[u]
-            c_lo, c_width, share = CHUNKS[c]
-            for nt in range(N_TILES):
-                place = nt % share
-                if u == first_unit[c] and place == 0:
-                    if c == len(CHUNKS) - 1 and nt < 2:
-                        acc[c, nt // share] = psum_a.tile([P, BANK], F32, name="bank_a")
-                    else:
-                        acc[c, nt // share] = psum_y.tile([P, BANK], F32, name="bank_y")
-                target = acc[c, nt // share][:, place * c_width + lo - c_lo : place * c_width + lo - c_lo + width]
-                nc.tensor.matmul_mx(
-                    out=target,
-                    lhsT=w4w[:, a, 2 * nt * P : 2 * (nt + 1) * P].bitcast(FP4X4),
-                    lhsT_scale=w4s[:, a, nt * P : (nt + 1) * P],
-                    rhs=hq[u][:].bitcast(FP8X4),
-                    rhs_scale=hqs[u][:],
-                    start=(u == first_unit[c] and place == 0),
-                    stop=False,
-                )
-                nc.tensor.matmul_mx(
-                    out=target,
-                    lhsT=wq[a][:, nt * P : (nt + 1) * P].bitcast(FP8X4),
-                    lhsT_scale=wqs[a][:, nt * P : (nt + 1) * P],
-                    rhs=hq[u][:].bitcast(FP8X4),
-                    rhs_scale=hqs[u][:],
-                    start=False,
-                    stop=(u == last_unit[c] and place == share - 1),
-                )
+            a = UNITS[u][2]
+            c = u // PASSES
+            c_width, share = CHUNKS[c][1:]
+            width = c_width // parts[u]
+            for part in range(parts[u]):
+                for nt in range(N_TILES):
+                    place = nt % share
+                    if a == 0 and part == 0 and place == 0:
+                        if c == len(CHUNKS) - 1 and nt < 2:
+                            acc[c, nt // share] = psum_a.tile([P, BANK], F32, name="bank_a")
+                        else:
+                            acc[c, nt // share] = psum_y.tile([P, BANK], F32, name="bank_y")
+                    left = place * c_width + part * width
+                    target = acc[c, nt // share][:, left : left + width]
+                    nc.tensor.matmul_mx(
+                        out=target,
+                        lhsT=w4w[:, a, 2 * nt * P : 2 * (nt + 1) * P].bitcast(FP4X4),
+                        lhsT_scale=w4s[:, a, nt * P : (nt + 1) * P],
+                        rhs=hq[u, part][:].bitcast(FP8X4),
+                        rhs_scale=hqs[u, part][:],
+                        start=(a == 0 and part == 0 and place == 0),
+                        stop=False,
+                    )
+                    nc.tensor.matmul_mx(
+                        out=target,
+                        lhsT=wq[a][:, nt * P : (nt + 1) * P].bitcast(FP8X4),
+                        lhsT_scale=wqs[a][:, nt * P : (nt + 1) * P],
+                        rhs=hq[u, part][:].bitcast(FP8X4),
+                        rhs_scale=hqs[u, part][:],
+                        start=False,
+                        stop=(a == PASSES - 1 and part == parts[u] - 1 and place == share - 1),
+                    )
 
         def finish(c):
             lo, width, share = CHUNKS[c]
@@ -272,7 +280,6 @@ def tile_list_gp_inducing_mean_kernel(
                 )
 
         nc.vector.tensor_copy(vw[:].rearrange("p a (t m) -> p a m t", t=PACK), tabw[:].bitcast(U32).indirect(idx[:]))
-
         for g in range(len(GATHERS)):
             if GATHERS[g][2] is None:
                 gather_v2_words(g, f"v2w{g}")
@@ -286,23 +293,20 @@ def tile_list_gp_inducing_mean_kernel(
                 quantize_w(1)
             if u >= 2:
                 products_y(u - 2)
-
             for f in range(len(fills)):
                 if fills[f][0] == u:
                     exponents(f)
-                    if f + A_BANKS < len(fills) and fills[f + A_BANKS][0] not in HELD.get(u, ()):
+                    if f + A_BANKS < len(fills):
                         products_a(f + A_BANKS)
             if u < len(UNITS):
                 kernel_values(u)
             if 1 <= u <= len(UNITS):
                 quantize_h(u - 1)
-                for g in range(len(GATHERS)):
-                    if GATHERS[g][2] == u - 1:
-                        gather_v2_words(g, f"h_bf{u - 1}")
-            for f in range(len(fills)):
-                if fills[f][0] == u and f + A_BANKS < len(fills) and fills[f + A_BANKS][0] in HELD.get(u, ()):
-                    products_a(f + A_BANKS)
-            if u >= 2 and u - 2 in last_unit:
-                finish(chunk_of[u - 2])
+            for g in range(len(GATHERS)):
+                if GATHERS[g][2] == u - 1:
+                    gather_v2_words(g, f"h_bf{u - 1}_0")
+            for c in range(len(CHUNKS)):
+                if u == 2 * c + 3:
+                    finish(c)
             if u == 0:
-                round_w(1, "w_bf1")
+                round_w(2)

@@ -27,11 +27,12 @@ A_BANKS = 4
 LINE = 4
 LIST_ROWS = 16
 SCALE_ROWS = 4
-TABLE_ROW = P - 4 * SCALE_ROWS
+TABLE_ROW, TABLE_STEP = 32, 4
+TABLE_END = TABLE_ROW + TABLE_STEP * 4 * SCALE_ROWS
 CHUNKS = [(0, 512, 1), (512, 512, 1), (1024, 256, 2), (1280, 128, 2), (1408, 128, 1)]
 UNITS = [(lo, width, a) for lo, width, share in CHUNKS for a in range(PASSES)]
 HALVED = ()
-W_PIECES = [(0, 0, 256), (0, 256, 512), (1, 0, 512)]
+W_PIECES = [(0, 0, 256), (0, 256, 512), (1, 0, 256), (1, 256, 512)]
 GATHERS = [(0, 512, None), (512, 512, None), (1024, 256, 1), (1280, 256, 2)]
 SHIFT_FROM = 1024
 LN_LOW, LN_HIGH = 2.0**-64, 2.0**64
@@ -44,6 +45,7 @@ def tile_list_gp_inducing_mean_kernel(
     with ExitStack() as ctx:
         keep = ctx.enter_context(tc.tile_pool(name="keep", bufs=1))
         ring = ctx.enter_context(tc.tile_pool(name="ring", bufs=2))
+        head = ctx.enter_context(tc.tile_pool(name="head", bufs=1))
         late = ctx.enter_context(tc.tile_pool(name="late", bufs=1))
         psum_a = ctx.enter_context(tc.psum_pool(name="psum_a", bufs=A_BANKS))
         psum_y = ctx.enter_context(tc.psum_pool(name="psum_y", bufs=8 - A_BANKS))
@@ -52,7 +54,6 @@ def tile_list_gp_inducing_mean_kernel(
         idx2 = keep.tile([P, S2 // LIST_ROWS], U16, name="idx2", align_bytes=256)
         tabw = keep.tile([P, T], I32, name="tabw", align_bytes=256)
         tabs = keep.tile([P, T], U8, name="tabs", align_bytes=256)
-        tab2w = keep.tile([P, T2], I32, name="tab2w", align_bytes=256)
         tab2s = late.tile([P, T2], U8, name="tab2s", align_bytes=256, offset=0)
         w4w = late.tile([P, PASSES, 2 * N], U8, name="w4w", align_bytes=256, offset=0)
         b_t = late.tile([P, N_TILES], F32, name="b_t", align_bytes=256, offset=2 * PASSES * N)
@@ -65,13 +66,13 @@ def tile_list_gp_inducing_mean_kernel(
         picked = keep.tile([P, S + S2], U8, name="picked", align_bytes=256)
         planes = keep.tile([P, S + S2], U8, name="planes", align_bytes=256)
         hx_t = keep.tile([P, PASSES, PACK], F32, name="hx_t", align_bytes=256)
-        pw_t = keep.tile([P, PASSES, PACK], F32, name="pw_t", align_bytes=256)
-        hz_col = keep.tile([P, S2 // P], F32, name="hz_col", align_bytes=256)
+        pw_t = head.tile([P, PASSES, PACK], F32, name="pw_t", align_bytes=256, offset=0)
+        hz_col = head.tile([P, S2 // P], F32, name="hz_col", align_bytes=256, offset=4 * T2)
         hz_t = keep.tile([P, S2], F32, name="hz_t", align_bytes=256)
         ident = keep.tile([P, P], F32, name="ident", align_bytes=256)
 
-        nc.vector.memset(tabs[0:TABLE_ROW, :].bitcast(I32), 0)
-        nc.vector.memset(tab2s[0:TABLE_ROW, :].bitcast(I32), 0)
+        nc.gpsimd.memset(tabs[:].bitcast(I32), 0)
+        nc.vector.memset(tab2s[:].bitcast(I32), 0)
         make_identity(nc, ident[:])
         nc.vector.memset(w4s[:].bitcast(I32), 0)
         nc.vector.memset(planes[:].bitcast(I32), 0)
@@ -83,9 +84,9 @@ def tile_list_gp_inducing_mean_kernel(
         nc.scalar.dma_start(pw_t[:], pw.rearrange("(a p t) -> p a t", a=PASSES, t=PACK))
         nc.scalar.dma_start(hz_col[:], hz.rearrange("(p c) -> p c", p=P))
         nc.sync.dma_start(idx[:], offs)
-        nc.sync.dma_start(tabs[TABLE_ROW:P, :].bitcast(I32), tab_scales[0].bitcast(I32))
+        nc.sync.dma_start(tabs[TABLE_ROW:TABLE_END:TABLE_STEP, :].bitcast(I32), tab_scales[0].bitcast(I32))
         nc.sync.dma_start(idx2[:], offs2)
-        nc.sync.dma_start(tab2s[TABLE_ROW:P, :].bitcast(I32), tab2_scales[0].bitcast(I32))
+        nc.sync.dma_start(tab2s[TABLE_ROW:TABLE_END:TABLE_STEP, :].bitcast(I32), tab2_scales[0].bitcast(I32))
         nc.sync.dma_start(tabw[:], tab_words[0].rearrange("p t i -> p (t i)").bitcast(I32))
         nc.sync.dma_start(hx_t[:], hx.rearrange("(a p t) -> p a t", a=PASSES, t=PACK))
         for r in range(SCALE_ROWS):
@@ -94,19 +95,24 @@ def tile_list_gp_inducing_mean_kernel(
                 w4_scales[:, r : 4 * SCALE_ROWS : SCALE_ROWS, :].rearrange("a q c -> q a c").bitcast(I32),
             )
 
-        nc.sync.dma_start(tab2w[:], tab2_words[0].rearrange("p t i -> p (t i)").bitcast(I32))
 
         factors = keep.tile([P, 3, PASSES, PACK], F32, name="factors", align_bytes=256)
         nc.vector.tensor_scalar(factors[:, 0], pw_t[:], LN_LOW, LN_HIGH, ALU.max, ALU.min)
         nc.vector.tensor_scalar(factors[:, 1], pw_t[:], LN_HIGH, LN_LOW, ALU.max, ALU.mult)
         nc.vector.tensor_scalar(factors[:, 2], pw_t[:], LN_LOW, LN_HIGH, ALU.min, ALU.mult)
 
+        tab2w = head.tile([P, T2], I32, name="tab2w", align_bytes=256, offset=0)
+        nc.sync.dma_start(tab2w[:], tab2_words[0].rearrange("p t i -> p (t i)").bitcast(I32))
+        w_first = head.tile([P, PACK, W_PIECES[0][2]], F32, name="w_first", align_bytes=256, offset=4 * T2)
+        w_raw[0] = w_first[:]
+        load_w(0)
+
         nc.vector.tensor_copy(picked[:, 0:S].rearrange("p (a t m) -> p a m t", a=PASSES, t=PACK), tabs[:].indirect(idx[:]))
         nc.vector.tensor_copy(picked[:, S : S + S2], tab2s[:].indirect(idx2[:]))
         for r in range(SCALE_ROWS):
-            nc.sync.dma_start(planes[r:P:32, :].bitcast(I32), picked[TABLE_ROW + r : P : SCALE_ROWS, :].bitcast(I32))
+            nc.sync.dma_start(planes[r:P:32, :].bitcast(I32), picked[TABLE_ROW + TABLE_STEP * r : TABLE_END : TABLE_STEP * SCALE_ROWS, :].bitcast(I32))
 
-        for k in range(len(W_PIECES)):
+        for k in range(1, len(W_PIECES)):
             load_w(k)
         nc.sync.dma_start(w4w[:].bitcast(I32), w4_words.rearrange("a p c -> p a c").bitcast(I32))
         with nc.allow_non_contiguous_dma(reason="one bias value a partition"):
@@ -159,6 +165,7 @@ def tile_list_gp_inducing_mean_kernel(
 
         round_w(0)
         round_w(1)
+        round_w(2)
         shift = keep.tile([P, PASSES, PACK, S2 - SHIFT_FROM], F32, name="shift", align_bytes=256)
         for a in range(PASSES):
             for t in range(PACK):
@@ -309,4 +316,4 @@ def tile_list_gp_inducing_mean_kernel(
                 if u == 2 * c + 3:
                     finish(c)
             if u == 0:
-                round_w(2)
+                round_w(3)

@@ -57,12 +57,12 @@ def tile_list_gp_inducing_mean_kernel(
         tab2s = late.tile([P, T2], U8, name="tab2s", align_bytes=256, offset=0)
         w4w = late.tile([P, PASSES, 2 * N], U8, name="w4w", align_bytes=256, offset=0)
         b_t = late.tile([P, N_TILES], F32, name="b_t", align_bytes=256, offset=2 * PASSES * N)
-        w_both = late.tile([P, PASSES * PACK * N], F32, name="w_both", align_bytes=256, offset=2 * PASSES * N + 256)
+        w_both = late.tile([P, PASSES * PACK * N], F32, name="w_both", align_bytes=256, offset=3 * PASSES * N + 256)
+        w4s = late.tile([P, PASSES, N], U8, name="w4s", align_bytes=256, offset=2 * PASSES * N + 256)
         w_raw = [
             w_both[:, PACK * (a * N + lo) : PACK * (a * N + hi)].rearrange("p (t n) -> p t n", t=PACK)
             for a, lo, hi in W_PIECES
         ]
-        w4s = keep.tile([P, PASSES, N], U8, name="w4s", align_bytes=256)
         picked = keep.tile([P, S + S2], U8, name="picked", align_bytes=256)
         planes = keep.tile([P, S + S2], U8, name="planes", align_bytes=256)
         hx_t = keep.tile([P, PASSES, PACK], F32, name="hx_t", align_bytes=256)
@@ -74,7 +74,6 @@ def tile_list_gp_inducing_mean_kernel(
         nc.gpsimd.memset(tabs[:].bitcast(I32), 0)
         nc.vector.memset(tab2s[:].bitcast(I32), 0)
         make_identity(nc, ident[:])
-        nc.vector.memset(w4s[:].bitcast(I32), 0)
         nc.vector.memset(planes[:].bitcast(I32), 0)
 
         def load_w(k):
@@ -89,11 +88,6 @@ def tile_list_gp_inducing_mean_kernel(
         nc.sync.dma_start(tab2s[TABLE_ROW:TABLE_END:TABLE_STEP, :].bitcast(I32), tab2_scales[0].bitcast(I32))
         nc.sync.dma_start(tabw[:], tab_words[0].rearrange("p t i -> p (t i)").bitcast(I32))
         nc.sync.dma_start(hx_t[:], hx.rearrange("(a p t) -> p a t", a=PASSES, t=PACK))
-        for r in range(SCALE_ROWS):
-            nc.sync.dma_start(
-                w4s[r:P:32, :, :].bitcast(I32),
-                w4_scales[:, r : 4 * SCALE_ROWS : SCALE_ROWS, :].rearrange("a q c -> q a c").bitcast(I32),
-            )
 
 
         factors = keep.tile([P, 3, PASSES, PACK], F32, name="factors", align_bytes=256)
@@ -115,6 +109,12 @@ def tile_list_gp_inducing_mean_kernel(
         for k in range(1, len(W_PIECES)):
             load_w(k)
         nc.sync.dma_start(w4w[:].bitcast(I32), w4_words.rearrange("a p c -> p a c").bitcast(I32))
+        nc.gpsimd.memset(w4s[:].bitcast(I32), 0)
+        for r in range(SCALE_ROWS):
+            nc.sync.dma_start(
+                w4s[r:P:32, :, :].bitcast(I32),
+                w4_scales[:, r : 4 * SCALE_ROWS : SCALE_ROWS, :].rearrange("a q c -> q a c").bitcast(I32),
+            )
         with nc.allow_non_contiguous_dma(reason="one bias value a partition"):
             nc.sync.dma_start(b_t[:], b.rearrange("(c p) -> p c", p=P))
 

@@ -27,13 +27,12 @@ A_BANKS = 4
 LINE = 4
 LIST_ROWS = 16
 SCALE_ROWS = 4
-TABLE_ROW, TABLE_STEP = 32, 4
-TABLE_END = TABLE_ROW + TABLE_STEP * 4 * SCALE_ROWS
+TABLE_ROW = P - 4 * SCALE_ROWS
 CHUNKS = [(0, 512, 1), (512, 512, 1), (1024, 256, 2), (1280, 128, 2), (1408, 128, 1)]
 UNITS = [(lo, width, a) for lo, width, share in CHUNKS for a in range(PASSES)]
 HALVED = ()
 W_PIECES = [(0, 0, 256), (0, 256, 512), (1, 0, 256), (1, 256, 512)]
-GATHERS = [(0, 512, None), (512, 512, None), (1024, 256, 1), (1280, 256, 2)]
+GATHERS = [(0, 512, None), (512, 768, None), (1280, 256, 2)]
 SHIFT_FROM = 1024
 LN_LOW, LN_HIGH = 2.0**-64, 2.0**64
 
@@ -71,8 +70,8 @@ def tile_list_gp_inducing_mean_kernel(
         hz_t = keep.tile([P, S2], F32, name="hz_t", align_bytes=256)
         ident = keep.tile([P, P], F32, name="ident", align_bytes=256)
 
-        nc.gpsimd.memset(tabs[:].bitcast(I32), 0)
-        nc.vector.memset(tab2s[:].bitcast(I32), 0)
+        nc.vector.memset(tabs[0:TABLE_ROW, :].bitcast(I32), 0)
+        nc.vector.memset(tab2s[0:TABLE_ROW, :].bitcast(I32), 0)
         make_identity(nc, ident[:])
         nc.vector.memset(planes[:].bitcast(I32), 0)
 
@@ -83,9 +82,9 @@ def tile_list_gp_inducing_mean_kernel(
         nc.scalar.dma_start(pw_t[:], pw.rearrange("(a p t) -> p a t", a=PASSES, t=PACK))
         nc.scalar.dma_start(hz_col[:], hz.rearrange("(p c) -> p c", p=P))
         nc.sync.dma_start(idx[:], offs)
-        nc.sync.dma_start(tabs[TABLE_ROW:TABLE_END:TABLE_STEP, :].bitcast(I32), tab_scales[0].bitcast(I32))
+        nc.sync.dma_start(tabs[TABLE_ROW:P, :].bitcast(I32), tab_scales[0].bitcast(I32))
         nc.sync.dma_start(idx2[:], offs2)
-        nc.sync.dma_start(tab2s[TABLE_ROW:TABLE_END:TABLE_STEP, :].bitcast(I32), tab2_scales[0].bitcast(I32))
+        nc.sync.dma_start(tab2s[TABLE_ROW:P, :].bitcast(I32), tab2_scales[0].bitcast(I32))
         nc.sync.dma_start(tabw[:], tab_words[0].rearrange("p t i -> p (t i)").bitcast(I32))
         nc.sync.dma_start(hx_t[:], hx.rearrange("(a p t) -> p a t", a=PASSES, t=PACK))
 
@@ -104,7 +103,7 @@ def tile_list_gp_inducing_mean_kernel(
         nc.vector.tensor_copy(picked[:, 0:S].rearrange("p (a t m) -> p a m t", a=PASSES, t=PACK), tabs[:].indirect(idx[:]))
         nc.vector.tensor_copy(picked[:, S : S + S2], tab2s[:].indirect(idx2[:]))
         for r in range(SCALE_ROWS):
-            nc.sync.dma_start(planes[r:P:32, :].bitcast(I32), picked[TABLE_ROW + TABLE_STEP * r : TABLE_END : TABLE_STEP * SCALE_ROWS, :].bitcast(I32))
+            nc.sync.dma_start(planes[r:P:32, :].bitcast(I32), picked[TABLE_ROW + r : P : SCALE_ROWS, :].bitcast(I32))
 
         for k in range(1, len(W_PIECES)):
             load_w(k)

@@ -56,12 +56,12 @@ def tile_list_gp_inducing_mean_kernel(
         tab2s = late.tile([P, T2], U8, name="tab2s", align_bytes=256, offset=0)
         w4w = late.tile([P, PASSES, 2 * N], U8, name="w4w", align_bytes=256, offset=0)
         b_t = late.tile([P, N_TILES], F32, name="b_t", align_bytes=256, offset=2 * PASSES * N)
-        w_both = late.tile([P, PASSES * PACK * N], F32, name="w_both", align_bytes=256, offset=3 * PASSES * N + 256)
-        w4s = late.tile([P, PASSES, N], U8, name="w4s", align_bytes=256, offset=2 * PASSES * N + 256)
+        w_both = late.tile([P, PASSES * PACK * N], F32, name="w_both", align_bytes=256, offset=2 * PASSES * N + 256)
         w_raw = [
             w_both[:, PACK * (a * N + lo) : PACK * (a * N + hi)].rearrange("p (t n) -> p t n", t=PACK)
             for a, lo, hi in W_PIECES
         ]
+        w4s = keep.tile([P, PASSES, N], U8, name="w4s", align_bytes=256)
         picked = keep.tile([P, S + S2], U8, name="picked", align_bytes=256)
         planes = keep.tile([P, S + S2], U8, name="planes", align_bytes=256)
         hx_t = keep.tile([P, PASSES, PACK], F32, name="hx_t", align_bytes=256)
@@ -73,6 +73,7 @@ def tile_list_gp_inducing_mean_kernel(
         nc.vector.memset(tabs[0:TABLE_ROW, :].bitcast(I32), 0)
         nc.vector.memset(tab2s[0:TABLE_ROW, :].bitcast(I32), 0)
         make_identity(nc, ident[:])
+        nc.vector.memset(w4s[:].bitcast(I32), 0)
         nc.vector.memset(planes[:].bitcast(I32), 0)
 
         def load_w(k):
@@ -87,6 +88,11 @@ def tile_list_gp_inducing_mean_kernel(
         nc.sync.dma_start(tab2s[TABLE_ROW:P, :].bitcast(I32), tab2_scales[0].bitcast(I32))
         nc.sync.dma_start(tabw[:], tab_words[0].rearrange("p t i -> p (t i)").bitcast(I32))
         nc.sync.dma_start(hx_t[:], hx.rearrange("(a p t) -> p a t", a=PASSES, t=PACK))
+        for r in range(SCALE_ROWS):
+            nc.sync.dma_start(
+                w4s[r:P:32, :, :].bitcast(I32),
+                w4_scales[:, r : 4 * SCALE_ROWS : SCALE_ROWS, :].rearrange("a q c -> q a c").bitcast(I32),
+            )
 
 
         factors = keep.tile([P, 3, PASSES, PACK], F32, name="factors", align_bytes=256)
@@ -108,12 +114,6 @@ def tile_list_gp_inducing_mean_kernel(
         for k in range(1, len(W_PIECES)):
             load_w(k)
         nc.sync.dma_start(w4w[:].bitcast(I32), w4_words.rearrange("a p c -> p a c").bitcast(I32))
-        nc.gpsimd.memset(w4s[:].bitcast(I32), 0)
-        for r in range(SCALE_ROWS):
-            nc.sync.dma_start(
-                w4s[r:P:32, :, :].bitcast(I32),
-                w4_scales[:, r : 4 * SCALE_ROWS : SCALE_ROWS, :].rearrange("a q c -> q a c").bitcast(I32),
-            )
         with nc.allow_non_contiguous_dma(reason="one bias value a partition"):
             nc.sync.dma_start(b_t[:], b.rearrange("(c p) -> p c", p=P))
 

@@ -27,7 +27,8 @@ A_BANKS = 4
 LINE = 4
 LIST_ROWS = 16
 SCALE_ROWS = 4
-TABLE_ROW = P - 4 * SCALE_ROWS
+TABLE_ROW, TABLE_STEP = 32, 4
+TABLE_END = TABLE_ROW + TABLE_STEP * 4 * SCALE_ROWS
 CHUNKS = [(0, 512, 1), (512, 512, 1), (1024, 256, 2), (1280, 128, 2), (1408, 128, 1)]
 UNITS = [(lo, width, a) for lo, width, share in CHUNKS for a in range(PASSES)]
 HALVED = ()
@@ -70,8 +71,8 @@ def tile_list_gp_inducing_mean_kernel(
         hz_t = keep.tile([P, S2], F32, name="hz_t", align_bytes=256)
         ident = keep.tile([P, P], F32, name="ident", align_bytes=256)
 
-        nc.vector.memset(tabs[0:TABLE_ROW, :].bitcast(I32), 0)
-        nc.vector.memset(tab2s[0:TABLE_ROW, :].bitcast(I32), 0)
+        nc.vector.memset(tabs[:].bitcast(I32), 0)
+        nc.vector.memset(tab2s[:].bitcast(I32), 0)
         make_identity(nc, ident[:])
         nc.vector.memset(w4s[:].bitcast(I32), 0)
         nc.vector.memset(planes[:].bitcast(I32), 0)
@@ -83,9 +84,9 @@ def tile_list_gp_inducing_mean_kernel(
         nc.scalar.dma_start(pw_t[:], pw.rearrange("(a p t) -> p a t", a=PASSES, t=PACK))
         nc.scalar.dma_start(hz_col[:], hz.rearrange("(p c) -> p c", p=P))
         nc.sync.dma_start(idx[:], offs)
-        nc.sync.dma_start(tabs[TABLE_ROW:P, :].bitcast(I32), tab_scales[0].bitcast(I32))
+        nc.sync.dma_start(tabs[TABLE_ROW:TABLE_END:TABLE_STEP, :].bitcast(I32), tab_scales[0].bitcast(I32))
         nc.sync.dma_start(idx2[:], offs2)
-        nc.sync.dma_start(tab2s[TABLE_ROW:P, :].bitcast(I32), tab2_scales[0].bitcast(I32))
+        nc.sync.dma_start(tab2s[TABLE_ROW:TABLE_END:TABLE_STEP, :].bitcast(I32), tab2_scales[0].bitcast(I32))
         nc.sync.dma_start(tabw[:], tab_words[0].rearrange("p t i -> p (t i)").bitcast(I32))
         nc.sync.dma_start(hx_t[:], hx.rearrange("(a p t) -> p a t", a=PASSES, t=PACK))
         for r in range(SCALE_ROWS):
@@ -109,7 +110,7 @@ def tile_list_gp_inducing_mean_kernel(
         nc.vector.tensor_copy(picked[:, 0:S].rearrange("p (a t m) -> p a m t", a=PASSES, t=PACK), tabs[:].indirect(idx[:]))
         nc.vector.tensor_copy(picked[:, S : S + S2], tab2s[:].indirect(idx2[:]))
         for r in range(SCALE_ROWS):
-            nc.sync.dma_start(planes[r:P:32, :].bitcast(I32), picked[TABLE_ROW + r : P : SCALE_ROWS, :].bitcast(I32))
+            nc.sync.dma_start(planes[r:P:32, :].bitcast(I32), picked[TABLE_ROW + TABLE_STEP * r : TABLE_END : TABLE_STEP * SCALE_ROWS, :].bitcast(I32))
 
         for k in range(1, len(W_PIECES)):
             load_w(k)

@@ -73,7 +73,8 @@ def tile_list_gp_inducing_mean_kernel(
 
         nc.vector.memset(tabs[:].bitcast(I32), 0)
         nc.vector.memset(tab2s[:].bitcast(I32), 0)
-        make_identity(nc, ident[:])
+        nc.vector.memset(ident[:], 0.0)
+        make_identity(nc, ident[:], nomemset=True)
         nc.vector.memset(w4s[:].bitcast(I32), 0)
         nc.vector.memset(planes[:].bitcast(I32), 0)
 

from contextlib import ExitStack

import concourse.mybir as mybir
from concourse.masks import make_identity

K, T, S, T2, S2, N = 512, 2048, 1024, 4096, 1536, 512
FLOPS = 2 * K * S * S2 + 2 * 2 * S * N * S2

F32 = mybir.dt.float32
BF16 = mybir.dt.bfloat16
I32 = mybir.dt.int32
U32 = mybir.dt.uint32
U16 = mybir.dt.uint16
U8 = mybir.dt.uint8
FP8X4 = mybir.dt.float8_e4m3fn_x4
FP4X4 = mybir.dt.float4_e2m1fn_x4
ALU = mybir.AluOpType
ACT = mybir.ActivationFunctionType

P = 128
PACK = 4
PASS = P * PACK
PASSES = S // PASS
N_TILES = N // P
BANK = 512
A_BANKS = 4
LINE = 4
LIST_ROWS = 16
SCALE_ROWS = 4
TABLE_ROW, TABLE_STEP = 32, 4
TABLE_END = TABLE_ROW + TABLE_STEP * 4 * SCALE_ROWS
CHUNKS = [(0, 512, 1), (512, 512, 1), (1024, 256, 2), (1280, 128, 2), (1408, 128, 1)]
UNITS = [(lo, width, a) for lo, width, share in CHUNKS for a in range(PASSES)]
HALVED = ()
W_PIECES = [(0, 0, 256), (0, 256, 512), (1, 0, 256), (1, 256, 512)]
GATHERS = [(0, 512, None), (512, 768, None), (1280, 256, 2)]
SHIFT_FROM = 1024
LN_LOW, LN_HIGH = 2.0**-64, 2.0**64


def tile_list_gp_inducing_mean_kernel(
    tc, tab_words, tab_scales, tab2_words, tab2_scales, offs, offs2, hx, hz, pw, w4_words, w4_scales, w, b, out
):
    nc = tc.nc
    with ExitStack() as ctx:
        keep = ctx.enter_context(tc.tile_pool(name="keep", bufs=1))
        ring = ctx.enter_context(tc.tile_pool(name="ring", bufs=2))
        head = ctx.enter_context(tc.tile_pool(name="head", bufs=1))
        late = ctx.enter_context(tc.tile_pool(name="late", bufs=1))
        psum_a = ctx.enter_context(tc.psum_pool(name="psum_a", bufs=A_BANKS))
        psum_y = ctx.enter_context(tc.psum_pool(name="psum_y", bufs=8 - A_BANKS))

        idx = keep.tile([P, S // LIST_ROWS], U16, name="idx", align_bytes=256)
        idx2 = keep.tile([P, S2 // LIST_ROWS], U16, name="idx2", align_bytes=256)
        tabw = keep.tile([P, T], I32, name="tabw", align_bytes=256)
        tabs = keep.tile([P, T], U8, name="tabs", align_bytes=256)
        tab2s = late.tile([P, T2], U8, name="tab2s", align_bytes=256, offset=0)
        w4w = late.tile([P, PASSES, 2 * N], U8, name="w4w", align_bytes=256, offset=0)
        b_t = late.tile([P, N_TILES], F32, name="b_t", align_bytes=256, offset=2 * PASSES * N)
        w_both = late.tile([P, PASSES * PACK * N], F32, name="w_both", align_bytes=256, offset=2 * PASSES * N + 256)
        w_raw = [
            w_both[:, PACK * (a * N + lo) : PACK * (a * N + hi)].rearrange("p (t n) -> p t n", t=PACK)
            for a, lo, hi in W_PIECES
        ]
        w4s = keep.tile([P, PASSES, N], U8, name="w4s", align_bytes=256)
        picked = keep.tile([P, S + S2], U8, name="picked", align_bytes=256)
        planes = keep.tile([P, S + S2], U8, name="planes", align_bytes=256)
        hx_t = keep.tile([P, PASSES, PACK], F32, name="hx_t", align_bytes=256)
        pw_t = head.tile([P, PASSES, PACK], F32, name="pw_t", align_bytes=256, offset=0)
        hz_col = head.tile([P, S2 // P], F32, name="hz_col", align_bytes=256, offset=4 * T2)
        hz_t = keep.tile([P, S2], F32, name="hz_t", align_bytes=256)
        ident = keep.tile([P, P], F32, name="ident", align_bytes=256)

        nc.vector.memset(tabs[:].bitcast(I32), 0)
        nc.vector.memset(tab2s[:].bitcast(I32), 0)
        nc.vector.memset(ident[:], 0.0)
        make_identity(nc, ident[:], nomemset=True)
        nc.vector.memset(w4s[:].bitcast(I32), 0)
        nc.vector.memset(planes[:].bitcast(I32), 0)

        def load_w(k):
            a, lo, hi = W_PIECES[k]
            nc.sync.dma_start(w_raw[k], w[a * PASS : (a + 1) * PASS, lo:hi].rearrange("(p t) n -> p t n", t=PACK))

        nc.scalar.dma_start(pw_t[:], pw.rearrange("(a p t) -> p a t", a=PASSES, t=PACK))
        nc.scalar.dma_start(hz_col[:], hz.rearrange("(p c) -> p c", p=P))
        nc.sync.dma_start(idx[:], offs)
        nc.sync.dma_start(tabs[TABLE_ROW:TABLE_END:TABLE_STEP, :].bitcast(I32), tab_scales[0].bitcast(I32))
        nc.sync.dma_start(idx2[:], offs2)
        nc.sync.dma_start(tab2s[TABLE_ROW:TABLE_END:TABLE_STEP, :].bitcast(I32), tab2_scales[0].bitcast(I32))
        nc.sync.dma_start(tabw[:], tab_words[0].rearrange("p t i -> p (t i)").bitcast(I32))
        nc.sync.dma_start(hx_t[:], hx.rearrange("(a p t) -> p a t", a=PASSES, t=PACK))
        for r in range(SCALE_ROWS):
            nc.sync.dma_start(
                w4s[r:P:32, :, :].bitcast(I32),
                w4_scales[:, r : 4 * SCALE_ROWS : SCALE_ROWS, :].rearrange("a q c -> q a c").bitcast(I32),
            )


        factors = keep.tile([P, 3, PASSES, PACK], F32, name="factors", align_bytes=256)
        nc.vector.tensor_scalar(factors[:, 0], pw_t[:], LN_LOW, LN_HIGH, ALU.max, ALU.min)
        nc.vector.tensor_scalar(factors[:, 1], pw_t[:], LN_HIGH, LN_LOW, ALU.max, ALU.mult)
        nc.vector.tensor_scalar(factors[:, 2], pw_t[:], LN_LOW, LN_HIGH, ALU.min, ALU.mult)

        tab2w = head.tile([P, T2], I32, name="tab2w", align_bytes=256, offset=0)
        nc.sync.dma_start(tab2w[:], tab2_words[0].rearrange("p t i -> p (t i)").bitcast(I32))
        w_first = head.tile([P, PACK, W_PIECES[0][2]], F32, name="w_first", align_bytes=256, offset=4 * T2)
        w_raw[0] = w_first[:]
        load_w(0)

        nc.vector.tensor_copy(picked[:, 0:S].rearrange("p (a t m) -> p a m t", a=PASSES, t=PACK), tabs[:].indirect(idx[:]))
        nc.vector.tensor_copy(picked[:, S : S + S2], tab2s[:].indirect(idx2[:]))
        for r in range(SCALE_ROWS):
            nc.sync.dma_start(planes[r:P:32, :].bitcast(I32), picked[TABLE_ROW + TABLE_STEP * r : TABLE_END : TABLE_STEP * SCALE_ROWS, :].bitcast(I32))

        for k in range(1, len(W_PIECES)):
            load_w(k)
        nc.sync.dma_start(w4w[:].bitcast(I32), w4_words.rearrange("a p c -> p a c").bitcast(I32))
        with nc.allow_non_contiguous_dma(reason="one bias value a partition"):
            nc.sync.dma_start(b_t[:], b.rearrange("(c p) -> p c", p=P))

        for group in range(S2 // BANK):
            spread = psum_y.tile([P, BANK], F32, name="bank_y")
            for c in range(LINE):
                column = hz_col[:, LINE * group + c : LINE * group + c + 1]
                nc.tensor.transpose(spread[:, c * P : (c + 1) * P], column.to_broadcast([P, P]), ident[:])
            nc.scalar.copy(
                hz_t[:].rearrange("p (m c) -> p m c", m=P)[:, :, LINE * group : LINE * (group + 1)],
                spread[:].rearrange("p (c m) -> p m c", c=LINE),
            )

        terms = keep.tile([P, 4, PASSES * PACK], F32, name="terms", align_bytes=256)
        terms_out = keep.tile([P, PASSES * PACK, 4], F32, name="terms_out", align_bytes=256)
        bias = keep.tile([P, PASSES, PACK], F32, name="bias", align_bytes=256)
        nc.scalar.activation(terms[:, 0:3, :], factors[:].rearrange("p f a t -> p f (a t)"), ACT.Ln)
        warm = keep.tile([P, 1], F32, name="warm")
        nc.scalar.activation(warm[:], terms[:, 0, 0:1], ACT.Exp)
        nc.scalar.activation(terms[:, 3, :], hx_t[:].rearrange("p a t -> p (a t)"), ACT.Identity, scale=-1.0)
        for a in range(PASSES):
            for t in range(PACK):
                slab = a * PACK + t
                nc.scalar.activation(terms_out[:, slab, :], terms[:, :, slab], ACT.Identity, accum_out=bias[:, a, t : t + 1])

        vw = keep.tile([P, PASSES, PASS], U32, name="vw", align_bytes=256)
        wq = [keep.tile([P, N], U32, name=f"wq{a}", align_bytes=256) for a in range(PASSES)]
        wqs = [keep.tile([P, N], U8, name=f"wqs{a}", align_bytes=256) for a in range(PASSES)]
        w_bf = [keep.tile([P, N * PACK], BF16, name=f"w_bf{a}", align_bytes=256) for a in range(PASSES)]
        v2w = {}

        def gather_v2_words(g, tag):
            lo, width, after = GATHERS[g]
            v2w[g] = keep.tile([P, width], U32, name=tag, align_bytes=256)
            entries = idx2[:, lo // LIST_ROWS : (lo + width) // LIST_ROWS]
            nc.vector.tensor_copy(v2w[g][:], tab2w[:].bitcast(U32).indirect(entries))

        def round_w(k):
            a, lo, hi = W_PIECES[k]
            nc.scalar.activation(
                w_bf[a][:, PACK * lo : PACK * hi].rearrange("p (c i t) -> p c t i", i=LINE, t=PACK),
                w_raw[k].rearrange("p t (c i) -> p c t i", i=LINE),
                ACT.Copy,
            )

        def quantize_w(a):
            nc.vector.quantize_mx(out=wq[a][:].bitcast(FP8X4), scales=wqs[a][:], in_=w_bf[a][:])

        round_w(0)
        round_w(1)
        round_w(2)
        shift = keep.tile([P, PASSES, PACK, S2 - SHIFT_FROM], F32, name="shift", align_bytes=256)
        for a in range(PASSES):
            for t in range(PACK):
                nc.scalar.activation(
                    shift[:, a, t, :], hz_t[:, SHIFT_FROM:S2], ACT.Identity, bias=bias[:, a, t : t + 1], scale=-1.0
                )

        fills = [(u, t, BANK // width) for u, (lo, width, a) in enumerate(UNITS) for t in range(0, PACK, BANK // width)]
        banks, z, h_bf, hq, hqs, acc = {}, {}, {}, {}, {}, {}

        def products_a(f):
            u, first, count = fills[f]
            lo, width, a = UNITS[u]
            banks[f] = psum_a.tile([P, BANK], F32, name="bank_a")
            g = max(g for g in range(len(GATHERS)) if GATHERS[g][0] <= lo)
            for t in range(first, first + count):
                nc.tensor.matmul_mx(
                    out=banks[f][:, (t - first) * width : (t - first + 1) * width],
                    lhsT=vw[:, a, t * P : (t + 1) * P].bitcast(FP8X4),
                    lhsT_scale=planes[:, a * PASS + t * P : a * PASS + (t + 1) * P],
                    rhs=v2w[g][:, lo - GATHERS[g][0] : lo - GATHERS[g][0] + width].bitcast(FP8X4),
                    rhs_scale=planes[:, S + lo : S + lo + width],
                    start=True,
                    stop=True,
                )

        def exponents(f):
            u, first, count = fills[f]
            lo, width, a = UNITS[u]
            if first == 0:
                z[u] = ring.tile([P, width // LINE, PACK, LINE], F32, name="z", align_bytes=256)
            if lo < SHIFT_FROM:
                for t in range(first, first + count):
                    nc.vector.scalar_tensor_tensor(
                        z[u][:, :, t, :],
                        banks[f][:, (t - first) * width : (t - first + 1) * width].rearrange("p (c i) -> p c i", i=LINE),
                        bias[:, a, t : t + 1],
                        hz_t[:, lo : lo + width].rearrange("p (c i) -> p c i", i=LINE),
                        ALU.add,
                        ALU.subtract,
                    )
            else:
                nc.vector.tensor_tensor(
                    z[u][:, :, first : first + count, :].rearrange("p c t i -> p t c i"),
                    banks[f][:].rearrange("p (t c i) -> p t c i", t=count, i=LINE),
                    shift[:, a, first : first + count, lo - SHIFT_FROM : lo - SHIFT_FROM + width].rearrange("p t (c i) -> p t c i", i=LINE),
                    ALU.add,
                )

        parts = [2 if u in HALVED else 1 for u in range(len(UNITS))]

        def kernel_values(u):
            width = UNITS[u][1] // parts[u]
            for part in range(parts[u]):
                h_bf[u, part] = keep.tile([P, width * PACK], BF16, name=f"h_bf{u}_{part}", align_bytes=256)
                nc.scalar.activation(
                    h_bf[u, part][:].rearrange("p (c i t) -> p c t i", i=LINE, t=PACK),
                    z[u][:, part * width // LINE : (part + 1) * width // LINE],
                    ACT.Exp,
                )

        def quantize_h(u):
            width = UNITS[u][1] // parts[u]
            for part in range(parts[u]):
                hq[u, part] = keep.tile([P, width], U32, name=f"hq{u}_{part}", align_bytes=256)
                hqs[u, part] = keep.tile([P, width], U8, name=f"hqs{u}_{part}", align_bytes=256)
                nc.vector.quantize_mx(out=hq[u, part][:].bitcast(FP8X4), scales=hqs[u, part][:], in_=h_bf[u, part][:])

        def products_y(u):
            a = UNITS[u][2]
            c = u // PASSES
            c_width, share = CHUNKS[c][1:]
            width = c_width // parts[u]
            for part in range(parts[u]):
                for nt in range(N_TILES):
                    place = nt % share
                    if a == 0 and part == 0 and place == 0:
                        if c == len(CHUNKS) - 1 and nt < 2:
                            acc[c, nt // share] = psum_a.tile([P, BANK], F32, name="bank_a")
                        else:
                            acc[c, nt // share] = psum_y.tile([P, BANK], F32, name="bank_y")
                    left = place * c_width + part * width
                    target = acc[c, nt // share][:, left : left + width]
                    nc.tensor.matmul_mx(
                        out=target,
                        lhsT=w4w[:, a, 2 * nt * P : 2 * (nt + 1) * P].bitcast(FP4X4),
                        lhsT_scale=w4s[:, a, nt * P : (nt + 1) * P],
                        rhs=hq[u, part][:].bitcast(FP8X4),
                        rhs_scale=hqs[u, part][:],
                        start=(a == 0 and part == 0 and place == 0),
                        stop=False,
                    )
                    nc.tensor.matmul_mx(
                        out=target,
                        lhsT=wq[a][:, nt * P : (nt + 1) * P].bitcast(FP8X4),
                        lhsT_scale=wqs[a][:, nt * P : (nt + 1) * P],
                        rhs=hq[u, part][:].bitcast(FP8X4),
                        rhs_scale=hqs[u, part][:],
                        start=False,
                        stop=(a == PASSES - 1 and part == parts[u] - 1 and place == share - 1),
                    )

        def finish(c):
            lo, width, share = CHUNKS[c]
            for k in range(N_TILES // share):
                first = k * share
                bank = acc[c, k][:, 0 : share * width].rearrange("p (s j) -> p s j", s=share)
                res = keep.tile([P, share, width], F32, name=f"res{c}_{first}", align_bytes=256)
                if c > 0 and k % 2 == (0 if c < 2 else 1):
                    nc.vector.tensor_tensor(
                        res[:], bank, b_t[:, first : first + share].unsqueeze(2).to_broadcast([P, share, width]), ALU.add
                    )
                else:
                    for s in range(share):
                        nc.scalar.activation(res[:, s, :], bank[:, s, :], ACT.Identity, bias=b_t[:, first + s : first + s + 1])
                nc.sync.dma_start(
                    out[first * P : (first + share) * P, lo : lo + width].rearrange("(s p) j -> p s j", p=P),
                    res[:],
                )

        nc.vector.tensor_copy(vw[:].rearrange("p a (t m) -> p a m t", t=PACK), tabw[:].bitcast(U32).indirect(idx[:]))
        for g in range(len(GATHERS)):
            if GATHERS[g][2] is None:
                gather_v2_words(g, f"v2w{g}")
        for f in range(A_BANKS):
            products_a(f)

        for u in range(len(UNITS) + 2):
            if u == 1:
                quantize_w(0)
            if u == 3:
                quantize_w(1)
            if u >= 2:
                products_y(u - 2)
            for f in range(len(fills)):
                if fills[f][0] == u:
                    exponents(f)
                    if f + A_BANKS < len(fills):
                        products_a(f + A_BANKS)
            if u < len(UNITS):
                kernel_values(u)
            if 1 <= u <= len(UNITS):
                quantize_h(u - 1)
            for g in range(len(GATHERS)):
                if GATHERS[g][2] == u - 1:
                    gather_v2_words(g, f"h_bf{u - 1}_0")
            for c in range(len(CHUNKS)):
                if u == 2 * c + 3:
                    finish(c)
            if u == 0:
                round_w(3)
